import numpy as np
import ml_dtypes


def mxq(x, axis, fmt="e4m3"):
    dtype, down = {"e4m3": (ml_dtypes.float8_e4m3fn, 7), "e5m2": (ml_dtypes.float8_e5m2, 14)}[fmt]
    v = np.moveaxis(np.asarray(x, np.float32).astype(ml_dtypes.bfloat16).astype(np.float64), axis, -1)
    blocks = v.reshape(v.shape[:-1] + (-1, 32))
    amax = np.abs(blocks).max(-1, keepdims=True)
    byte = np.maximum(np.where(amax > 0, np.frexp(amax)[1] - 1 + 127, 0) - down, 1)
    scale = np.exp2(byte - 127.0)
    codes = (blocks / scale).astype(np.float32).astype(dtype).astype(np.float64)
    return np.moveaxis((codes * scale).reshape(v.shape), -1, axis)


WIDE = False


def mx_kscale(k):
    if not WIDE:
        return np.ones(k)
    levels = np.array([18, -18])
    if k % 512:
        return np.exp2(np.random.permutation(np.resize(levels, k // 32))).repeat(32)
    a = np.empty((k // 512, 16))
    for p in range(k // 512):
        a[p, :8] = np.random.permutation(np.resize(levels, 8))
        for g in range(8):
            far = levels[np.abs(levels - a[p, g]) >= 10]
            a[p, g + 8] = far[np.random.randint(len(far))]
    return np.exp2(a.ravel()).repeat(32)


def f64(x):
    return np.asarray(x).astype(np.float64)


def striped(idx):
    return np.tile(np.asarray(idx).reshape(-1, 16).T, (8, 1)).astype(np.uint16)


def unstriped(offs):
    return offs[:16].T.reshape(-1).astype(np.int64)


B, N, T, D, R = 1, 512, 2048, 512, 1024
LR = 0.1
BETA = 0.9


def setup_inputs():
    n = np.random.standard_normal
    idx = np.random.permutation(T)[:B * N]
    s = mx_kscale(D)[:, None]
    z = mx_kscale(R)[:, None]
    x = n((B, D, R))
    return {
        "xT": (x * s).astype(np.float32),
        "wT": (n((D, T)) * (1.00 / np.sqrt(D)) / s).astype(np.float32),
        "y": n((B, R, N)).astype(np.float32),
        "wt": (np.random.uniform(0.5, 1.5, (B, R, 1)) * 1.0 / np.sqrt(R) * z).astype(np.float32),
        "xm": (x.transpose(0, 2, 1) / z / s[:, 0]).astype(np.float32),
        "mT": (0.3 * n((D, T)) / s).astype(np.float32),
        "offs": striped(idx),
    }


def reference(xT, wT, y, wt, xm, mT, offs):
    idx = unstriped(offs)
    pick = lambda x: x[:, idx].reshape(x.shape[0], B, N).transpose(1, 0, 2)
    w = pick(f64(wT))
    a = mxq(f64(xT), 1, "e4m3").transpose(0, 2, 1) @ mxq(w, 1, "e4m3")
    g = f64(wt) * (a - f64(y))
    dw = mxq(f64(xm), 1, "e4m3").transpose(0, 2, 1) @ mxq(g, 1, "e5m2")
    nm = BETA * pick(f64(mT)) + dw
    nw = w - LR * (dw + BETA * nm)
    tables = []
    for old, new in ((wT, nw), (mT, nm),):
        table = f64(old)
        table[:, idx] = new.transpose(1, 0, 2).reshape(D, B * N)
        tables.append(table)
    return tuple(tables)

@@ -1,0 +1,154 @@
+from contextlib import ExitStack
+
+import concourse.mybir as mybir
+
+D, T, N, R = 512, 2048, 512, 1024
+LR, BETA = 0.1, 0.9
+FLOPS = 2 * 2 * D * N * R
+
+F32 = mybir.dt.float32
+BF16 = mybir.dt.bfloat16
+U32 = mybir.dt.uint32
+U16 = mybir.dt.uint16
+U8 = mybir.dt.uint8
+E4M3 = mybir.dt.float8_e4m3fn_x4
+E5M2 = mybir.dt.float8_e5m2_x4
+MULT = mybir.AluOpType.mult
+ADD = mybir.AluOpType.add
+SUB = mybir.AluOpType.subtract
+COPY = mybir.ActivationFunctionType.Copy
+
+P = 128
+PACK = 4
+K = P * PACK
+HALVES = R // K
+
+
+def tile_attend_gsq_nag_kernel(tc, xT, wT, y, wt, xm, mT, offs, out_0, out_1):
+    nc = tc.nc
+    with ExitStack() as ctx:
+        lists = ctx.enter_context(tc.tile_pool(name="lists", bufs=1))
+        keep = ctx.enter_context(tc.tile_pool(name="keep", bufs=1))
+        ring = ctx.enter_context(tc.tile_pool(name="ring", bufs=2))
+        psum = ctx.enter_context(tc.psum_pool(name="psum", bufs=1))
+
+        def plane(table, t):
+            return table.rearrange("(p t) c -> p t c", t=PACK)[:, t, :]
+
+        def rows(src):
+            return src.rearrange("(p j) c -> p j c", j=PACK)
+
+        def quantise(name, grouped, fmt):
+            codes = keep.tile([P, K], U32, name=name + "_codes", align_bytes=64)
+            scales = keep.tile([P, K], U8, name=name + "_scales", align_bytes=64)
+            nc.vector.quantize_mx(out=codes[:].bitcast(fmt), scales=scales[:], in_=grouped[:])
+            return codes, scales
+
+        def group_stationary(name, raw):
+            grouped = keep.tile([P, K * PACK], BF16, name=name, align_bytes=64)
+            nc.scalar.copy(
+                out=grouped[:].rearrange("p (t m j) -> p m j t", t=PACK, j=PACK),
+                in_=raw[:].rearrange("p j (m t) -> p m j t", t=PACK),
+            )
+            return grouped
+
+        def group_moving(name, planes):
+            grouped = keep.tile([P, N * PACK], BF16, name=name, align_bytes=64)
+            nc.vector.tensor_copy(
+                out=grouped[:].rearrange("p (c i t) -> p c t i", i=4, t=PACK),
+                in_=planes[:].rearrange("p t (c i) -> p c t i", i=4),
+            )
+            return grouped
+
+        offsets = lists.tile([P, N // 16], U16, name="offsets")
+        x_raw = [keep.tile([P, PACK, K], F32, name="x_raw%d" % h, tag="shared%d" % h) for h in range(HALVES)]
+        xm_raw = [keep.tile([P, PACK, D], F32, name="xm_raw%d" % h, tag="shared%d" % (2 + h)) for h in range(HALVES)]
+        y_sb = [keep.tile([P, PACK, N], F32, name="y_sb%d" % h) for h in range(HALVES)]
+        w_src = [keep.tile([P, T], F32, name="w_src%d" % t) for t in range(PACK)]
+        m_src = [keep.tile([P, T], F32, name="m_src%d" % t) for t in range(PACK)]
+        wt_sb = keep.tile([P, HALVES, PACK], F32, name="wt_sb")
+
+        nc.sync.dma_start(out=x_raw[0][:], in_=rows(xT[0, :, 0:K]))
+        nc.sync.dma_start(offsets[:], offs)
+        for t in range(PACK):
+            nc.sync.dma_start(out=w_src[t][:], in_=plane(wT, t))
+        nc.sync.dma_start(out=wt_sb[:], in_=wt[0].rearrange("(h p t) o -> p h (t o)", h=HALVES, t=PACK))
+        nc.sync.dma_start(out=y_sb[0][:], in_=rows(y[0, 0:K, :]))
+        nc.sync.dma_start(out=x_raw[1][:], in_=rows(xT[0, :, K:R]))
+        nc.sync.dma_start(out=y_sb[1][:], in_=rows(y[0, K:R, :]))
+        for h in range(HALVES):
+            nc.sync.dma_start(out=xm_raw[h][:], in_=rows(xm[0, h * K : (h + 1) * K, :]))
+        for t in range(PACK):
+            nc.sync.dma_start(out=m_src[t][:], in_=plane(mT, t))
+
+        x_q = [quantise("x0", group_stationary("x_grouped0", x_raw[0]), E4M3)]
+        w_cols = keep.tile([P, PACK, N], F32, name="w_cols")
+        w_dst = []
+        for t in range(PACK):
+            nc.vector.tensor_copy(w_cols[:, t, :], w_src[t][:].indirect(offsets[:]))
+            dst = keep.tile([P, T], F32, name="w_dst%d" % t)
+            nc.scalar.activation(dst[:], w_src[t][:], COPY)
+            w_dst.append(dst)
+        w_codes, w_scales = quantise("w", group_moving("w_grouped", w_cols), E4M3)
+
+        def residual(h):
+            codes, scales = x_q[h]
+            for t in range(PACK):
+                nc.scalar.activation(y_sb[h][:, t, :], y_sb[h][:, t, :], COPY, scale=wt_sb[:, h, t : t + 1])
+            for t in range(PACK):
+                cols = slice(t * P, (t + 1) * P)
+                a = psum.tile([P, N], F32, name="a%d%d" % (h, t), tag="bank%d" % (PACK * h + t))
+                nc.tensor.matmul_mx(
+                    out=a[:], lhsT=codes[:, cols].bitcast(E4M3), lhsT_scale=scales[:, cols],
+                    rhs=w_codes[:].bitcast(E4M3), rhs_scale=w_scales[:], start=True, stop=True,
+                )
+                nc.vector.scalar_tensor_tensor(
+                    out=y_sb[h][:, t, :], in0=a[:], scalar=wt_sb[:, h, t : t + 1], in1=y_sb[h][:, t, :],
+                    op0=MULT, op1=SUB,
+                )
+            return group_moving("g_grouped%d" % h, y_sb[h])
+
+        g_grouped0 = residual(0)
+        x_grouped1 = group_stationary("x_grouped1", x_raw[1])
+        g_q = [quantise("g0", g_grouped0, E5M2)]
+        x_q.append(quantise("x1", x_grouped1, E4M3))
+        g_grouped1 = residual(1)
+        xm_q = [quantise("xm0", group_stationary("xm_grouped0", xm_raw[0]), E4M3)]
+        g_q.append(quantise("g1", g_grouped1, E5M2))
+        xm_q.append(quantise("xm1", group_stationary("xm_grouped1", xm_raw[1]), E4M3))
+
+        dw = [psum.tile([P, N], F32, name="dw%d" % t, tag="bank%d" % t) for t in range(PACK)]
+        for h in range(HALVES):
+            for t in range(PACK):
+                cols = slice(t * P, (t + 1) * P)
+                nc.tensor.matmul_mx(
+                    out=dw[t][:], lhsT=xm_q[h][0][:, cols].bitcast(E4M3), lhsT_scale=xm_q[h][1][:, cols],
+                    rhs=g_q[h][0][:].bitcast(E5M2), rhs_scale=g_q[h][1][:],
+                    start=(h == 0), stop=(h == HALVES - 1),
+                )
+
+        def gather_m(t):
+            cols = ring.tile([P, N], F32, name="m_cols")
+            nc.vector.tensor_copy(cols[:], m_src[t][:].indirect(offsets[:]))
+            dst = keep.tile([P, T], F32, name="m_dst%d" % t, tag="shared%d" % t)
+            nc.scalar.activation(dst[:], m_src[t][:], COPY)
+            return cols, dst
+
+        m_cols, m_dst = gather_m(0)
+        for t in range(PACK):
+            base = ring.tile([P, N], F32, name="base")
+            new_m = ring.tile([P, N], F32, name="new_m")
+            new_w = ring.tile([P, N], F32, name="new_w")
+            nc.vector.scalar_tensor_tensor(
+                out=base[:], in0=m_cols[:], scalar=-LR * BETA * BETA, in1=w_cols[:, t, :], op0=MULT, op1=ADD)
+            nc.vector.scalar_tensor_tensor(
+                out=new_m[:], in0=m_cols[:], scalar=BETA, in1=dw[t][:], op0=MULT, op1=ADD)
+            nc.vector.scalar_tensor_tensor(
+                out=new_w[:], in0=dw[t][:], scalar=-LR * (1.0 + BETA), in1=base[:], op0=MULT, op1=ADD)
+            this_dst = m_dst
+            if t + 1 < PACK:
+                m_cols, m_dst = gather_m(t + 1)
+            nc.vector.tensor_copy(w_dst[t][:].indirect(offsets[:]), new_w[:])
+            nc.sync.dma_start(out=plane(out_0, t), in_=w_dst[t][:])
+            nc.vector.tensor_copy(this_dst[:].indirect(offsets[:]), new_m[:])
+            nc.sync.dma_start(out=plane(out_1, t), in_=this_dst[:])

@@ -29,7 +29,6 @@ def tile_attend_gsq_nag_kernel(tc, xT, wT, y, wt, xm, mT, offs, out_0, out_1):
     with ExitStack() as ctx:
         lists = ctx.enter_context(tc.tile_pool(name="lists", bufs=1))
         keep = ctx.enter_context(tc.tile_pool(name="keep", bufs=1))
-        ring = ctx.enter_context(tc.tile_pool(name="ring", bufs=2))
         psum = ctx.enter_context(tc.psum_pool(name="psum", bufs=1))
 
         def plane(table, t):
@@ -44,12 +43,13 @@ def tile_attend_gsq_nag_kernel(tc, xT, wT, y, wt, xm, mT, offs, out_0, out_1):
             nc.vector.quantize_mx(out=codes[:].bitcast(fmt), scales=scales[:], in_=grouped[:])
             return codes, scales
 
-        def group_stationary(name, raw):
+        def group_stationary(name, raw, on_scalar=P):
             grouped = keep.tile([P, K * PACK], BF16, name=name, align_bytes=64)
-            nc.scalar.copy(
-                out=grouped[:].rearrange("p (t m j) -> p m j t", t=PACK, j=PACK),
-                in_=raw[:].rearrange("p j (m t) -> p m j t", t=PACK),
-            )
+            dst = grouped[:].rearrange("p (t m j) -> p m j t", t=PACK, j=PACK)
+            src = raw[:].rearrange("p j (m t) -> p m j t", t=PACK)
+            nc.scalar.copy(out=dst[:, :on_scalar], in_=src[:, :on_scalar])
+            if on_scalar < P:
+                nc.vector.tensor_copy(out=dst[:, on_scalar:], in_=src[:, on_scalar:])
             return grouped
 
         def group_moving(name, planes):
@@ -63,16 +63,16 @@ def tile_attend_gsq_nag_kernel(tc, xT, wT, y, wt, xm, mT, offs, out_0, out_1):
         offsets = lists.tile([P, N // 16], U16, name="offsets")
         x_raw = [keep.tile([P, PACK, K], F32, name="x_raw%d" % h, tag="shared%d" % h) for h in range(HALVES)]
         xm_raw = [keep.tile([P, PACK, D], F32, name="xm_raw%d" % h, tag="shared%d" % (2 + h)) for h in range(HALVES)]
-        y_sb = [keep.tile([P, PACK, N], F32, name="y_sb%d" % h) for h in range(HALVES)]
+        y_sb = [keep.tile([P, PACK, N], F32, name="y_sb%d" % h, tag="y%d" % h) for h in range(HALVES)]
         w_src = [keep.tile([P, T], F32, name="w_src%d" % t) for t in range(PACK)]
         m_src = [keep.tile([P, T], F32, name="m_src%d" % t) for t in range(PACK)]
         wt_sb = keep.tile([P, HALVES, PACK], F32, name="wt_sb")
 
-        nc.sync.dma_start(out=x_raw[0][:], in_=rows(xT[0, :, 0:K]))
+        nc.scalar.dma_start(out=wt_sb[:], in_=wt[0].rearrange("(h p t) o -> p h (t o)", h=HALVES, t=PACK))
         nc.sync.dma_start(offsets[:], offs)
         for t in range(PACK):
             nc.sync.dma_start(out=w_src[t][:], in_=plane(wT, t))
-        nc.sync.dma_start(out=wt_sb[:], in_=wt[0].rearrange("(h p t) o -> p h (t o)", h=HALVES, t=PACK))
+        nc.sync.dma_start(out=x_raw[0][:], in_=rows(xT[0, :, 0:K]))
         nc.sync.dma_start(out=y_sb[0][:], in_=rows(y[0, 0:K, :]))
         nc.sync.dma_start(out=x_raw[1][:], in_=rows(xT[0, :, K:R]))
         nc.sync.dma_start(out=y_sb[1][:], in_=rows(y[0, K:R, :]))
@@ -81,15 +81,20 @@ def tile_attend_gsq_nag_kernel(tc, xT, wT, y, wt, xm, mT, offs, out_0, out_1):
         for t in range(PACK):
             nc.sync.dma_start(out=m_src[t][:], in_=plane(mT, t))
 
-        x_q = [quantise("x0", group_stationary("x_grouped0", x_raw[0]), E4M3)]
         w_cols = keep.tile([P, PACK, N], F32, name="w_cols")
+
+        def second_copy(name, src, tag):
+            dst = keep.tile([P, T], F32, name=name, tag=tag)
+            for half in (slice(0, T // 2), slice(T // 2, T)):
+                nc.scalar.activation(dst[:, half], src[:, half], COPY)
+            return dst
+
         w_dst = []
         for t in range(PACK):
             nc.vector.tensor_copy(w_cols[:, t, :], w_src[t][:].indirect(offsets[:]))
-            dst = keep.tile([P, T], F32, name="w_dst%d" % t)
-            nc.scalar.activation(dst[:], w_src[t][:], COPY)
-            w_dst.append(dst)
+            w_dst.append(second_copy("w_dst%d" % t, w_src[t], "w_dst%d" % t))
         w_codes, w_scales = quantise("w", group_moving("w_grouped", w_cols), E4M3)
+        x_q = [quantise("x0", group_stationary("x_grouped0", x_raw[0], on_scalar=80), E4M3)]
 
         def residual(h):
             codes, scales = x_q[h]
@@ -110,16 +115,30 @@ def tile_attend_gsq_nag_kernel(tc, xT, wT, y, wt, xm, mT, offs, out_0, out_1):
 
         g_grouped0 = residual(0)
         x_grouped1 = group_stationary("x_grouped1", x_raw[1])
-        g_q = [quantise("g0", g_grouped0, E5M2)]
         x_q.append(quantise("x1", x_grouped1, E4M3))
+        g_q = [quantise("g0", g_grouped0, E5M2)]
         g_grouped1 = residual(1)
         xm_q = [quantise("xm0", group_stationary("xm_grouped0", xm_raw[0]), E4M3)]
         g_q.append(quantise("g1", g_grouped1, E5M2))
-        xm_q.append(quantise("xm1", group_stationary("xm_grouped1", xm_raw[1]), E4M3))
+        xm_grouped1 = group_stationary("xm_grouped1", xm_raw[1])
+        m_cols = keep.tile([P, PACK, N], F32, name="m_cols")
+
+        def gather_m(t):
+            nc.vector.tensor_copy(m_cols[:, t, :], m_src[t][:].indirect(offsets[:]))
+
+        codes = keep.tile([P, K], U32, name="xm1_codes", align_bytes=64)
+        scales = keep.tile([P, K], U8, name="xm1_scales", align_bytes=64)
+        for lo, hi in ((0, P), (P, 2 * P), (2 * P, K)):
+            nc.vector.quantize_mx(
+                out=codes[:, lo:hi].bitcast(E4M3), scales=scales[:, lo:hi], in_=xm_grouped1[:, PACK * lo : PACK * hi])
+            if lo == 0:
+                gather_m(0)
+                m_dst = second_copy("m_dst0", m_src[0], "shared0")
+        xm_q.append((codes, scales))
 
         dw = [psum.tile([P, N], F32, name="dw%d" % t, tag="bank%d" % t) for t in range(PACK)]
-        for h in range(HALVES):
-            for t in range(PACK):
+        for t in range(PACK):
+            for h in range(HALVES):
                 cols = slice(t * P, (t + 1) * P)
                 nc.tensor.matmul_mx(
                     out=dw[t][:], lhsT=xm_q[h][0][:, cols].bitcast(E4M3), lhsT_scale=xm_q[h][1][:, cols],
@@ -127,28 +146,36 @@ def tile_attend_gsq_nag_kernel(tc, xT, wT, y, wt, xm, mT, offs, out_0, out_1):
                     start=(h == 0), stop=(h == HALVES - 1),
                 )
 
-        def gather_m(t):
-            cols = ring.tile([P, N], F32, name="m_cols")
-            nc.vector.tensor_copy(cols[:], m_src[t][:].indirect(offsets[:]))
-            dst = keep.tile([P, T], F32, name="m_dst%d" % t, tag="shared%d" % t)
-            nc.scalar.activation(dst[:], m_src[t][:], COPY)
-            return cols, dst
+        new_m = keep.tile([P, PACK, N], F32, name="new_m")
+        m_term = keep.tile([P, PACK, N], F32, name="m_term")
+        dw_sb = keep.tile([P, PACK, N], F32, name="dw_sb", tag="y0")
+        dw_term = keep.tile([P, PACK, N], F32, name="dw_term", tag="y1")
 
-        m_cols, m_dst = gather_m(0)
+        def update_w(t):
+            nc.scalar.activation(dw_term[:, t, :], dw[t][:], COPY, scale=-LR * (1.0 + BETA))
+            nc.gpsimd.tensor_tensor(w_cols[:, t, :], w_cols[:, t, :], dw_term[:, t, :], ADD)
+            nc.scalar.activation(m_term[:, t, :], m_cols[:, t, :], COPY, scale=-LR * BETA * BETA)
+            nc.gpsimd.tensor_tensor(w_cols[:, t, :], w_cols[:, t, :], m_term[:, t, :], ADD)
+
+        def update_m(t):
+            if t == 0:
+                nc.vector.scalar_tensor_tensor(
+                    out=new_m[:, t, :], in0=m_cols[:, t, :], scalar=BETA, in1=dw[t][:], op0=MULT, op1=ADD)
+            else:
+                nc.scalar.activation(new_m[:, t, :], m_cols[:, t, :], COPY, scale=BETA)
+                nc.scalar.copy(dw_sb[:, t, :], dw[t][:])
+                nc.gpsimd.tensor_tensor(new_m[:, t, :], new_m[:, t, :], dw_sb[:, t, :], ADD)
+
+        def scatter(dst, cols, out, t):
+            nc.vector.tensor_copy(dst[:].indirect(offsets[:]), cols[:, t, :])
+            nc.sync.dma_start(out=plane(out, t), in_=dst[:])
+
         for t in range(PACK):
-            base = ring.tile([P, N], F32, name="base")
-            new_m = ring.tile([P, N], F32, name="new_m")
-            new_w = ring.tile([P, N], F32, name="new_w")
-            nc.vector.scalar_tensor_tensor(
-                out=base[:], in0=m_cols[:], scalar=-LR * BETA * BETA, in1=w_cols[:, t, :], op0=MULT, op1=ADD)
-            nc.vector.scalar_tensor_tensor(
-                out=new_m[:], in0=m_cols[:], scalar=BETA, in1=dw[t][:], op0=MULT, op1=ADD)
-            nc.vector.scalar_tensor_tensor(
-                out=new_w[:], in0=dw[t][:], scalar=-LR * (1.0 + BETA), in1=base[:], op0=MULT, op1=ADD)
-            this_dst = m_dst
+            update_m(t)
+            if t > 0:
+                m_dst = second_copy("m_dst%d" % t, m_src[t], "shared%d" % t)
+            scatter(m_dst, new_m, out_1, t)
             if t + 1 < PACK:
-                m_cols, m_dst = gather_m(t + 1)
-            nc.vector.tensor_copy(w_dst[t][:].indirect(offsets[:]), new_w[:])
-            nc.sync.dma_start(out=plane(out_0, t), in_=w_dst[t][:])
-            nc.vector.tensor_copy(this_dst[:].indirect(offsets[:]), new_m[:])
-            nc.sync.dma_start(out=plane(out_1, t), in_=this_dst[:])
+                gather_m(t + 1)
+            update_w(t)
+            scatter(w_dst[t], w_cols, out_0, t)

@@ -52,12 +52,14 @@ def tile_attend_gsq_nag_kernel(tc, xT, wT, y, wt, xm, mT, offs, out_0, out_1):
                 nc.vector.tensor_copy(out=dst[:, on_scalar:], in_=src[:, on_scalar:])
             return grouped
 
-        def group_moving(name, planes):
+        def group_moving(name, planes, on_scalar=0):
             grouped = keep.tile([P, N * PACK], BF16, name=name, align_bytes=64)
-            nc.vector.tensor_copy(
-                out=grouped[:].rearrange("p (c i t) -> p c t i", i=4, t=PACK),
-                in_=planes[:].rearrange("p t (c i) -> p c t i", i=4),
-            )
+            dst = grouped[:].rearrange("p (c i t) -> p c t i", i=4, t=PACK)
+            src = planes[:].rearrange("p t (c i) -> p c t i", i=4)
+            if on_scalar:
+                nc.scalar.copy(out=dst, in_=src)
+            else:
+                nc.vector.tensor_copy(out=dst, in_=src)
             return grouped
 
         offsets = lists.tile([P, N // 16], U16, name="offsets")
@@ -69,16 +71,20 @@ def tile_attend_gsq_nag_kernel(tc, xT, wT, y, wt, xm, mT, offs, out_0, out_1):
         wt_sb = keep.tile([P, HALVES, PACK], F32, name="wt_sb")
 
         nc.scalar.dma_start(out=wt_sb[:], in_=wt[0].rearrange("(h p t) o -> p h (t o)", h=HALVES, t=PACK))
-        nc.sync.dma_start(offsets[:], offs)
         for t in range(PACK):
             nc.sync.dma_start(out=w_src[t][:], in_=plane(wT, t))
-        nc.sync.dma_start(out=x_raw[0][:], in_=rows(xT[0, :, 0:K]))
-        nc.sync.dma_start(out=y_sb[0][:], in_=rows(y[0, 0:K, :]))
-        nc.sync.dma_start(out=x_raw[1][:], in_=rows(xT[0, :, K:R]))
-        nc.sync.dma_start(out=y_sb[1][:], in_=rows(y[0, K:R, :]))
+            if t == 0:
+                nc.sync.dma_start(offsets[:], offs)
+        for h in range(HALVES):
+            nc.sync.dma_start(out=x_raw[h][:], in_=rows(xT[0, :, h * K : (h + 1) * K]))
+        for h in range(HALVES):
+            for pair in (slice(0, 2), slice(2, 4)):
+                nc.sync.dma_start(out=y_sb[h][:, pair, :], in_=rows(y[0, h * K : (h + 1) * K, :])[:, pair, :])
         for h in range(HALVES):
             nc.sync.dma_start(out=xm_raw[h][:], in_=rows(xm[0, h * K : (h + 1) * K, :]))
-        for t in range(PACK):
+        for half in (slice(0, T // 2), slice(T // 2, T)):
+            nc.sync.dma_start(out=m_src[0][:, half], in_=plane(mT, 0)[:, half])
+        for t in range(1, PACK):
             nc.sync.dma_start(out=m_src[t][:], in_=plane(mT, t))
 
         w_cols = keep.tile([P, PACK, N], F32, name="w_cols")
@@ -95,11 +101,16 @@ def tile_attend_gsq_nag_kernel(tc, xT, wT, y, wt, xm, mT, offs, out_0, out_1):
             w_dst.append(second_copy("w_dst%d" % t, w_src[t], "w_dst%d" % t))
         w_codes, w_scales = quantise("w", group_moving("w_grouped", w_cols), E4M3)
         x_q = [quantise("x0", group_stationary("x_grouped0", x_raw[0], on_scalar=80), E4M3)]
+        x_q.append(quantise("x1", group_stationary("x_grouped1", x_raw[1], on_scalar=56), E4M3))
 
         def residual(h):
             codes, scales = x_q[h]
             for t in range(PACK):
-                nc.scalar.activation(y_sb[h][:, t, :], y_sb[h][:, t, :], COPY, scale=wt_sb[:, h, t : t + 1])
+                if h == 0:
+                    nc.scalar.activation(y_sb[h][:, t, :], y_sb[h][:, t, :], COPY, scale=wt_sb[:, h, t : t + 1])
+                else:
+                    nc.gpsimd.tensor_scalar(
+                        y_sb[h][:, t, :], y_sb[h][:, t, :], wt_sb[:, h, t : t + 1], 0.0, MULT, ADD)
             for t in range(PACK):
                 cols = slice(t * P, (t + 1) * P)
                 a = psum.tile([P, N], F32, name="a%d%d" % (h, t), tag="bank%d" % (PACK * h + t))
@@ -111,16 +122,15 @@ def tile_attend_gsq_nag_kernel(tc, xT, wT, y, wt, xm, mT, offs, out_0, out_1):
                     out=y_sb[h][:, t, :], in0=a[:], scalar=wt_sb[:, h, t : t + 1], in1=y_sb[h][:, t, :],
                     op0=MULT, op1=SUB,
                 )
-            return group_moving("g_grouped%d" % h, y_sb[h])
 
-        g_grouped0 = residual(0)
-        x_grouped1 = group_stationary("x_grouped1", x_raw[1])
-        x_q.append(quantise("x1", x_grouped1, E4M3))
+        residual(0)
+        residual(1)
+        g_grouped0 = group_moving("g_grouped0", y_sb[0], on_scalar=True)
+        g_grouped1 = group_moving("g_grouped1", y_sb[1])
         g_q = [quantise("g0", g_grouped0, E5M2)]
-        g_grouped1 = residual(1)
         xm_q = [quantise("xm0", group_stationary("xm_grouped0", xm_raw[0]), E4M3)]
         g_q.append(quantise("g1", g_grouped1, E5M2))
-        xm_grouped1 = group_stationary("xm_grouped1", xm_raw[1])
+        xm_grouped1 = group_stationary("xm_grouped1", xm_raw[1], on_scalar=96)
         m_cols = keep.tile([P, PACK, N], F32, name="m_cols")
 
         def gather_m(t):
@@ -168,7 +178,11 @@ def tile_attend_gsq_nag_kernel(tc, xT, wT, y, wt, xm, mT, offs, out_0, out_1):
 
         def scatter(dst, cols, out, t):
             nc.vector.tensor_copy(dst[:].indirect(offsets[:]), cols[:, t, :])
-            nc.sync.dma_start(out=plane(out, t), in_=dst[:])
+            if out is out_0 and t == PACK - 1:
+                nc.sync.dma_start(out=plane(out, t)[:, : T // 2], in_=dst[:, : T // 2])
+                nc.scalar.dma_start(out=plane(out, t)[:, T // 2 :], in_=dst[:, T // 2 :])
+            else:
+                nc.sync.dma_start(out=plane(out, t), in_=dst[:])
 
         for t in range(PACK):
             update_m(t)

@@ -22,6 +22,7 @@ P = 128
 PACK = 4
 K = P * PACK
 HALVES = R // K
+LATE = 128
 
 
 def tile_attend_gsq_nag_kernel(tc, xT, wT, y, wt, xm, mT, offs, out_0, out_1):
@@ -37,30 +38,32 @@ def tile_attend_gsq_nag_kernel(tc, xT, wT, y, wt, xm, mT, offs, out_0, out_1):
         def rows(src):
             return src.rearrange("(p j) c -> p j c", j=PACK)
 
-        def quantise(name, grouped, fmt):
+        def operand(name, scales_tag=None):
+            grouped = keep.tile([P, K * PACK], BF16, name=name + "_grouped", align_bytes=64)
             codes = keep.tile([P, K], U32, name=name + "_codes", align_bytes=64)
-            scales = keep.tile([P, K], U8, name=name + "_scales", align_bytes=64)
-            nc.vector.quantize_mx(out=codes[:].bitcast(fmt), scales=scales[:], in_=grouped[:])
-            return codes, scales
+            scales = keep.tile([P, K], U8, name=name + "_scales", tag=scales_tag or name + "_scales", align_bytes=64)
+            return grouped, codes, scales
 
-        def group_stationary(name, raw, on_scalar=P):
-            grouped = keep.tile([P, K * PACK], BF16, name=name, align_bytes=64)
-            dst = grouped[:].rearrange("p (t m j) -> p m j t", t=PACK, j=PACK)
-            src = raw[:].rearrange("p j (m t) -> p m j t", t=PACK)
-            nc.scalar.copy(out=dst[:, :on_scalar], in_=src[:, :on_scalar])
+        def quantise(op, fmt, lo=0, hi=K):
+            grouped, codes, scales = op
+            nc.vector.quantize_mx(
+                out=codes[:, lo:hi].bitcast(fmt), scales=scales[:, lo:hi], in_=grouped[:, PACK * lo : PACK * hi])
+
+        def weave(dst, src, on_scalar):
+            if on_scalar > 0:
+                nc.scalar.copy(out=dst[:, :on_scalar], in_=src[:, :on_scalar])
             if on_scalar < P:
                 nc.vector.tensor_copy(out=dst[:, on_scalar:], in_=src[:, on_scalar:])
-            return grouped
 
-        def group_moving(name, planes, on_scalar=0):
-            grouped = keep.tile([P, N * PACK], BF16, name=name, align_bytes=64)
-            dst = grouped[:].rearrange("p (c i t) -> p c t i", i=4, t=PACK)
+        def stationary_views(op, raw):
+            dst = op[0][:].rearrange("p (t m j) -> p m j t", t=PACK, j=PACK)
+            src = raw[:].rearrange("p j (m t) -> p m j t", t=PACK)
+            return dst, src
+
+        def moving_views(op, planes):
+            dst = op[0][:].rearrange("p (c i t) -> p c t i", i=4, t=PACK)
             src = planes[:].rearrange("p t (c i) -> p c t i", i=4)
-            if on_scalar:
-                nc.scalar.copy(out=dst, in_=src)
-            else:
-                nc.vector.tensor_copy(out=dst, in_=src)
-            return grouped
+            return dst, src
 
         offsets = lists.tile([P, N // 16], U16, name="offsets")
         x_raw = [keep.tile([P, PACK, K], F32, name="x_raw%d" % h, tag="shared%d" % h) for h in range(HALVES)]
@@ -68,98 +71,118 @@ def tile_attend_gsq_nag_kernel(tc, xT, wT, y, wt, xm, mT, offs, out_0, out_1):
         y_sb = [keep.tile([P, PACK, N], F32, name="y_sb%d" % h, tag="y%d" % h) for h in range(HALVES)]
         w_src = [keep.tile([P, T], F32, name="w_src%d" % t) for t in range(PACK)]
         m_src = [keep.tile([P, T], F32, name="m_src%d" % t) for t in range(PACK)]
-        wt_sb = keep.tile([P, HALVES, PACK], F32, name="wt_sb")
+        wt_sb = [keep.tile([P, PACK], F32, name="wt_sb%d" % h, tag="wt%d" % h, align_bytes=64) for h in range(HALVES)]
 
-        nc.scalar.dma_start(out=wt_sb[:], in_=wt[0].rearrange("(h p t) o -> p h (t o)", h=HALVES, t=PACK))
+        def load_x(h):
+            nc.sync.dma_start(out=x_raw[h][:], in_=rows(xT[0, :, h * K : (h + 1) * K]))
+
+        def load_y(h):
+            for pair in (slice(0, 2), slice(2, 4)):
+                nc.sync.dma_start(out=y_sb[h][:, pair, :], in_=rows(y[0, h * K : (h + 1) * K, :])[:, pair, :])
+
+        for h in range(HALVES):
+            nc.scalar.dma_start(out=wt_sb[h][:], in_=wt[0, h * K : (h + 1) * K, :].rearrange("(p t) o -> p (t o)", t=PACK))
         for t in range(PACK):
             nc.sync.dma_start(out=w_src[t][:], in_=plane(wT, t))
             if t == 0:
                 nc.sync.dma_start(offsets[:], offs)
-        for h in range(HALVES):
-            nc.sync.dma_start(out=x_raw[h][:], in_=rows(xT[0, :, h * K : (h + 1) * K]))
-        for h in range(HALVES):
-            for pair in (slice(0, 2), slice(2, 4)):
-                nc.sync.dma_start(out=y_sb[h][:, pair, :], in_=rows(y[0, h * K : (h + 1) * K, :])[:, pair, :])
+        load_x(0)
+        load_x(1)
+        load_y(0)
+        load_y(1)
         for h in range(HALVES):
             nc.sync.dma_start(out=xm_raw[h][:], in_=rows(xm[0, h * K : (h + 1) * K, :]))
-        for half in (slice(0, T // 2), slice(T // 2, T)):
-            nc.sync.dma_start(out=m_src[0][:, half], in_=plane(mT, 0)[:, half])
-        for t in range(1, PACK):
-            nc.sync.dma_start(out=m_src[t][:], in_=plane(mT, t))
+        nc.sync.dma_start(out=m_src[0][:], in_=plane(mT, 0))
 
         w_cols = keep.tile([P, PACK, N], F32, name="w_cols")
+        w_dst = [keep.tile([P, T], F32, name="w_dst%d" % t) for t in range(PACK - 1)]
 
-        def second_copy(name, src, tag):
-            dst = keep.tile([P, T], F32, name=name, tag=tag)
-            for half in (slice(0, T // 2), slice(T // 2, T)):
+        def fill(dst, src, last=T):
+            for half in (slice(0, T // 2), slice(T // 2, last)):
                 nc.scalar.activation(dst[:, half], src[:, half], COPY)
-            return dst
 
-        w_dst = []
+        w_op = operand("w")
+        x_op = [operand("x%d" % h) for h in range(HALVES)]
+        g_op = [operand("g0", "wt1"), operand("g1")]
+        xm_op = [operand("xm%d" % h) for h in range(HALVES)]
+
         for t in range(PACK):
             nc.vector.tensor_copy(w_cols[:, t, :], w_src[t][:].indirect(offsets[:]))
-            w_dst.append(second_copy("w_dst%d" % t, w_src[t], "w_dst%d" % t))
-        w_codes, w_scales = quantise("w", group_moving("w_grouped", w_cols), E4M3)
-        x_q = [quantise("x0", group_stationary("x_grouped0", x_raw[0], on_scalar=80), E4M3)]
-        x_q.append(quantise("x1", group_stationary("x_grouped1", x_raw[1], on_scalar=56), E4M3))
+            if t < 3:
+                fill(w_dst[t], w_src[t])
+        weave(*moving_views(w_op, w_cols), on_scalar=40)
+        quantise(w_op, E4M3)
 
-        def residual(h):
-            codes, scales = x_q[h]
+        def weigh_y(h, on_scalar):
             for t in range(PACK):
-                if h == 0:
-                    nc.scalar.activation(y_sb[h][:, t, :], y_sb[h][:, t, :], COPY, scale=wt_sb[:, h, t : t + 1])
+                if t < on_scalar:
+                    nc.scalar.activation(y_sb[h][:, t, :], y_sb[h][:, t, :], COPY, scale=wt_sb[h][:, t : t + 1])
                 else:
                     nc.gpsimd.tensor_scalar(
-                        y_sb[h][:, t, :], y_sb[h][:, t, :], wt_sb[:, h, t : t + 1], 0.0, MULT, ADD)
+                        y_sb[h][:, t, :], y_sb[h][:, t, :], wt_sb[h][:, t : t + 1], 0.0, MULT, ADD)
+
+        def residual(h):
+            grouped, codes, scales = x_op[h]
             for t in range(PACK):
                 cols = slice(t * P, (t + 1) * P)
                 a = psum.tile([P, N], F32, name="a%d%d" % (h, t), tag="bank%d" % (PACK * h + t))
                 nc.tensor.matmul_mx(
                     out=a[:], lhsT=codes[:, cols].bitcast(E4M3), lhsT_scale=scales[:, cols],
-                    rhs=w_codes[:].bitcast(E4M3), rhs_scale=w_scales[:], start=True, stop=True,
+                    rhs=w_op[1][:].bitcast(E4M3), rhs_scale=w_op[2][:], start=True, stop=True,
                 )
                 nc.vector.scalar_tensor_tensor(
-                    out=y_sb[h][:, t, :], in0=a[:], scalar=wt_sb[:, h, t : t + 1], in1=y_sb[h][:, t, :],
+                    out=y_sb[h][:, t, :], in0=a[:], scalar=wt_sb[h][:, t : t + 1], in1=y_sb[h][:, t, :],
                     op0=MULT, op1=SUB,
                 )
 
+        weave(*stationary_views(x_op[0], x_raw[0]), on_scalar=64)
+        quantise(x_op[0], E4M3)
+        weave(*stationary_views(x_op[1], x_raw[1]), on_scalar=44)
+        quantise(x_op[1], E4M3)
+        weigh_y(0, 4)
         residual(0)
+        weigh_y(1, 0)
+        weave(*moving_views(g_op[0], y_sb[0]), on_scalar=128)
         residual(1)
-        g_grouped0 = group_moving("g_grouped0", y_sb[0], on_scalar=True)
-        g_grouped1 = group_moving("g_grouped1", y_sb[1])
-        g_q = [quantise("g0", g_grouped0, E5M2)]
-        xm_q = [quantise("xm0", group_stationary("xm_grouped0", xm_raw[0]), E4M3)]
-        g_q.append(quantise("g1", g_grouped1, E5M2))
-        xm_grouped1 = group_stationary("xm_grouped1", xm_raw[1], on_scalar=96)
-        m_cols = keep.tile([P, PACK, N], F32, name="m_cols")
-
-        def gather_m(t):
-            nc.vector.tensor_copy(m_cols[:, t, :], m_src[t][:].indirect(offsets[:]))
-
-        codes = keep.tile([P, K], U32, name="xm1_codes", align_bytes=64)
-        scales = keep.tile([P, K], U8, name="xm1_scales", align_bytes=64)
-        for lo, hi in ((0, P), (P, 2 * P), (2 * P, K)):
-            nc.vector.quantize_mx(
-                out=codes[:, lo:hi].bitcast(E4M3), scales=scales[:, lo:hi], in_=xm_grouped1[:, PACK * lo : PACK * hi])
-            if lo == 0:
-                gather_m(0)
-                m_dst = second_copy("m_dst0", m_src[0], "shared0")
-        xm_q.append((codes, scales))
+        weave(*moving_views(g_op[1], y_sb[1]), on_scalar=0)
+        quantise(g_op[0], E5M2)
+        quantise(g_op[1], E5M2)
+        weave(*stationary_views(xm_op[0], xm_raw[0]), on_scalar=128)
+        dst, src = stationary_views(xm_op[1], xm_raw[1])
+        nc.vector.tensor_copy(out=dst[:, :, :, 0], in_=src[:, :, :, 0])
+        nc.scalar.copy(out=dst[:, :, :, 1:], in_=src[:, :, :, 1:])
 
         dw = [psum.tile([P, N], F32, name="dw%d" % t, tag="bank%d" % t) for t in range(PACK)]
-        for t in range(PACK):
+
+        def gradient(t):
             for h in range(HALVES):
                 cols = slice(t * P, (t + 1) * P)
                 nc.tensor.matmul_mx(
-                    out=dw[t][:], lhsT=xm_q[h][0][:, cols].bitcast(E4M3), lhsT_scale=xm_q[h][1][:, cols],
-                    rhs=g_q[h][0][:].bitcast(E5M2), rhs_scale=g_q[h][1][:],
+                    out=dw[t][:], lhsT=xm_op[h][1][:, cols].bitcast(E4M3), lhsT_scale=xm_op[h][2][:, cols],
+                    rhs=g_op[h][1][:].bitcast(E5M2), rhs_scale=g_op[h][2][:],
                     start=(h == 0), stop=(h == HALVES - 1),
                 )
 
+        m_cols = keep.tile([P, PACK, N], F32, name="m_cols")
         new_m = keep.tile([P, PACK, N], F32, name="new_m")
         m_term = keep.tile([P, PACK, N], F32, name="m_term")
         dw_sb = keep.tile([P, PACK, N], F32, name="dw_sb", tag="y0")
         dw_term = keep.tile([P, PACK, N], F32, name="dw_term", tag="y1")
+
+        w_dst.append(keep.tile([P, T], F32, name="w_dst3", tag="shared3"))
+        m_dst = []
+        for t, tag in enumerate(("shared0", "shared1", "m_dst2", "shared2")):
+            m_dst.append(keep.tile([P, T], F32, name="m_dst%d" % t, tag=tag))
+        for t in range(1, PACK):
+            nc.sync.dma_start(out=m_src[t][:], in_=plane(mT, t))
+            nc.sync.dma_start(out=m_dst[t - 1][:, T - LATE :], in_=plane(mT, t - 1)[:, T - LATE :])
+
+        def store(dst, out, t):
+            if out is out_1 and t == PACK - 1:
+                nc.sync.dma_start(out=plane(out, t)[:, : T // 2], in_=dst[:, : T // 2])
+                nc.scalar.dma_start(out=plane(out, t)[:, T // 2 :], in_=dst[:, T // 2 :])
+            else:
+                nc.sync.dma_start(out=plane(out, t), in_=dst[:])
 
         def update_w(t):
             nc.scalar.activation(dw_term[:, t, :], dw[t][:], COPY, scale=-LR * (1.0 + BETA))
@@ -167,29 +190,36 @@ def tile_attend_gsq_nag_kernel(tc, xT, wT, y, wt, xm, mT, offs, out_0, out_1):
             nc.scalar.activation(m_term[:, t, :], m_cols[:, t, :], COPY, scale=-LR * BETA * BETA)
             nc.gpsimd.tensor_tensor(w_cols[:, t, :], w_cols[:, t, :], m_term[:, t, :], ADD)
 
-        def update_m(t):
-            if t == 0:
-                nc.vector.scalar_tensor_tensor(
-                    out=new_m[:, t, :], in0=m_cols[:, t, :], scalar=BETA, in1=dw[t][:], op0=MULT, op1=ADD)
-            else:
-                nc.scalar.activation(new_m[:, t, :], m_cols[:, t, :], COPY, scale=BETA)
-                nc.scalar.copy(dw_sb[:, t, :], dw[t][:])
-                nc.gpsimd.tensor_tensor(new_m[:, t, :], new_m[:, t, :], dw_sb[:, t, :], ADD)
+        def update_m(t, src, scale):
+            nc.scalar.activation(new_m[:, t, :], src[:, t, :], COPY, scale=scale)
+            nc.scalar.copy(dw_sb[:, t, :], dw[t][:])
+            nc.gpsimd.tensor_tensor(new_m[:, t, :], new_m[:, t, :], dw_sb[:, t, :], ADD)
 
-        def scatter(dst, cols, out, t):
-            nc.vector.tensor_copy(dst[:].indirect(offsets[:]), cols[:, t, :])
-            if out is out_0 and t == PACK - 1:
-                nc.sync.dma_start(out=plane(out, t)[:, : T // 2], in_=dst[:, : T // 2])
-                nc.scalar.dma_start(out=plane(out, t)[:, T // 2 :], in_=dst[:, T // 2 :])
-            else:
-                nc.sync.dma_start(out=plane(out, t), in_=dst[:])
-
+        quantise(xm_op[0], E4M3)
+        quantise(xm_op[1], E4M3, 0, P)
+        gradient(0)
+        nc.vector.tensor_scalar(
+            m_term[:, 0, :], m_src[0][:].indirect(offsets[:]), -LR * BETA * BETA, 0.0, MULT, ADD)
+        nc.vector.scalar_tensor_tensor(
+            out=dw_term[:, 0, :], in0=dw[0][:], scalar=-LR * (1.0 + BETA), in1=m_term[:, 0, :], op0=MULT, op1=ADD)
+        nc.vector.tensor_tensor(w_dst[0][:].indirect(offsets[:]), w_cols[:, 0, :], dw_term[:, 0, :], ADD)
+        store(w_dst[0], out_0, 0)
+        for h in range(1, HALVES):
+            quantise(xm_op[h], E4M3, P, 2 * P)
+            quantise(xm_op[h], E4M3, 2 * P, K)
+        for t in range(1, PACK):
+            gradient(t)
+        update_m(0, m_term, -1.0 / (LR * BETA))
         for t in range(PACK):
-            update_m(t)
-            if t > 0:
-                m_dst = second_copy("m_dst%d" % t, m_src[t], "shared%d" % t)
-            scatter(m_dst, new_m, out_1, t)
+            fill(m_dst[t], m_src[t], T if t == PACK - 1 else T - LATE)
             if t + 1 < PACK:
-                gather_m(t + 1)
-            update_w(t)
-            scatter(w_dst[t], w_cols, out_0, t)
+                nc.vector.tensor_copy(m_cols[:, t + 1, :], m_src[t + 1][:].indirect(offsets[:]))
+                update_w(t + 1)
+            nc.vector.tensor_copy(m_dst[t][:].indirect(offsets[:]), new_m[:, t, :])
+            store(m_dst[t], out_1, t)
+            if t + 1 < PACK:
+                if t + 1 >= 3:
+                    fill(w_dst[t + 1], w_src[t + 1])
+                update_m(t + 1, m_cols, BETA)
+                nc.vector.tensor_copy(w_dst[t + 1][:].indirect(offsets[:]), w_cols[:, t + 1, :])
+                store(w_dst[t + 1], out_0, t + 1)

@@ -22,7 +22,6 @@ P = 128
 PACK = 4
 K = P * PACK
 HALVES = R // K
-LATE = 128
 
 
 def tile_attend_gsq_nag_kernel(tc, xT, wT, y, wt, xm, mT, offs, out_0, out_1):
@@ -97,8 +96,8 @@ def tile_attend_gsq_nag_kernel(tc, xT, wT, y, wt, xm, mT, offs, out_0, out_1):
         w_cols = keep.tile([P, PACK, N], F32, name="w_cols")
         w_dst = [keep.tile([P, T], F32, name="w_dst%d" % t) for t in range(PACK - 1)]
 
-        def fill(dst, src, last=T):
-            for half in (slice(0, T // 2), slice(T // 2, last)):
+        def fill(dst, src):
+            for half in (slice(0, T // 2), slice(T // 2, T)):
                 nc.scalar.activation(dst[:, half], src[:, half], COPY)
 
         w_op = operand("w")
@@ -141,26 +140,25 @@ def tile_attend_gsq_nag_kernel(tc, xT, wT, y, wt, xm, mT, offs, out_0, out_1):
         quantise(x_op[1], E4M3)
         weigh_y(0, 4)
         residual(0)
-        weigh_y(1, 0)
+        weigh_y(1, 1)
         weave(*moving_views(g_op[0], y_sb[0]), on_scalar=128)
         residual(1)
         weave(*moving_views(g_op[1], y_sb[1]), on_scalar=0)
         quantise(g_op[0], E5M2)
         quantise(g_op[1], E5M2)
         weave(*stationary_views(xm_op[0], xm_raw[0]), on_scalar=128)
-        dst, src = stationary_views(xm_op[1], xm_raw[1])
-        nc.vector.tensor_copy(out=dst[:, :, :, 0], in_=src[:, :, :, 0])
-        nc.scalar.copy(out=dst[:, :, :, 1:], in_=src[:, :, :, 1:])
+        weave(*stationary_views(xm_op[1], xm_raw[1]), on_scalar=72)
 
         dw = [psum.tile([P, N], F32, name="dw%d" % t, tag="bank%d" % t) for t in range(PACK)]
 
         def gradient(t):
-            for h in range(HALVES):
+            order = (0, 1) if t == 0 else (1, 0)
+            for h in order:
                 cols = slice(t * P, (t + 1) * P)
                 nc.tensor.matmul_mx(
                     out=dw[t][:], lhsT=xm_op[h][1][:, cols].bitcast(E4M3), lhsT_scale=xm_op[h][2][:, cols],
                     rhs=g_op[h][1][:].bitcast(E5M2), rhs_scale=g_op[h][2][:],
-                    start=(h == 0), stop=(h == HALVES - 1),
+                    start=(h == order[0]), stop=(h == order[-1]),
                 )
 
         m_cols = keep.tile([P, PACK, N], F32, name="m_cols")
@@ -175,7 +173,6 @@ def tile_attend_gsq_nag_kernel(tc, xT, wT, y, wt, xm, mT, offs, out_0, out_1):
             m_dst.append(keep.tile([P, T], F32, name="m_dst%d" % t, tag=tag))
         for t in range(1, PACK):
             nc.sync.dma_start(out=m_src[t][:], in_=plane(mT, t))
-            nc.sync.dma_start(out=m_dst[t - 1][:, T - LATE :], in_=plane(mT, t - 1)[:, T - LATE :])
 
         def store(dst, out, t):
             if out is out_1 and t == PACK - 1:
@@ -196,7 +193,7 @@ def tile_attend_gsq_nag_kernel(tc, xT, wT, y, wt, xm, mT, offs, out_0, out_1):
             nc.gpsimd.tensor_tensor(new_m[:, t, :], new_m[:, t, :], dw_sb[:, t, :], ADD)
 
         quantise(xm_op[0], E4M3)
-        quantise(xm_op[1], E4M3, 0, P)
+        quantise(xm_op[1], E4M3)
         gradient(0)
         nc.vector.tensor_scalar(
             m_term[:, 0, :], m_src[0][:].indirect(offsets[:]), -LR * BETA * BETA, 0.0, MULT, ADD)
@@ -204,14 +201,11 @@ def tile_attend_gsq_nag_kernel(tc, xT, wT, y, wt, xm, mT, offs, out_0, out_1):
             out=dw_term[:, 0, :], in0=dw[0][:], scalar=-LR * (1.0 + BETA), in1=m_term[:, 0, :], op0=MULT, op1=ADD)
         nc.vector.tensor_tensor(w_dst[0][:].indirect(offsets[:]), w_cols[:, 0, :], dw_term[:, 0, :], ADD)
         store(w_dst[0], out_0, 0)
-        for h in range(1, HALVES):
-            quantise(xm_op[h], E4M3, P, 2 * P)
-            quantise(xm_op[h], E4M3, 2 * P, K)
         for t in range(1, PACK):
             gradient(t)
         update_m(0, m_term, -1.0 / (LR * BETA))
         for t in range(PACK):
-            fill(m_dst[t], m_src[t], T if t == PACK - 1 else T - LATE)
+            fill(m_dst[t], m_src[t])
             if t + 1 < PACK:
                 nc.vector.tensor_copy(m_cols[:, t + 1, :], m_src[t + 1][:].indirect(offsets[:]))
                 update_w(t + 1)

@@ -1,6 +1,7 @@
 from contextlib import ExitStack
 
 import concourse.mybir as mybir
+from concourse.masks import make_identity
 
 D, T, N, R = 512, 2048, 512, 1024
 LR, BETA = 0.1, 0.9
@@ -22,6 +23,11 @@ P = 128
 PACK = 4
 K = P * PACK
 HALVES = R // K
+BLOCKS = D // P
+CHUNKS = N // P
+X_ON_SCALAR = (0, 64)
+Y_ON_SCALAR = (4, 2)
+G_ON_SCALAR = (128, 0)
 
 
 def tile_attend_gsq_nag_kernel(tc, xT, wT, y, wt, xm, mT, offs, out_0, out_1):
@@ -31,90 +37,123 @@ def tile_attend_gsq_nag_kernel(tc, xT, wT, y, wt, xm, mT, offs, out_0, out_1):
         keep = ctx.enter_context(tc.tile_pool(name="keep", bufs=1))
         psum = ctx.enter_context(tc.psum_pool(name="psum", bufs=1))
 
-        def plane(table, t):
-            return table.rearrange("(p t) c -> p t c", t=PACK)[:, t, :]
+        def block(table, b):
+            return table[b * P : (b + 1) * P, :]
 
         def rows(src):
             return src.rearrange("(p j) c -> p j c", j=PACK)
 
-        def operand(name, scales_tag=None):
-            grouped = keep.tile([P, K * PACK], BF16, name=name + "_grouped", align_bytes=64)
-            codes = keep.tile([P, K], U32, name=name + "_codes", align_bytes=64)
-            scales = keep.tile([P, K], U8, name=name + "_scales", tag=scales_tag or name + "_scales", align_bytes=64)
+        def operand(name, width=K, codes_tag=None):
+            grouped = keep.tile([P, width * PACK], BF16, name=name + "_grouped", align_bytes=64)
+            codes = keep.tile([P, width], U32, name=name + "_codes", tag=codes_tag or name + "_codes", align_bytes=64)
+            scales = keep.tile([P, width], U8, name=name + "_scales", align_bytes=64)
             return grouped, codes, scales
 
-        def quantise(op, fmt, lo=0, hi=K):
+        def quantise(op, fmt):
             grouped, codes, scales = op
-            nc.vector.quantize_mx(
-                out=codes[:, lo:hi].bitcast(fmt), scales=scales[:, lo:hi], in_=grouped[:, PACK * lo : PACK * hi])
+            nc.vector.quantize_mx(out=codes[:].bitcast(fmt), scales=scales[:], in_=grouped[:])
 
         def weave(dst, src, on_scalar):
             if on_scalar > 0:
                 nc.scalar.copy(out=dst[:, :on_scalar], in_=src[:, :on_scalar])
-            if on_scalar < P:
+            if on_scalar < dst.shape[1]:
                 nc.vector.tensor_copy(out=dst[:, on_scalar:], in_=src[:, on_scalar:])
 
-        def stationary_views(op, raw):
+        def dealt_views(op, raw):
             dst = op[0][:].rearrange("p (t m j) -> p m j t", t=PACK, j=PACK)
             src = raw[:].rearrange("p j (m t) -> p m j t", t=PACK)
             return dst, src
 
-        def moving_views(op, planes):
-            dst = op[0][:].rearrange("p (c i t) -> p c t i", i=4, t=PACK)
-            src = planes[:].rearrange("p t (c i) -> p c t i", i=4)
+        def plain_views(grouped, planes):
+            dst = grouped.rearrange("p (c i t) -> p c t i", i=4, t=PACK)
+            src = planes.rearrange("p t (c i) -> p c t i", i=4)
             return dst, src
 
         offsets = lists.tile([P, N // 16], U16, name="offsets")
         x_raw = [keep.tile([P, PACK, K], F32, name="x_raw%d" % h, tag="shared%d" % h) for h in range(HALVES)]
-        xm_raw = [keep.tile([P, PACK, D], F32, name="xm_raw%d" % h, tag="shared%d" % (2 + h)) for h in range(HALVES)]
         y_sb = [keep.tile([P, PACK, N], F32, name="y_sb%d" % h, tag="y%d" % h) for h in range(HALVES)]
-        w_src = [keep.tile([P, T], F32, name="w_src%d" % t) for t in range(PACK)]
-        m_src = [keep.tile([P, T], F32, name="m_src%d" % t) for t in range(PACK)]
-        wt_sb = [keep.tile([P, PACK], F32, name="wt_sb%d" % h, tag="wt%d" % h, align_bytes=64) for h in range(HALVES)]
-
-        def load_x(h):
-            nc.sync.dma_start(out=x_raw[h][:], in_=rows(xT[0, :, h * K : (h + 1) * K]))
-
-        def load_y(h):
-            for pair in (slice(0, 2), slice(2, 4)):
-                nc.sync.dma_start(out=y_sb[h][:, pair, :], in_=rows(y[0, h * K : (h + 1) * K, :])[:, pair, :])
+        xm_first = [keep.tile([P, PACK, P], F32, name="xm_first%d" % h) for h in range(HALVES)]
+        xm_rest = [keep.tile([P, PACK, D - P], F32, name="xm_rest%d" % h, tag="rest%d" % h) for h in range(HALVES)]
+        w_src = [keep.tile([P, T], F32, name="w_src%d" % b, tag="table%d" % b) for b in range(BLOCKS)]
+        m_src = [keep.tile([P, T], F32, name="m_src%d" % b) for b in range(BLOCKS)]
+        wt_sb = [keep.tile([P, PACK], F32, name="wt_sb%d" % h, align_bytes=64) for h in range(HALVES)]
+        ident = keep.tile([P, P], F32, name="ident")
+        make_identity(nc, ident[:])
 
         for h in range(HALVES):
             nc.scalar.dma_start(out=wt_sb[h][:], in_=wt[0, h * K : (h + 1) * K, :].rearrange("(p t) o -> p (t o)", t=PACK))
-        for t in range(PACK):
-            nc.sync.dma_start(out=w_src[t][:], in_=plane(wT, t))
-            if t == 0:
+        for b in range(BLOCKS):
+            nc.sync.dma_start(out=w_src[b][:], in_=block(wT, b))
+            if b == 0:
                 nc.sync.dma_start(offsets[:], offs)
-        load_x(0)
-        load_x(1)
-        load_y(0)
-        load_y(1)
         for h in range(HALVES):
-            nc.sync.dma_start(out=xm_raw[h][:], in_=rows(xm[0, h * K : (h + 1) * K, :]))
-        nc.sync.dma_start(out=m_src[0][:], in_=plane(mT, 0))
+            nc.sync.dma_start(out=x_raw[h][:], in_=rows(xT[0, :, h * K : (h + 1) * K]))
+        for h in range(HALVES):
+            for pair in (slice(0, 2), slice(2, 4)):
+                nc.sync.dma_start(out=y_sb[h][:, pair, :], in_=rows(y[0, h * K : (h + 1) * K, :])[:, pair, :])
+        for h in range(HALVES):
+            nc.sync.dma_start(out=xm_first[h][:], in_=rows(xm[0, h * K : (h + 1) * K, :P]))
+        nc.sync.dma_start(out=m_src[0][:], in_=block(mT, 0))
+        for h in range(HALVES):
+            nc.sync.dma_start(out=xm_rest[h][:], in_=rows(xm[0, h * K : (h + 1) * K, P:]))
+        for b in range(1, BLOCKS):
+            nc.sync.dma_start(out=m_src[b][:], in_=block(mT, b))
 
-        w_cols = keep.tile([P, PACK, N], F32, name="w_cols")
-        w_dst = [keep.tile([P, T], F32, name="w_dst%d" % t) for t in range(PACK - 1)]
+        w_cols = keep.tile([P, BLOCKS, N], F32, name="w_cols")
+        w_dst = [keep.tile([P, T], F32, name="w_dst%d" % b) for b in range(2)]
+        w_turned = [keep.tile([P, 2, 2, P, 2], BF16, name="w_turned%d" % i, align_bytes=64) for i in range(CHUNKS // 2)]
 
         def fill(dst, src):
             for half in (slice(0, T // 2), slice(T // 2, T)):
                 nc.scalar.activation(dst[:, half], src[:, half], COPY)
 
-        w_op = operand("w")
         x_op = [operand("x%d" % h) for h in range(HALVES)]
-        g_op = [operand("g0", "wt1"), operand("g1")]
-        xm_op = [operand("xm%d" % h) for h in range(HALVES)]
+        w_op = operand("w", codes_tag="x0_grouped")
+        g_op = [operand("g%d" % h) for h in range(HALVES)]
+        xm_ops = [operand("xm0", HALVES * P), operand("xm12", 2 * HALVES * P), operand("xm3", HALVES * P)]
+        xm_place = [(0, 0), (1, 0), (1, HALVES * P), (2, 0)]
 
-        for t in range(PACK):
-            nc.vector.tensor_copy(w_cols[:, t, :], w_src[t][:].indirect(offsets[:]))
-            if t < 3:
-                fill(w_dst[t], w_src[t])
-        weave(*moving_views(w_op, w_cols), on_scalar=40)
+        def turn(b, chunks):
+            cols = slice(chunks[0] * P, (chunks[-1] + 1) * P)
+            nc.vector.tensor_copy(w_cols[:, b, cols], w_src[b][:].indirect(offsets[:, cols.start // 16 : cols.stop // 16]))
+            turned = psum.tile([P, len(chunks), P], F32, name="turned%d%d" % (b, chunks[0]), tag="bank%d" % (b + chunks[0] // 2))
+            for i, c in enumerate(chunks):
+                nc.tensor.transpose(turned[:, i, :], w_cols[:, b, c * P : (c + 1) * P], ident[:])
+            for i in range(0, len(chunks), 2):
+                nc.scalar.copy(
+                    out=w_turned[chunks[i] // 2][:, :, :, 32 * b : 32 * (b + 1), :].rearrange("s c u q e -> s c q u e"),
+                    in_=turned[:, i : i + 2, :].rearrange("s c (q u e) -> s c q u e", u=2, e=2))
+
+        w_words = w_op[0][:].bitcast(F32)
+
+        def turn_back(pair):
+            back = psum.tile([P, 2, 2, P], F32, name="back%d" % pair, tag="bank%d" % (5 + pair))
+            words = w_turned[pair][:].rearrange("s c u q e -> s (c u q e)").bitcast(F32)
+            for c in range(2):
+                for u in range(2):
+                    k = 2 * c + u
+                    nc.tensor.transpose(back[:, c, u, :], words[:, k * P : (k + 1) * P], ident[:])
+            dst = w_words[:, pair * K : (pair + 1) * K].rearrange("p (c s u) -> p c s u", c=2, u=2)
+            nc.scalar.copy(out=dst, in_=back[:].rearrange("p c u s -> p c s u"))
+
+        fill(w_dst[0], w_src[0])
+        turn(0, (0, 1, 2, 3))
+        fill(w_dst[1], w_src[1])
+        turn(1, (0, 1, 2, 3))
+        turn(2, (0, 1, 2, 3))
+        turn(3, (0, 1))
+        turn(3, (2, 3))
+        turn_back(0)
+        turn_back(1)
+        weave(*dealt_views(x_op[0], x_raw[0]), on_scalar=X_ON_SCALAR[0])
+        quantise(x_op[0], E4M3)
         quantise(w_op, E4M3)
+        weave(*dealt_views(x_op[1], x_raw[1]), on_scalar=X_ON_SCALAR[1])
+        quantise(x_op[1], E4M3)
 
-        def weigh_y(h, on_scalar):
+        def weigh_y(h):
             for t in range(PACK):
-                if t < on_scalar:
+                if t < Y_ON_SCALAR[h]:
                     nc.scalar.activation(y_sb[h][:, t, :], y_sb[h][:, t, :], COPY, scale=wt_sb[h][:, t : t + 1])
                 else:
                     nc.gpsimd.tensor_scalar(
@@ -134,86 +173,100 @@ def tile_attend_gsq_nag_kernel(tc, xT, wT, y, wt, xm, mT, offs, out_0, out_1):
                     op0=MULT, op1=SUB,
                 )
 
-        weave(*stationary_views(x_op[0], x_raw[0]), on_scalar=64)
-        quantise(x_op[0], E4M3)
-        weave(*stationary_views(x_op[1], x_raw[1]), on_scalar=44)
-        quantise(x_op[1], E4M3)
-        weigh_y(0, 4)
+        def weave_xm(b):
+            for h in range(HALVES):
+                raw = xm_first[h][:] if b == 0 else xm_rest[h][:, :, (b - 1) * P : b * P]
+                op, first = xm_place[b]
+                lo = PACK * (first + h * P)
+                dst, src = plain_views(xm_ops[op][0][:, lo : lo + K], raw)
+                nc.scalar.copy(out=dst, in_=src)
+
+        weigh_y(0)
         residual(0)
-        weigh_y(1, 1)
-        weave(*moving_views(g_op[0], y_sb[0]), on_scalar=128)
+        weigh_y(1)
+        weave(*plain_views(g_op[0][0][:], y_sb[0][:]), on_scalar=G_ON_SCALAR[0])
+        weave_xm(0)
         residual(1)
-        weave(*moving_views(g_op[1], y_sb[1]), on_scalar=0)
+        weave(*plain_views(g_op[1][0][:], y_sb[1][:]), on_scalar=G_ON_SCALAR[1])
         quantise(g_op[0], E5M2)
+        quantise(xm_ops[0], E4M3)
         quantise(g_op[1], E5M2)
-        weave(*stationary_views(xm_op[0], xm_raw[0]), on_scalar=128)
-        weave(*stationary_views(xm_op[1], xm_raw[1]), on_scalar=72)
 
-        dw = [psum.tile([P, N], F32, name="dw%d" % t, tag="bank%d" % t) for t in range(PACK)]
+        dw = [psum.tile([P, N], F32, name="dw%d" % b, tag="bank%d" % b) for b in range(BLOCKS)]
 
-        def gradient(t):
-            order = (0, 1) if t == 0 else (1, 0)
-            for h in order:
-                cols = slice(t * P, (t + 1) * P)
+        def gradient(b):
+            for h in range(HALVES):
+                op, first = xm_place[b]
+                cols = slice(first + h * P, first + (h + 1) * P)
                 nc.tensor.matmul_mx(
-                    out=dw[t][:], lhsT=xm_op[h][1][:, cols].bitcast(E4M3), lhsT_scale=xm_op[h][2][:, cols],
+                    out=dw[b][:], lhsT=xm_ops[op][1][:, cols].bitcast(E4M3), lhsT_scale=xm_ops[op][2][:, cols],
                     rhs=g_op[h][1][:].bitcast(E5M2), rhs_scale=g_op[h][2][:],
-                    start=(h == order[0]), stop=(h == order[-1]),
+                    start=(h == 0), stop=(h == HALVES - 1),
                 )
 
-        m_cols = keep.tile([P, PACK, N], F32, name="m_cols")
-        new_m = keep.tile([P, PACK, N], F32, name="new_m")
-        m_term = keep.tile([P, PACK, N], F32, name="m_term")
-        dw_sb = keep.tile([P, PACK, N], F32, name="dw_sb", tag="y0")
-        dw_term = keep.tile([P, PACK, N], F32, name="dw_term", tag="y1")
+        m_cols = keep.tile([P, BLOCKS, N], F32, name="m_cols")
+        new_m = keep.tile([P, BLOCKS, N], F32, name="new_m")
+        m_term = keep.tile([P, BLOCKS, N], F32, name="m_term")
+        dw_sb = keep.tile([P, BLOCKS, N], F32, name="dw_sb", tag="y0")
+        dw_term = keep.tile([P, BLOCKS, N], F32, name="dw_term", tag="y1")
+        m_dst = [keep.tile([P, T], F32, name="m_dst%d" % b, tag="table%d" % b) for b in range(BLOCKS)]
+        for b in range(2, BLOCKS):
+            w_dst.append(keep.tile([P, T], F32, name="w_dst%d" % b, tag="rest%d" % (b - 2)))
 
-        w_dst.append(keep.tile([P, T], F32, name="w_dst3", tag="shared3"))
-        m_dst = []
-        for t, tag in enumerate(("shared0", "shared1", "m_dst2", "shared2")):
-            m_dst.append(keep.tile([P, T], F32, name="m_dst%d" % t, tag=tag))
-        for t in range(1, PACK):
-            nc.sync.dma_start(out=m_src[t][:], in_=plane(mT, t))
-
-        def store(dst, out, t):
-            if out is out_1 and t == PACK - 1:
-                nc.sync.dma_start(out=plane(out, t)[:, : T // 2], in_=dst[:, : T // 2])
-                nc.scalar.dma_start(out=plane(out, t)[:, T // 2 :], in_=dst[:, T // 2 :])
+        def store(dst, out, b):
+            if out is out_1 and b == BLOCKS - 1:
+                nc.sync.dma_start(out=block(out, b)[:, : T // 2], in_=dst[:, : T // 2])
+                nc.scalar.dma_start(out=block(out, b)[:, T // 2 :], in_=dst[:, T // 2 :])
             else:
-                nc.sync.dma_start(out=plane(out, t), in_=dst[:])
+                nc.sync.dma_start(out=block(out, b), in_=dst[:])
 
-        def update_w(t):
-            nc.scalar.activation(dw_term[:, t, :], dw[t][:], COPY, scale=-LR * (1.0 + BETA))
-            nc.gpsimd.tensor_tensor(w_cols[:, t, :], w_cols[:, t, :], dw_term[:, t, :], ADD)
-            nc.scalar.activation(m_term[:, t, :], m_cols[:, t, :], COPY, scale=-LR * BETA * BETA)
-            nc.gpsimd.tensor_tensor(w_cols[:, t, :], w_cols[:, t, :], m_term[:, t, :], ADD)
+        def update_w(b):
+            nc.scalar.activation(dw_term[:, b, :], dw[b][:], COPY, scale=-LR * (1.0 + BETA))
+            nc.gpsimd.tensor_tensor(w_cols[:, b, :], w_cols[:, b, :], dw_term[:, b, :], ADD)
+            nc.scalar.activation(m_term[:, b, :], m_cols[:, b, :], COPY, scale=-LR * BETA * BETA)
+            nc.gpsimd.tensor_tensor(w_cols[:, b, :], w_cols[:, b, :], m_term[:, b, :], ADD)
 
-        def update_m(t, src, scale):
-            nc.scalar.activation(new_m[:, t, :], src[:, t, :], COPY, scale=scale)
-            nc.scalar.copy(dw_sb[:, t, :], dw[t][:])
-            nc.gpsimd.tensor_tensor(new_m[:, t, :], new_m[:, t, :], dw_sb[:, t, :], ADD)
+        def update_m(b, src, scale):
+            nc.scalar.activation(new_m[:, b, :], src[:, b, :], COPY, scale=scale)
+            nc.scalar.copy(dw_sb[:, b, :], dw[b][:])
+            nc.gpsimd.tensor_tensor(new_m[:, b, :], new_m[:, b, :], dw_sb[:, b, :], ADD)
 
-        quantise(xm_op[0], E4M3)
-        quantise(xm_op[1], E4M3)
+        def gather_m(b):
+            nc.vector.tensor_copy(m_cols[:, b, :], m_src[b][:].indirect(offsets[:]))
+
+        def scatter(dst, src, out, b):
+            nc.vector.tensor_copy(dst[b][:].indirect(offsets[:]), src)
+            store(dst[b], out, b)
+
         gradient(0)
         nc.vector.tensor_scalar(
             m_term[:, 0, :], m_src[0][:].indirect(offsets[:]), -LR * BETA * BETA, 0.0, MULT, ADD)
         nc.vector.scalar_tensor_tensor(
-            out=dw_term[:, 0, :], in0=dw[0][:], scalar=-LR * (1.0 + BETA), in1=m_term[:, 0, :], op0=MULT, op1=ADD)
-        nc.vector.tensor_tensor(w_dst[0][:].indirect(offsets[:]), w_cols[:, 0, :], dw_term[:, 0, :], ADD)
+            out=dw_term[:, 0, :], in0=dw[0][:], scalar=-LR * (1.0 + BETA), in1=w_cols[:, 0, :], op0=MULT, op1=ADD)
+        nc.vector.tensor_tensor(w_dst[0][:].indirect(offsets[:]), m_term[:, 0, :], dw_term[:, 0, :], ADD)
         store(w_dst[0], out_0, 0)
-        for t in range(1, PACK):
-            gradient(t)
-        update_m(0, m_term, -1.0 / (LR * BETA))
-        for t in range(PACK):
-            fill(m_dst[t], m_src[t])
-            if t + 1 < PACK:
-                nc.vector.tensor_copy(m_cols[:, t + 1, :], m_src[t + 1][:].indirect(offsets[:]))
-                update_w(t + 1)
-            nc.vector.tensor_copy(m_dst[t][:].indirect(offsets[:]), new_m[:, t, :])
-            store(m_dst[t], out_1, t)
-            if t + 1 < PACK:
-                if t + 1 >= 3:
-                    fill(w_dst[t + 1], w_src[t + 1])
-                update_m(t + 1, m_cols, BETA)
-                nc.vector.tensor_copy(w_dst[t + 1][:].indirect(offsets[:]), w_cols[:, t + 1, :])
-                store(w_dst[t + 1], out_0, t + 1)
+        fill(m_dst[0], m_src[0])
+        for b in range(1, BLOCKS):
+            weave_xm(b)
+        quantise(xm_ops[1], E4M3)
+        quantise(xm_ops[2], E4M3)
+        for b in range(1, BLOCKS):
+            gradient(b)
+        first_m = keep.tile([P, N], F32, name="first_m", tag="xm12_grouped", align_bytes=64)
+        nc.scalar.activation(new_m[:, 0, :], m_term[:, 0, :], COPY, scale=-1.0 / (LR * BETA))
+        nc.scalar.copy(dw_sb[:, 0, :], dw[0][:])
+        nc.gpsimd.tensor_tensor(first_m[:], new_m[:, 0, :], dw_sb[:, 0, :], ADD)
+        gather_m(1)
+        update_w(1)
+        scatter(m_dst, first_m[:], out_1, 0)
+        for b in range(1, BLOCKS):
+            if b >= 2:
+                fill(w_dst[b], w_src[b])
+            update_m(b, m_cols, BETA)
+            fill(m_dst[b], m_src[b])
+            if b + 1 < BLOCKS:
+                gather_m(b + 1)
+            scatter(w_dst, w_cols[:, b, :], out_0, b)
+            if b + 1 < BLOCKS:
+                update_w(b + 1)
+            scatter(m_dst, new_m[:, b, :], out_1, b)

@@ -28,6 +28,7 @@ CHUNKS = N // P
 X_ON_SCALAR = (0, 64)
 Y_ON_SCALAR = (4, 2)
 G_ON_SCALAR = (128, 0)
+EARLY_FILL = 1536
 
 
 def tile_attend_gsq_nag_kernel(tc, xT, wT, y, wt, xm, mT, offs, out_0, out_1):
@@ -43,10 +44,10 @@ def tile_attend_gsq_nag_kernel(tc, xT, wT, y, wt, xm, mT, offs, out_0, out_1):
         def rows(src):
             return src.rearrange("(p j) c -> p j c", j=PACK)
 
-        def operand(name, width=K, codes_tag=None):
+        def operand(name, width=K, codes_tag=None, scales_tag=None):
             grouped = keep.tile([P, width * PACK], BF16, name=name + "_grouped", align_bytes=64)
             codes = keep.tile([P, width], U32, name=name + "_codes", tag=codes_tag or name + "_codes", align_bytes=64)
-            scales = keep.tile([P, width], U8, name=name + "_scales", align_bytes=64)
+            scales = keep.tile([P, width], U8, name=name + "_scales", tag=scales_tag or name + "_scales", align_bytes=64)
             return grouped, codes, scales
 
         def quantise(op, fmt):
@@ -69,14 +70,17 @@ def tile_attend_gsq_nag_kernel(tc, xT, wT, y, wt, xm, mT, offs, out_0, out_1):
             src = planes.rearrange("p t (c i) -> p c t i", i=4)
             return dst, src
 
+        slot_halves = (slice(0, N // 2), slice(N // 2, N))
+
         offsets = lists.tile([P, N // 16], U16, name="offsets")
         x_raw = [keep.tile([P, PACK, K], F32, name="x_raw%d" % h, tag="shared%d" % h) for h in range(HALVES)]
         y_sb = [keep.tile([P, PACK, N], F32, name="y_sb%d" % h, tag="y%d" % h) for h in range(HALVES)]
         xm_first = [keep.tile([P, PACK, P], F32, name="xm_first%d" % h) for h in range(HALVES)]
-        xm_rest = [keep.tile([P, PACK, D - P], F32, name="xm_rest%d" % h, tag="rest%d" % h) for h in range(HALVES)]
+        xm_mid = [keep.tile([P, PACK, 2 * P], F32, name="xm_mid%d" % h) for h in range(HALVES)]
+        xm_last = [keep.tile([P, PACK, P], F32, name="xm_last%d" % h, tag="rest%d" % h) for h in range(HALVES)]
         w_src = [keep.tile([P, T], F32, name="w_src%d" % b, tag="table%d" % b) for b in range(BLOCKS)]
         m_src = [keep.tile([P, T], F32, name="m_src%d" % b) for b in range(BLOCKS)]
-        wt_sb = [keep.tile([P, PACK], F32, name="wt_sb%d" % h, align_bytes=64) for h in range(HALVES)]
+        wt_sb = [keep.tile([P, PACK], F32, name="wt_sb%d" % h, tag="wt%d" % h, align_bytes=64) for h in range(HALVES)]
         ident = keep.tile([P, P], F32, name="ident")
         make_identity(nc, ident[:])
 
@@ -95,7 +99,9 @@ def tile_attend_gsq_nag_kernel(tc, xT, wT, y, wt, xm, mT, offs, out_0, out_1):
             nc.sync.dma_start(out=xm_first[h][:], in_=rows(xm[0, h * K : (h + 1) * K, :P]))
         nc.sync.dma_start(out=m_src[0][:], in_=block(mT, 0))
         for h in range(HALVES):
-            nc.sync.dma_start(out=xm_rest[h][:], in_=rows(xm[0, h * K : (h + 1) * K, P:]))
+            nc.sync.dma_start(out=xm_mid[h][:], in_=rows(xm[0, h * K : (h + 1) * K, P : 3 * P]))
+        for h in range(HALVES):
+            nc.sync.dma_start(out=xm_last[h][:], in_=rows(xm[0, h * K : (h + 1) * K, 3 * P :]))
         for b in range(1, BLOCKS):
             nc.sync.dma_start(out=m_src[b][:], in_=block(mT, b))
 
@@ -103,13 +109,13 @@ def tile_attend_gsq_nag_kernel(tc, xT, wT, y, wt, xm, mT, offs, out_0, out_1):
         w_dst = [keep.tile([P, T], F32, name="w_dst%d" % b) for b in range(2)]
         w_turned = [keep.tile([P, 2, 2, P, 2], BF16, name="w_turned%d" % i, align_bytes=64) for i in range(CHUNKS // 2)]
 
-        def fill(dst, src):
-            for half in (slice(0, T // 2), slice(T // 2, T)):
-                nc.scalar.activation(dst[:, half], src[:, half], COPY)
+        def fill(dst, src, parts=(slice(0, T // 2), slice(T // 2, T))):
+            for part in parts:
+                nc.scalar.activation(dst[:, part], src[:, part], COPY)
 
         x_op = [operand("x%d" % h) for h in range(HALVES)]
         w_op = operand("w", codes_tag="x0_grouped")
-        g_op = [operand("g%d" % h) for h in range(HALVES)]
+        g_op = [operand("g0", scales_tag="wt1"), operand("g1")]
         xm_ops = [operand("xm0", HALVES * P), operand("xm12", 2 * HALVES * P), operand("xm3", HALVES * P)]
         xm_place = [(0, 0), (1, 0), (1, HALVES * P), (2, 0)]
 
@@ -168,14 +174,16 @@ def tile_attend_gsq_nag_kernel(tc, xT, wT, y, wt, xm, mT, offs, out_0, out_1):
                     out=a[:], lhsT=codes[:, cols].bitcast(E4M3), lhsT_scale=scales[:, cols],
                     rhs=w_op[1][:].bitcast(E4M3), rhs_scale=w_op[2][:], start=True, stop=True,
                 )
-                nc.vector.scalar_tensor_tensor(
-                    out=y_sb[h][:, t, :], in0=a[:], scalar=wt_sb[h][:, t : t + 1], in1=y_sb[h][:, t, :],
-                    op0=MULT, op1=SUB,
-                )
+                last = h == HALVES - 1 and t == PACK - 1
+                for part in (slot_halves if last else (slice(0, N),)):
+                    nc.vector.scalar_tensor_tensor(
+                        out=y_sb[h][:, t, part], in0=a[:, part], scalar=wt_sb[h][:, t : t + 1], in1=y_sb[h][:, t, part],
+                        op0=MULT, op1=SUB,
+                    )
 
         def weave_xm(b):
             for h in range(HALVES):
-                raw = xm_first[h][:] if b == 0 else xm_rest[h][:, :, (b - 1) * P : b * P]
+                raw = (xm_first[h][:], xm_mid[h][:, :, :P], xm_mid[h][:, :, P:], xm_last[h][:])[b]
                 op, first = xm_place[b]
                 lo = PACK * (first + h * P)
                 dst, src = plain_views(xm_ops[op][0][:, lo : lo + K], raw)
@@ -187,7 +195,8 @@ def tile_attend_gsq_nag_kernel(tc, xT, wT, y, wt, xm, mT, offs, out_0, out_1):
         weave(*plain_views(g_op[0][0][:], y_sb[0][:]), on_scalar=G_ON_SCALAR[0])
         weave_xm(0)
         residual(1)
-        weave(*plain_views(g_op[1][0][:], y_sb[1][:]), on_scalar=G_ON_SCALAR[1])
+        for part in slot_halves:
+            weave(*plain_views(g_op[1][0][:, PACK * part.start : PACK * part.stop], y_sb[1][:, :, part]), on_scalar=0)
         quantise(g_op[0], E5M2)
         quantise(xm_ops[0], E4M3)
         quantise(g_op[1], E5M2)
@@ -209,12 +218,13 @@ def tile_attend_gsq_nag_kernel(tc, xT, wT, y, wt, xm, mT, offs, out_0, out_1):
         m_term = keep.tile([P, BLOCKS, N], F32, name="m_term")
         dw_sb = keep.tile([P, BLOCKS, N], F32, name="dw_sb", tag="y0")
         dw_term = keep.tile([P, BLOCKS, N], F32, name="dw_term", tag="y1")
-        m_dst = [keep.tile([P, T], F32, name="m_dst%d" % b, tag="table%d" % b) for b in range(BLOCKS)]
+        m_dst = [keep.tile([P, T], F32, name="m_dst%d" % b, tag=tag)
+                 for b, tag in enumerate(("table0", "table1", "shared0", "shared1"))]
         for b in range(2, BLOCKS):
             w_dst.append(keep.tile([P, T], F32, name="w_dst%d" % b, tag="rest%d" % (b - 2)))
 
         def store(dst, out, b):
-            if out is out_1 and b == BLOCKS - 1:
+            if out is out_0 and b == BLOCKS - 1:
                 nc.sync.dma_start(out=block(out, b)[:, : T // 2], in_=dst[:, : T // 2])
                 nc.scalar.dma_start(out=block(out, b)[:, T // 2 :], in_=dst[:, T // 2 :])
             else:
@@ -223,16 +233,15 @@ def tile_attend_gsq_nag_kernel(tc, xT, wT, y, wt, xm, mT, offs, out_0, out_1):
         def update_w(b):
             nc.scalar.activation(dw_term[:, b, :], dw[b][:], COPY, scale=-LR * (1.0 + BETA))
             nc.gpsimd.tensor_tensor(w_cols[:, b, :], w_cols[:, b, :], dw_term[:, b, :], ADD)
-            nc.scalar.activation(m_term[:, b, :], m_cols[:, b, :], COPY, scale=-LR * BETA * BETA)
+            nc.scalar.activation(m_term[:, b, :], m_cols[:, b, :], COPY, scale=-LR * BETA)
             nc.gpsimd.tensor_tensor(w_cols[:, b, :], w_cols[:, b, :], m_term[:, b, :], ADD)
 
-        def update_m(b, src, scale):
-            nc.scalar.activation(new_m[:, b, :], src[:, b, :], COPY, scale=scale)
+        def update_m(b):
             nc.scalar.copy(dw_sb[:, b, :], dw[b][:])
-            nc.gpsimd.tensor_tensor(new_m[:, b, :], new_m[:, b, :], dw_sb[:, b, :], ADD)
+            nc.gpsimd.tensor_tensor(new_m[:, b, :], m_cols[:, b, :], dw_sb[:, b, :], ADD)
 
         def gather_m(b):
-            nc.vector.tensor_copy(m_cols[:, b, :], m_src[b][:].indirect(offsets[:]))
+            nc.vector.tensor_scalar(m_cols[:, b, :], m_src[b][:].indirect(offsets[:]), BETA, 0.0, MULT, ADD)
 
         def scatter(dst, src, out, b):
             nc.vector.tensor_copy(dst[b][:].indirect(offsets[:]), src)
@@ -245,7 +254,7 @@ def tile_attend_gsq_nag_kernel(tc, xT, wT, y, wt, xm, mT, offs, out_0, out_1):
             out=dw_term[:, 0, :], in0=dw[0][:], scalar=-LR * (1.0 + BETA), in1=w_cols[:, 0, :], op0=MULT, op1=ADD)
         nc.vector.tensor_tensor(w_dst[0][:].indirect(offsets[:]), m_term[:, 0, :], dw_term[:, 0, :], ADD)
         store(w_dst[0], out_0, 0)
-        fill(m_dst[0], m_src[0])
+        fill(m_dst[0], m_src[0], (slice(0, EARLY_FILL),))
         for b in range(1, BLOCKS):
             weave_xm(b)
         quantise(xm_ops[1], E4M3)
@@ -256,17 +265,16 @@ def tile_attend_gsq_nag_kernel(tc, xT, wT, y, wt, xm, mT, offs, out_0, out_1):
         nc.scalar.activation(new_m[:, 0, :], m_term[:, 0, :], COPY, scale=-1.0 / (LR * BETA))
         nc.scalar.copy(dw_sb[:, 0, :], dw[0][:])
         nc.gpsimd.tensor_tensor(first_m[:], new_m[:, 0, :], dw_sb[:, 0, :], ADD)
+        fill(m_dst[0], m_src[0], (slice(EARLY_FILL, T),))
         gather_m(1)
-        update_w(1)
         scatter(m_dst, first_m[:], out_1, 0)
         for b in range(1, BLOCKS):
-            if b >= 2:
-                fill(w_dst[b], w_src[b])
-            update_m(b, m_cols, BETA)
+            update_m(b)
             fill(m_dst[b], m_src[b])
             if b + 1 < BLOCKS:
                 gather_m(b + 1)
-            scatter(w_dst, w_cols[:, b, :], out_0, b)
-            if b + 1 < BLOCKS:
-                update_w(b + 1)
             scatter(m_dst, new_m[:, b, :], out_1, b)
+            update_w(b)
+            if b >= 2:
+                fill(w_dst[b], w_src[b])
+            scatter(w_dst, w_cols[:, b, :], out_0, b)

@@ -25,10 +25,10 @@ K = P * PACK
 HALVES = R // K
 BLOCKS = D // P
 CHUNKS = N // P
-X_ON_SCALAR = (0, 64)
+X_ON_SCALAR = (0, 56)
 Y_ON_SCALAR = (4, 2)
 G_ON_SCALAR = (128, 0)
-EARLY_FILL = 1536
+COPIED = (1536, 1536, 1536, 2048)
 
 
 def tile_attend_gsq_nag_kernel(tc, xT, wT, y, wt, xm, mT, offs, out_0, out_1):
@@ -50,9 +50,12 @@ def tile_attend_gsq_nag_kernel(tc, xT, wT, y, wt, xm, mT, offs, out_0, out_1):
             scales = keep.tile([P, width], U8, name=name + "_scales", tag=scales_tag or name + "_scales", align_bytes=64)
             return grouped, codes, scales
 
-        def quantise(op, fmt):
+        def quantise(op, fmt, part=None):
             grouped, codes, scales = op
-            nc.vector.quantize_mx(out=codes[:].bitcast(fmt), scales=scales[:], in_=grouped[:])
+            part = part or slice(0, codes.shape[1])
+            nc.vector.quantize_mx(
+                out=codes[:, part].bitcast(fmt), scales=scales[:, part],
+                in_=grouped[:, PACK * part.start : PACK * part.stop])
 
         def weave(dst, src, on_scalar):
             if on_scalar > 0:
@@ -102,8 +105,7 @@ def tile_attend_gsq_nag_kernel(tc, xT, wT, y, wt, xm, mT, offs, out_0, out_1):
             nc.sync.dma_start(out=xm_mid[h][:], in_=rows(xm[0, h * K : (h + 1) * K, P : 3 * P]))
         for h in range(HALVES):
             nc.sync.dma_start(out=xm_last[h][:], in_=rows(xm[0, h * K : (h + 1) * K, 3 * P :]))
-        for b in range(1, BLOCKS):
-            nc.sync.dma_start(out=m_src[b][:], in_=block(mT, b))
+
 
         w_cols = keep.tile([P, BLOCKS, N], F32, name="w_cols")
         w_dst = [keep.tile([P, T], F32, name="w_dst%d" % b) for b in range(2)]
@@ -198,8 +200,9 @@ def tile_attend_gsq_nag_kernel(tc, xT, wT, y, wt, xm, mT, offs, out_0, out_1):
         for part in slot_halves:
             weave(*plain_views(g_op[1][0][:, PACK * part.start : PACK * part.stop], y_sb[1][:, :, part]), on_scalar=0)
         quantise(g_op[0], E5M2)
-        quantise(xm_ops[0], E4M3)
+        quantise(xm_ops[0], E4M3, slice(0, P))
         quantise(g_op[1], E5M2)
+        quantise(xm_ops[0], E4M3, slice(P, 2 * P))
 
         dw = [psum.tile([P, N], F32, name="dw%d" % b, tag="bank%d" % b) for b in range(BLOCKS)]
 
@@ -220,6 +223,9 @@ def tile_attend_gsq_nag_kernel(tc, xT, wT, y, wt, xm, mT, offs, out_0, out_1):
         dw_term = keep.tile([P, BLOCKS, N], F32, name="dw_term", tag="y1")
         m_dst = [keep.tile([P, T], F32, name="m_dst%d" % b, tag=tag)
                  for b, tag in enumerate(("table0", "table1", "shared0", "shared1"))]
+        for b in range(1, BLOCKS):
+            nc.sync.dma_start(out=m_src[b][:], in_=block(mT, b))
+            nc.sync.dma_start(out=m_dst[b - 1][:, COPIED[b - 1]:], in_=block(mT, b - 1)[:, COPIED[b - 1]:])
         for b in range(2, BLOCKS):
             w_dst.append(keep.tile([P, T], F32, name="w_dst%d" % b, tag="rest%d" % (b - 2)))
 
@@ -231,10 +237,10 @@ def tile_attend_gsq_nag_kernel(tc, xT, wT, y, wt, xm, mT, offs, out_0, out_1):
                 nc.sync.dma_start(out=block(out, b), in_=dst[:])
 
         def update_w(b):
-            nc.scalar.activation(dw_term[:, b, :], dw[b][:], COPY, scale=-LR * (1.0 + BETA))
-            nc.gpsimd.tensor_tensor(w_cols[:, b, :], w_cols[:, b, :], dw_term[:, b, :], ADD)
             nc.scalar.activation(m_term[:, b, :], m_cols[:, b, :], COPY, scale=-LR * BETA)
             nc.gpsimd.tensor_tensor(w_cols[:, b, :], w_cols[:, b, :], m_term[:, b, :], ADD)
+            nc.scalar.activation(dw_term[:, b, :], dw[b][:], COPY, scale=-LR * (1.0 + BETA))
+            nc.gpsimd.tensor_tensor(w_cols[:, b, :], w_cols[:, b, :], dw_term[:, b, :], ADD)
 
         def update_m(b):
             nc.scalar.copy(dw_sb[:, b, :], dw[b][:])
@@ -252,25 +258,22 @@ def tile_attend_gsq_nag_kernel(tc, xT, wT, y, wt, xm, mT, offs, out_0, out_1):
             m_term[:, 0, :], m_src[0][:].indirect(offsets[:]), -LR * BETA * BETA, 0.0, MULT, ADD)
         nc.vector.scalar_tensor_tensor(
             out=dw_term[:, 0, :], in0=dw[0][:], scalar=-LR * (1.0 + BETA), in1=w_cols[:, 0, :], op0=MULT, op1=ADD)
+        nc.vector.scalar_tensor_tensor(
+            out=new_m[:, 0, :], in0=m_term[:, 0, :], scalar=-1.0 / (LR * BETA), in1=dw[0][:], op0=MULT, op1=ADD)
         nc.vector.tensor_tensor(w_dst[0][:].indirect(offsets[:]), m_term[:, 0, :], dw_term[:, 0, :], ADD)
         store(w_dst[0], out_0, 0)
-        fill(m_dst[0], m_src[0], (slice(0, EARLY_FILL),))
+        fill(m_dst[0], m_src[0], (slice(0, COPIED[0]),))
         for b in range(1, BLOCKS):
             weave_xm(b)
         quantise(xm_ops[1], E4M3)
         quantise(xm_ops[2], E4M3)
         for b in range(1, BLOCKS):
             gradient(b)
-        first_m = keep.tile([P, N], F32, name="first_m", tag="xm12_grouped", align_bytes=64)
-        nc.scalar.activation(new_m[:, 0, :], m_term[:, 0, :], COPY, scale=-1.0 / (LR * BETA))
-        nc.scalar.copy(dw_sb[:, 0, :], dw[0][:])
-        nc.gpsimd.tensor_tensor(first_m[:], new_m[:, 0, :], dw_sb[:, 0, :], ADD)
-        fill(m_dst[0], m_src[0], (slice(EARLY_FILL, T),))
         gather_m(1)
-        scatter(m_dst, first_m[:], out_1, 0)
+        scatter(m_dst, new_m[:, 0, :], out_1, 0)
         for b in range(1, BLOCKS):
             update_m(b)
-            fill(m_dst[b], m_src[b])
+            fill(m_dst[b], m_src[b], (slice(0, T // 2), slice(T // 2, COPIED[b])))
             if b + 1 < BLOCKS:
                 gather_m(b + 1)
             scatter(m_dst, new_m[:, b, :], out_1, b)

@@ -25,9 +25,10 @@ K = P * PACK
 HALVES = R // K
 BLOCKS = D // P
 CHUNKS = N // P
-X_ON_SCALAR = (0, 56)
+X_ON_SCALAR = (32, 64)
 Y_ON_SCALAR = (4, 2)
 G_ON_SCALAR = (128, 0)
+LAST_XM_AFTER = 2
 COPIED = (1536, 1536, 1536, 2048)
 
 
@@ -76,12 +77,12 @@ def tile_attend_gsq_nag_kernel(tc, xT, wT, y, wt, xm, mT, offs, out_0, out_1):
         slot_halves = (slice(0, N // 2), slice(N // 2, N))
 
         offsets = lists.tile([P, N // 16], U16, name="offsets")
-        x_raw = [keep.tile([P, PACK, K], F32, name="x_raw%d" % h, tag="shared%d" % h) for h in range(HALVES)]
+        x_raw = [keep.tile([P, PACK, K], F32, name="x_raw%d" % h, tag="shared%d" % h, align_bytes=64) for h in range(HALVES)]
         y_sb = [keep.tile([P, PACK, N], F32, name="y_sb%d" % h, tag="y%d" % h) for h in range(HALVES)]
         xm_first = [keep.tile([P, PACK, P], F32, name="xm_first%d" % h) for h in range(HALVES)]
         xm_mid = [keep.tile([P, PACK, 2 * P], F32, name="xm_mid%d" % h) for h in range(HALVES)]
         xm_last = [keep.tile([P, PACK, P], F32, name="xm_last%d" % h, tag="rest%d" % h) for h in range(HALVES)]
-        w_src = [keep.tile([P, T], F32, name="w_src%d" % b, tag="table%d" % b) for b in range(BLOCKS)]
+        w_src = [keep.tile([P, T], F32, name="w_src%d" % b, tag="table%d" % b, align_bytes=64) for b in range(BLOCKS)]
         m_src = [keep.tile([P, T], F32, name="m_src%d" % b) for b in range(BLOCKS)]
         wt_sb = [keep.tile([P, PACK], F32, name="wt_sb%d" % h, tag="wt%d" % h, align_bytes=64) for h in range(HALVES)]
         ident = keep.tile([P, P], F32, name="ident")
@@ -103,8 +104,6 @@ def tile_attend_gsq_nag_kernel(tc, xT, wT, y, wt, xm, mT, offs, out_0, out_1):
         nc.sync.dma_start(out=m_src[0][:], in_=block(mT, 0))
         for h in range(HALVES):
             nc.sync.dma_start(out=xm_mid[h][:], in_=rows(xm[0, h * K : (h + 1) * K, P : 3 * P]))
-        for h in range(HALVES):
-            nc.sync.dma_start(out=xm_last[h][:], in_=rows(xm[0, h * K : (h + 1) * K, 3 * P :]))
 
 
         w_cols = keep.tile([P, BLOCKS, N], F32, name="w_cols")
@@ -116,9 +115,12 @@ def tile_attend_gsq_nag_kernel(tc, xT, wT, y, wt, xm, mT, offs, out_0, out_1):
                 nc.scalar.activation(dst[:, part], src[:, part], COPY)
 
         x_op = [operand("x%d" % h) for h in range(HALVES)]
-        w_op = operand("w", codes_tag="x0_grouped")
+        w_whole = keep.tile([P, K * PACK], BF16, name="w_grouped", tag="shared0", align_bytes=64)
+        w_grouped = [w_whole[:, PACK * part.start : PACK * part.stop] for part in slot_halves]
+        w_codes = keep.tile([P, N], U32, name="w_codes", align_bytes=64)
+        w_scales = keep.tile([P, N], U8, name="w_scales", align_bytes=64)
         g_op = [operand("g0", scales_tag="wt1"), operand("g1")]
-        xm_ops = [operand("xm0", HALVES * P), operand("xm12", 2 * HALVES * P), operand("xm3", HALVES * P)]
+        xm_ops = [operand("xm0", HALVES * P), operand("xm12", 2 * HALVES * P), None]
         xm_place = [(0, 0), (1, 0), (1, HALVES * P), (2, 0)]
 
         def turn(b, chunks):
@@ -132,8 +134,6 @@ def tile_attend_gsq_nag_kernel(tc, xT, wT, y, wt, xm, mT, offs, out_0, out_1):
                     out=w_turned[chunks[i] // 2][:, :, :, 32 * b : 32 * (b + 1), :].rearrange("s c u q e -> s c q u e"),
                     in_=turned[:, i : i + 2, :].rearrange("s c (q u e) -> s c q u e", u=2, e=2))
 
-        w_words = w_op[0][:].bitcast(F32)
-
         def turn_back(pair):
             back = psum.tile([P, 2, 2, P], F32, name="back%d" % pair, tag="bank%d" % (5 + pair))
             words = w_turned[pair][:].rearrange("s c u q e -> s (c u q e)").bitcast(F32)
@@ -141,8 +141,15 @@ def tile_attend_gsq_nag_kernel(tc, xT, wT, y, wt, xm, mT, offs, out_0, out_1):
                 for u in range(2):
                     k = 2 * c + u
                     nc.tensor.transpose(back[:, c, u, :], words[:, k * P : (k + 1) * P], ident[:])
-            dst = w_words[:, pair * K : (pair + 1) * K].rearrange("p (c s u) -> p c s u", c=2, u=2)
-            nc.scalar.copy(out=dst, in_=back[:].rearrange("p c u s -> p c s u"))
+            return back
+
+        def copy_back(pair, back):
+            dst = w_grouped[pair].bitcast(F32).rearrange("p (c s u) -> p c s u", c=2, u=2)
+            src = back[:].rearrange("p c u s -> p c s u")
+            if pair == 0:
+                nc.scalar.copy(out=dst, in_=src)
+            else:
+                nc.vector.tensor_copy(out=dst, in_=src)
 
         fill(w_dst[0], w_src[0])
         turn(0, (0, 1, 2, 3))
@@ -151,11 +158,13 @@ def tile_attend_gsq_nag_kernel(tc, xT, wT, y, wt, xm, mT, offs, out_0, out_1):
         turn(2, (0, 1, 2, 3))
         turn(3, (0, 1))
         turn(3, (2, 3))
-        turn_back(0)
-        turn_back(1)
+        backs = [turn_back(pair) for pair in range(2)]
         weave(*dealt_views(x_op[0], x_raw[0]), on_scalar=X_ON_SCALAR[0])
         quantise(x_op[0], E4M3)
-        quantise(w_op, E4M3)
+        for pair in range(2):
+            copy_back(pair, backs[pair])
+        for pair, part in enumerate(slot_halves):
+            nc.vector.quantize_mx(out=w_codes[:, part].bitcast(E4M3), scales=w_scales[:, part], in_=w_grouped[pair])
         weave(*dealt_views(x_op[1], x_raw[1]), on_scalar=X_ON_SCALAR[1])
         quantise(x_op[1], E4M3)
 
@@ -174,7 +183,7 @@ def tile_attend_gsq_nag_kernel(tc, xT, wT, y, wt, xm, mT, offs, out_0, out_1):
                 a = psum.tile([P, N], F32, name="a%d%d" % (h, t), tag="bank%d" % (PACK * h + t))
                 nc.tensor.matmul_mx(
                     out=a[:], lhsT=codes[:, cols].bitcast(E4M3), lhsT_scale=scales[:, cols],
-                    rhs=w_op[1][:].bitcast(E4M3), rhs_scale=w_op[2][:], start=True, stop=True,
+                    rhs=w_codes[:].bitcast(E4M3), rhs_scale=w_scales[:], start=True, stop=True,
                 )
                 last = h == HALVES - 1 and t == PACK - 1
                 for part in (slot_halves if last else (slice(0, N),)):
@@ -217,15 +226,18 @@ def tile_attend_gsq_nag_kernel(tc, xT, wT, y, wt, xm, mT, offs, out_0, out_1):
                 )
 
         m_cols = keep.tile([P, BLOCKS, N], F32, name="m_cols")
-        new_m = keep.tile([P, BLOCKS, N], F32, name="new_m")
+        new_m = [keep.tile([P, N], F32, name="new_m%d" % b, align_bytes=64) for b in range(BLOCKS)]
         m_term = keep.tile([P, BLOCKS, N], F32, name="m_term")
         dw_sb = keep.tile([P, BLOCKS, N], F32, name="dw_sb", tag="y0")
         dw_term = keep.tile([P, BLOCKS, N], F32, name="dw_term", tag="y1")
-        m_dst = [keep.tile([P, T], F32, name="m_dst%d" % b, tag=tag)
+        m_dst = [keep.tile([P, T], F32, name="m_dst%d" % b, tag=tag, align_bytes=64)
                  for b, tag in enumerate(("table0", "table1", "shared0", "shared1"))]
         for b in range(1, BLOCKS):
             nc.sync.dma_start(out=m_src[b][:], in_=block(mT, b))
             nc.sync.dma_start(out=m_dst[b - 1][:, COPIED[b - 1]:], in_=block(mT, b - 1)[:, COPIED[b - 1]:])
+            if b == LAST_XM_AFTER:
+                for h in range(HALVES):
+                    nc.sync.dma_start(out=xm_last[h][:], in_=rows(xm[0, h * K : (h + 1) * K, 3 * P :]))
         for b in range(2, BLOCKS):
             w_dst.append(keep.tile([P, T], F32, name="w_dst%d" % b, tag="rest%d" % (b - 2)))
 
@@ -236,15 +248,15 @@ def tile_attend_gsq_nag_kernel(tc, xT, wT, y, wt, xm, mT, offs, out_0, out_1):
             else:
                 nc.sync.dma_start(out=block(out, b), in_=dst[:])
 
-        def update_w(b):
+        def update_w(b, new_w):
             nc.scalar.activation(m_term[:, b, :], m_cols[:, b, :], COPY, scale=-LR * BETA)
-            nc.gpsimd.tensor_tensor(w_cols[:, b, :], w_cols[:, b, :], m_term[:, b, :], ADD)
+            nc.gpsimd.tensor_tensor(new_w, w_cols[:, b, :], m_term[:, b, :], ADD)
             nc.scalar.activation(dw_term[:, b, :], dw[b][:], COPY, scale=-LR * (1.0 + BETA))
-            nc.gpsimd.tensor_tensor(w_cols[:, b, :], w_cols[:, b, :], dw_term[:, b, :], ADD)
+            nc.gpsimd.tensor_tensor(new_w, new_w, dw_term[:, b, :], ADD)
 
         def update_m(b):
             nc.scalar.copy(dw_sb[:, b, :], dw[b][:])
-            nc.gpsimd.tensor_tensor(new_m[:, b, :], m_cols[:, b, :], dw_sb[:, b, :], ADD)
+            nc.gpsimd.tensor_tensor(new_m[b][:], m_cols[:, b, :], dw_sb[:, b, :], ADD)
 
         def gather_m(b):
             nc.vector.tensor_scalar(m_cols[:, b, :], m_src[b][:].indirect(offsets[:]), BETA, 0.0, MULT, ADD)
@@ -259,25 +271,32 @@ def tile_attend_gsq_nag_kernel(tc, xT, wT, y, wt, xm, mT, offs, out_0, out_1):
         nc.vector.scalar_tensor_tensor(
             out=dw_term[:, 0, :], in0=dw[0][:], scalar=-LR * (1.0 + BETA), in1=w_cols[:, 0, :], op0=MULT, op1=ADD)
         nc.vector.scalar_tensor_tensor(
-            out=new_m[:, 0, :], in0=m_term[:, 0, :], scalar=-1.0 / (LR * BETA), in1=dw[0][:], op0=MULT, op1=ADD)
+            out=new_m[0][:], in0=m_term[:, 0, :], scalar=-1.0 / (LR * BETA), in1=dw[0][:], op0=MULT, op1=ADD)
         nc.vector.tensor_tensor(w_dst[0][:].indirect(offsets[:]), m_term[:, 0, :], dw_term[:, 0, :], ADD)
         store(w_dst[0], out_0, 0)
         fill(m_dst[0], m_src[0], (slice(0, COPIED[0]),))
-        for b in range(1, BLOCKS):
+        for b in (1, 2):
             weave_xm(b)
         quantise(xm_ops[1], E4M3)
-        quantise(xm_ops[2], E4M3)
-        for b in range(1, BLOCKS):
+        for b in (1, 2):
             gradient(b)
         gather_m(1)
-        scatter(m_dst, new_m[:, 0, :], out_1, 0)
+        scatter(m_dst, new_m[0][:], out_1, 0)
         for b in range(1, BLOCKS):
             update_m(b)
             fill(m_dst[b], m_src[b], (slice(0, T // 2), slice(T // 2, COPIED[b])))
             if b + 1 < BLOCKS:
                 gather_m(b + 1)
-            scatter(m_dst, new_m[:, b, :], out_1, b)
-            update_w(b)
+            scatter(m_dst, new_m[b][:], out_1, b)
+            new_w = w_cols[:, b, :]
+            if b == 2:
+                new_w = keep.tile([P, N], F32, name="new_w2", tag="xm3_grouped", align_bytes=64)[:]
+            update_w(b, new_w)
             if b >= 2:
                 fill(w_dst[b], w_src[b])
-            scatter(w_dst, w_cols[:, b, :], out_0, b)
+            scatter(w_dst, new_w, out_0, b)
+            if b == 1:
+                xm_ops[2] = operand("xm3", HALVES * P, codes_tag="new_m1")
+                weave_xm(3)
+                quantise(xm_ops[2], E4M3)
+                gradient(3)

@@ -28,8 +28,8 @@ CHUNKS = N // P
 X_ON_SCALAR = (32, 64)
 Y_ON_SCALAR = (4, 2)
 G_ON_SCALAR = (128, 0)
-LAST_XM_AFTER = 2
-COPIED = (1536, 1536, 1536, 2048)
+COPIED = 1792
+FIRST_PART = (0, 1536, 1024, 1024)
 
 
 def tile_attend_gsq_nag_kernel(tc, xT, wT, y, wt, xm, mT, offs, out_0, out_1):
@@ -80,7 +80,7 @@ def tile_attend_gsq_nag_kernel(tc, xT, wT, y, wt, xm, mT, offs, out_0, out_1):
         x_raw = [keep.tile([P, PACK, K], F32, name="x_raw%d" % h, tag="shared%d" % h, align_bytes=64) for h in range(HALVES)]
         y_sb = [keep.tile([P, PACK, N], F32, name="y_sb%d" % h, tag="y%d" % h) for h in range(HALVES)]
         xm_first = [keep.tile([P, PACK, P], F32, name="xm_first%d" % h) for h in range(HALVES)]
-        xm_mid = [keep.tile([P, PACK, 2 * P], F32, name="xm_mid%d" % h) for h in range(HALVES)]
+        xm_mid = [keep.tile([P, PACK, 2 * P], F32, name="xm_mid%d" % h, tag="mid%d" % h, align_bytes=64) for h in range(HALVES)]
         xm_last = [keep.tile([P, PACK, P], F32, name="xm_last%d" % h, tag="rest%d" % h) for h in range(HALVES)]
         w_src = [keep.tile([P, T], F32, name="w_src%d" % b, tag="table%d" % b, align_bytes=64) for b in range(BLOCKS)]
         m_src = [keep.tile([P, T], F32, name="m_src%d" % b) for b in range(BLOCKS)]
@@ -102,8 +102,6 @@ def tile_attend_gsq_nag_kernel(tc, xT, wT, y, wt, xm, mT, offs, out_0, out_1):
         for h in range(HALVES):
             nc.sync.dma_start(out=xm_first[h][:], in_=rows(xm[0, h * K : (h + 1) * K, :P]))
         nc.sync.dma_start(out=m_src[0][:], in_=block(mT, 0))
-        for h in range(HALVES):
-            nc.sync.dma_start(out=xm_mid[h][:], in_=rows(xm[0, h * K : (h + 1) * K, P : 3 * P]))
 
 
         w_cols = keep.tile([P, BLOCKS, N], F32, name="w_cols")
@@ -151,7 +149,7 @@ def tile_attend_gsq_nag_kernel(tc, xT, wT, y, wt, xm, mT, offs, out_0, out_1):
             else:
                 nc.vector.tensor_copy(out=dst, in_=src)
 
-        fill(w_dst[0], w_src[0])
+        fill(w_dst[0], w_src[0], (slice(0, T // 2), slice(T // 2, COPIED)))
         turn(0, (0, 1, 2, 3))
         fill(w_dst[1], w_src[1])
         turn(1, (0, 1, 2, 3))
@@ -227,17 +225,24 @@ def tile_attend_gsq_nag_kernel(tc, xT, wT, y, wt, xm, mT, offs, out_0, out_1):
 
         m_cols = keep.tile([P, BLOCKS, N], F32, name="m_cols")
         new_m = [keep.tile([P, N], F32, name="new_m%d" % b, align_bytes=64) for b in range(BLOCKS)]
-        m_term = keep.tile([P, BLOCKS, N], F32, name="m_term")
+        m_term = [keep.tile([P, N], F32, name="m_term%d" % b, tag=tag, align_bytes=64)
+                  for b, tag in enumerate(("m_term0", "mid0", "m_term2", "m_term3"))]
         dw_sb = keep.tile([P, BLOCKS, N], F32, name="dw_sb", tag="y0")
         dw_term = keep.tile([P, BLOCKS, N], F32, name="dw_term", tag="y1")
         m_dst = [keep.tile([P, T], F32, name="m_dst%d" % b, tag=tag, align_bytes=64)
-                 for b, tag in enumerate(("table0", "table1", "shared0", "shared1"))]
-        for b in range(1, BLOCKS):
-            nc.sync.dma_start(out=m_src[b][:], in_=block(mT, b))
-            nc.sync.dma_start(out=m_dst[b - 1][:, COPIED[b - 1]:], in_=block(mT, b - 1)[:, COPIED[b - 1]:])
-            if b == LAST_XM_AFTER:
-                for h in range(HALVES):
-                    nc.sync.dma_start(out=xm_last[h][:], in_=rows(xm[0, h * K : (h + 1) * K, 3 * P :]))
+                 for b, tag in enumerate(("table0", "mid1", "shared0", "shared1"))]
+        def load_tail(dst, table, b):
+            nc.sync.dma_start(out=dst[b][:, COPIED:], in_=block(table, b)[:, COPIED:])
+
+        nc.sync.dma_start(out=m_src[1][:], in_=block(mT, 1))
+        load_tail(m_dst, mT, 0)
+        for h in range(HALVES):
+            nc.sync.dma_start(out=xm_mid[h][:], in_=rows(xm[0, h * K : (h + 1) * K, P : 3 * P]))
+        nc.sync.dma_start(out=m_src[2][:], in_=block(mT, 2))
+        load_tail(w_dst, wT, 0)
+        for h in range(HALVES):
+            nc.sync.dma_start(out=xm_last[h][:], in_=rows(xm[0, h * K : (h + 1) * K, 3 * P :]))
+        nc.sync.dma_start(out=m_src[3][:], in_=block(mT, 3))
         for b in range(2, BLOCKS):
             w_dst.append(keep.tile([P, T], F32, name="w_dst%d" % b, tag="rest%d" % (b - 2)))
 
@@ -249,10 +254,10 @@ def tile_attend_gsq_nag_kernel(tc, xT, wT, y, wt, xm, mT, offs, out_0, out_1):
                 nc.sync.dma_start(out=block(out, b), in_=dst[:])
 
         def update_w(b, new_w):
-            nc.scalar.activation(m_term[:, b, :], m_cols[:, b, :], COPY, scale=-LR * BETA)
-            nc.gpsimd.tensor_tensor(new_w, w_cols[:, b, :], m_term[:, b, :], ADD)
-            nc.scalar.activation(dw_term[:, b, :], dw[b][:], COPY, scale=-LR * (1.0 + BETA))
-            nc.gpsimd.tensor_tensor(new_w, new_w, dw_term[:, b, :], ADD)
+            terms = [(dw_term[:, b, :], dw[b][:], -LR * (1.0 + BETA)), (m_term[b][:], m_cols[:, b, :], -LR * BETA)]
+            for (term, src, scale), total in zip(terms if b > 0 else terms[::-1], (w_cols[:, b, :], new_w)):
+                nc.scalar.activation(term, src, COPY, scale=scale)
+                nc.gpsimd.tensor_tensor(total, w_cols[:, b, :], term, ADD)
 
         def update_m(b):
             nc.scalar.copy(dw_sb[:, b, :], dw[b][:])
@@ -266,27 +271,33 @@ def tile_attend_gsq_nag_kernel(tc, xT, wT, y, wt, xm, mT, offs, out_0, out_1):
             store(dst[b], out, b)
 
         gradient(0)
-        nc.vector.tensor_scalar(
-            m_term[:, 0, :], m_src[0][:].indirect(offsets[:]), -LR * BETA * BETA, 0.0, MULT, ADD)
-        nc.vector.scalar_tensor_tensor(
-            out=dw_term[:, 0, :], in0=dw[0][:], scalar=-LR * (1.0 + BETA), in1=w_cols[:, 0, :], op0=MULT, op1=ADD)
-        nc.vector.scalar_tensor_tensor(
-            out=new_m[0][:], in0=m_term[:, 0, :], scalar=-1.0 / (LR * BETA), in1=dw[0][:], op0=MULT, op1=ADD)
-        nc.vector.tensor_tensor(w_dst[0][:].indirect(offsets[:]), m_term[:, 0, :], dw_term[:, 0, :], ADD)
-        store(w_dst[0], out_0, 0)
-        fill(m_dst[0], m_src[0], (slice(0, COPIED[0]),))
-        for b in (1, 2):
-            weave_xm(b)
-        quantise(xm_ops[1], E4M3)
-        for b in (1, 2):
-            gradient(b)
+        gather_m(0)
+        nc.vector.tensor_tensor(new_m[0][:], dw[0][:], m_cols[:, 0, :], ADD)
+        fill(m_dst[0], m_src[0], (slice(0, T // 2), slice(T // 2, COPIED)))
         gather_m(1)
         scatter(m_dst, new_m[0][:], out_1, 0)
+        update_w(0, w_cols[:, 0, :])
+        for b in (1, 2):
+            weave_xm(b)
+        for part in slot_halves:
+            quantise(xm_ops[1], E4M3, part)
+        for b in (1, 2):
+            gradient(b)
+        gather_m(2)
+        scatter(w_dst, w_cols[:, 0, :], out_0, 0)
+        gather_m(3)
         for b in range(1, BLOCKS):
-            update_m(b)
-            fill(m_dst[b], m_src[b], (slice(0, T // 2), slice(T // 2, COPIED[b])))
-            if b + 1 < BLOCKS:
-                gather_m(b + 1)
+            if b == 2:
+                fill(m_dst[b], m_src[b], (slice(0, FIRST_PART[b]),))
+                update_m(b)
+                xm_ops[2] = operand("xm3", HALVES * P, codes_tag="new_m1")
+                weave_xm(3)
+                quantise(xm_ops[2], E4M3)
+                gradient(3)
+            else:
+                update_m(b)
+                fill(m_dst[b], m_src[b], (slice(0, FIRST_PART[b]),))
+            fill(m_dst[b], m_src[b], (slice(FIRST_PART[b], T),))
             scatter(m_dst, new_m[b][:], out_1, b)
             new_w = w_cols[:, b, :]
             if b == 2:
@@ -295,8 +306,3 @@ def tile_attend_gsq_nag_kernel(tc, xT, wT, y, wt, xm, mT, offs, out_0, out_1):
             if b >= 2:
                 fill(w_dst[b], w_src[b])
             scatter(w_dst, new_w, out_0, b)
-            if b == 1:
-                xm_ops[2] = operand("xm3", HALVES * P, codes_tag="new_m1")
-                weave_xm(3)
-                quantise(xm_ops[2], E4M3)
-                gradient(3)

@@ -5,6 +5,7 @@ from concourse.masks import make_identity
 
 D, T, N, R = 512, 2048, 512, 1024
 LR, BETA = 0.1, 0.9
+DW_FACTOR = -LR * (1.0 + BETA)
 FLOPS = 2 * 2 * D * N * R
 
 F32 = mybir.dt.float32
@@ -25,11 +26,13 @@ K = P * PACK
 HALVES = R // K
 BLOCKS = D // P
 CHUNKS = N // P
+SPAN = P // PACK
+BAND = 16
+
 X_ON_SCALAR = (32, 64)
-Y_ON_SCALAR = (4, 2)
-G_ON_SCALAR = (128, 0)
+Y1_ON_SCALAR = 2
 COPIED = 1792
-FIRST_PART = (0, 1536, 1024, 1024)
+M1_FIRST = 1536
 
 
 def tile_attend_gsq_nag_kernel(tc, xT, wT, y, wt, xm, mT, offs, out_0, out_1):
@@ -38,6 +41,8 @@ def tile_attend_gsq_nag_kernel(tc, xT, wT, y, wt, xm, mT, offs, out_0, out_1):
         lists = ctx.enter_context(tc.tile_pool(name="lists", bufs=1))
         keep = ctx.enter_context(tc.tile_pool(name="keep", bufs=1))
         psum = ctx.enter_context(tc.psum_pool(name="psum", bufs=1))
+
+        slot_halves = (slice(0, N // 2), slice(N // 2, N))
 
         def block(table, b):
             return table[b * P : (b + 1) * P, :]
@@ -51,65 +56,56 @@ def tile_attend_gsq_nag_kernel(tc, xT, wT, y, wt, xm, mT, offs, out_0, out_1):
             scales = keep.tile([P, width], U8, name=name + "_scales", tag=scales_tag or name + "_scales", align_bytes=64)
             return grouped, codes, scales
 
-        def quantise(op, fmt, part=None):
+        def quantise(op, fmt, cols):
             grouped, codes, scales = op
-            part = part or slice(0, codes.shape[1])
             nc.vector.quantize_mx(
-                out=codes[:, part].bitcast(fmt), scales=scales[:, part],
-                in_=grouped[:, PACK * part.start : PACK * part.stop])
+                out=codes[:, cols].bitcast(fmt), scales=scales[:, cols],
+                in_=grouped[:, PACK * cols.start : PACK * cols.stop])
 
-        def weave(dst, src, on_scalar):
-            if on_scalar > 0:
-                nc.scalar.copy(out=dst[:, :on_scalar], in_=src[:, :on_scalar])
-            if on_scalar < dst.shape[1]:
-                nc.vector.tensor_copy(out=dst[:, on_scalar:], in_=src[:, on_scalar:])
-
-        def dealt_views(op, raw):
-            dst = op[0][:].rearrange("p (t m j) -> p m j t", t=PACK, j=PACK)
-            src = raw[:].rearrange("p j (m t) -> p m j t", t=PACK)
+        def weave_views(grouped, four_rows):
+            dst = grouped.rearrange("p (c i t) -> p c t i", i=PACK, t=PACK)
+            src = four_rows.rearrange("p t (c i) -> p c t i", i=PACK)
             return dst, src
 
-        def plain_views(grouped, planes):
-            dst = grouped.rearrange("p (c i t) -> p c t i", i=4, t=PACK)
-            src = planes.rearrange("p t (c i) -> p c t i", i=4)
-            return dst, src
-
-        slot_halves = (slice(0, N // 2), slice(N // 2, N))
-
-        offsets = lists.tile([P, N // 16], U16, name="offsets")
+        offsets = lists.tile([P, N // BAND], U16, name="offsets")
         x_raw = [keep.tile([P, PACK, K], F32, name="x_raw%d" % h, tag="shared%d" % h, align_bytes=64) for h in range(HALVES)]
         y_sb = [keep.tile([P, PACK, N], F32, name="y_sb%d" % h, tag="y%d" % h) for h in range(HALVES)]
         xm_first = [keep.tile([P, PACK, P], F32, name="xm_first%d" % h) for h in range(HALVES)]
-        xm_mid = [keep.tile([P, PACK, 2 * P], F32, name="xm_mid%d" % h, tag="mid%d" % h, align_bytes=64) for h in range(HALVES)]
-        xm_last = [keep.tile([P, PACK, P], F32, name="xm_last%d" % h, tag="rest%d" % h) for h in range(HALVES)]
+        xm_mid = [keep.tile([P, PACK, P], F32, name="xm_mid%d" % h, tag="mid%d" % h, align_bytes=64) for h in range(HALVES)]
+        xm_last = [keep.tile([P, PACK, 2 * P], F32, name="xm_last%d" % h, tag="rest%d" % h, align_bytes=64) for h in range(HALVES)]
         w_src = [keep.tile([P, T], F32, name="w_src%d" % b, tag="table%d" % b, align_bytes=64) for b in range(BLOCKS)]
         m_src = [keep.tile([P, T], F32, name="m_src%d" % b) for b in range(BLOCKS)]
-        wt_sb = [keep.tile([P, PACK], F32, name="wt_sb%d" % h, tag="wt%d" % h, align_bytes=64) for h in range(HALVES)]
+        wt_all = keep.tile([P, HALVES, 2 * PACK], F32, name="wt_sb", tag="wt1", align_bytes=64)
+        wt_sb = [wt_all[:, h, :PACK] for h in range(HALVES)]
         ident = keep.tile([P, P], F32, name="ident")
         make_identity(nc, ident[:])
 
-        for h in range(HALVES):
-            nc.scalar.dma_start(out=wt_sb[h][:], in_=wt[0, h * K : (h + 1) * K, :].rearrange("(p t) o -> p (t o)", t=PACK))
-        for b in range(BLOCKS):
+        def load_xm(tiles, first, last):
+            for h in range(HALVES):
+                nc.sync.dma_start(out=tiles[h][:], in_=rows(xm[0, h * K : (h + 1) * K, first * P : last * P]))
+
+        def load_m(b):
+            nc.sync.dma_start(out=m_src[b][:], in_=block(mT, b))
+
+        nc.scalar.dma_start(out=wt_all[:, :, :PACK], in_=wt[0].rearrange("(h p t) o -> p h (t o)", h=HALVES, t=PACK))
+        nc.sync.dma_start(out=w_src[0][:], in_=block(wT, 0))
+        nc.sync.dma_start(offsets[:], offs)
+        for b in range(1, BLOCKS):
             nc.sync.dma_start(out=w_src[b][:], in_=block(wT, b))
-            if b == 0:
-                nc.sync.dma_start(offsets[:], offs)
         for h in range(HALVES):
             nc.sync.dma_start(out=x_raw[h][:], in_=rows(xT[0, :, h * K : (h + 1) * K]))
         for h in range(HALVES):
-            for pair in (slice(0, 2), slice(2, 4)):
+            for pair in (slice(0, PACK // 2), slice(PACK // 2, PACK)):
                 nc.sync.dma_start(out=y_sb[h][:, pair, :], in_=rows(y[0, h * K : (h + 1) * K, :])[:, pair, :])
-        for h in range(HALVES):
-            nc.sync.dma_start(out=xm_first[h][:], in_=rows(xm[0, h * K : (h + 1) * K, :P]))
-        nc.sync.dma_start(out=m_src[0][:], in_=block(mT, 0))
-
+        load_xm(xm_first, 0, 1)
+        load_m(0)
 
         w_cols = keep.tile([P, BLOCKS, N], F32, name="w_cols")
         w_dst = [keep.tile([P, T], F32, name="w_dst%d" % b) for b in range(2)]
         w_turned = [keep.tile([P, 2, 2, P, 2], BF16, name="w_turned%d" % i, align_bytes=64) for i in range(CHUNKS // 2)]
 
-        def fill(dst, src, parts=(slice(0, T // 2), slice(T // 2, T))):
-            for part in parts:
+        def fill(dst, src, first=0, cut=T // 2, last=T):
+            for part in (slice(first, cut), slice(cut, last)):
                 nc.scalar.activation(dst[:, part], src[:, part], COPY)
 
         x_op = [operand("x%d" % h) for h in range(HALVES)]
@@ -118,64 +114,74 @@ def tile_attend_gsq_nag_kernel(tc, xT, wT, y, wt, xm, mT, offs, out_0, out_1):
         w_codes = keep.tile([P, N], U32, name="w_codes", align_bytes=64)
         w_scales = keep.tile([P, N], U8, name="w_scales", align_bytes=64)
         g_op = [operand("g0", scales_tag="wt1"), operand("g1")]
-        xm_ops = [operand("xm0", HALVES * P), operand("xm12", 2 * HALVES * P), None]
-        xm_place = [(0, 0), (1, 0), (1, HALVES * P), (2, 0)]
+        xm_width = HALVES * P
+        xm_op0 = operand("xm0", xm_width)
+        xm_op1 = operand("xm1", xm_width)
+        xm_place = [(xm_op0, 0), (xm_op1, 0)]
 
         def turn(b, chunks):
-            cols = slice(chunks[0] * P, (chunks[-1] + 1) * P)
-            nc.vector.tensor_copy(w_cols[:, b, cols], w_src[b][:].indirect(offsets[:, cols.start // 16 : cols.stop // 16]))
-            turned = psum.tile([P, len(chunks), P], F32, name="turned%d%d" % (b, chunks[0]), tag="bank%d" % (b + chunks[0] // 2))
+            slots = slice(chunks[0] * P, (chunks[-1] + 1) * P)
+            nc.vector.tensor_copy(
+                w_cols[:, b, slots], w_src[b][:].indirect(offsets[:, slots.start // BAND : slots.stop // BAND]))
+            turned = psum.tile(
+                [P, len(chunks), P], F32, name="turned%d%d" % (b, chunks[0]), tag="bank%d" % (b + chunks[0] // 2))
             for i, c in enumerate(chunks):
                 nc.tensor.transpose(turned[:, i, :], w_cols[:, b, c * P : (c + 1) * P], ident[:])
             for i in range(0, len(chunks), 2):
                 nc.scalar.copy(
-                    out=w_turned[chunks[i] // 2][:, :, :, 32 * b : 32 * (b + 1), :].rearrange("s c u q e -> s c q u e"),
+                    out=w_turned[chunks[i] // 2][:, :, :, SPAN * b : SPAN * (b + 1), :].rearrange("s c u q e -> s c q u e"),
                     in_=turned[:, i : i + 2, :].rearrange("s c (q u e) -> s c q u e", u=2, e=2))
 
-        def turn_back(pair):
-            back = psum.tile([P, 2, 2, P], F32, name="back%d" % pair, tag="bank%d" % (5 + pair))
-            words = w_turned[pair][:].rearrange("s c u q e -> s (c u q e)").bitcast(F32)
+        def turn_back(half):
+            back = psum.tile([P, 2, 2, P], F32, name="back%d" % half, tag="bank%d" % (BLOCKS + 1 + half))
+            pairs = w_turned[half][:].rearrange("s c u q e -> s (c u q e)").bitcast(F32)
             for c in range(2):
                 for u in range(2):
-                    k = 2 * c + u
-                    nc.tensor.transpose(back[:, c, u, :], words[:, k * P : (k + 1) * P], ident[:])
+                    run = 2 * c + u
+                    nc.tensor.transpose(back[:, c, u, :], pairs[:, run * P : (run + 1) * P], ident[:])
             return back
 
-        def copy_back(pair, back):
-            dst = w_grouped[pair].bitcast(F32).rearrange("p (c s u) -> p c s u", c=2, u=2)
-            src = back[:].rearrange("p c u s -> p c s u")
-            if pair == 0:
-                nc.scalar.copy(out=dst, in_=src)
-            else:
-                nc.vector.tensor_copy(out=dst, in_=src)
+        def copy_back(copy, half, back):
+            dst = w_grouped[half].bitcast(F32).rearrange("p (c s u) -> p c s u", c=2, u=2)
+            copy(out=dst, in_=back[:].rearrange("p c u s -> p c s u"))
 
-        fill(w_dst[0], w_src[0], (slice(0, T // 2), slice(T // 2, COPIED)))
-        turn(0, (0, 1, 2, 3))
-        fill(w_dst[1], w_src[1])
-        turn(1, (0, 1, 2, 3))
-        turn(2, (0, 1, 2, 3))
-        turn(3, (0, 1))
-        turn(3, (2, 3))
-        backs = [turn_back(pair) for pair in range(2)]
-        weave(*dealt_views(x_op[0], x_raw[0]), on_scalar=X_ON_SCALAR[0])
-        quantise(x_op[0], E4M3)
-        for pair in range(2):
-            copy_back(pair, backs[pair])
-        for pair, part in enumerate(slot_halves):
-            nc.vector.quantize_mx(out=w_codes[:, part].bitcast(E4M3), scales=w_scales[:, part], in_=w_grouped[pair])
-        weave(*dealt_views(x_op[1], x_raw[1]), on_scalar=X_ON_SCALAR[1])
-        quantise(x_op[1], E4M3)
+        def weave_x(h):
+            dst = x_op[h][0][:].rearrange("p (t m j) -> p m j t", t=PACK, j=PACK)
+            src = x_raw[h][:].rearrange("p j (m t) -> p m j t", t=PACK)
+            cut = X_ON_SCALAR[h]
+            nc.scalar.copy(out=dst[:, :cut], in_=src[:, :cut])
+            nc.vector.tensor_copy(out=dst[:, cut:], in_=src[:, cut:])
 
-        def weigh_y(h):
+        every_chunk = tuple(range(CHUNKS))
+        fill(w_dst[0], w_src[0], last=COPIED)
+        turn(0, every_chunk)
+        fill(w_dst[1], w_src[1], last=COPIED)
+        turn(1, every_chunk)
+        w0_scaled = keep.tile([P, N], F32, name="w0_scaled")
+        nc.scalar.activation(w0_scaled[:], w_cols[:, 0, :], COPY, scale=1.0 / DW_FACTOR)
+        turn(2, every_chunk)
+        turn(3, every_chunk[: CHUNKS // 2])
+        turn(3, every_chunk[CHUNKS // 2 :])
+        backs = [turn_back(half) for half in range(2)]
+        weave_x(0)
+        quantise(x_op[0], E4M3, slice(0, K))
+        copy_back(nc.scalar.copy, 0, backs[0])
+        copy_back(nc.vector.tensor_copy, 1, backs[1])
+        for half, part in enumerate(slot_halves):
+            nc.vector.quantize_mx(out=w_codes[:, part].bitcast(E4M3), scales=w_scales[:, part], in_=w_grouped[half])
+        weave_x(1)
+        quantise(x_op[1], E4M3, slice(0, K))
+
+        def weigh_y(h, on_scalar):
             for t in range(PACK):
-                if t < Y_ON_SCALAR[h]:
+                if t < on_scalar:
                     nc.scalar.activation(y_sb[h][:, t, :], y_sb[h][:, t, :], COPY, scale=wt_sb[h][:, t : t + 1])
                 else:
                     nc.gpsimd.tensor_scalar(
                         y_sb[h][:, t, :], y_sb[h][:, t, :], wt_sb[h][:, t : t + 1], 0.0, MULT, ADD)
 
         def residual(h):
-            grouped, codes, scales = x_op[h]
+            codes, scales = x_op[h][1:]
             for t in range(PACK):
                 cols = slice(t * P, (t + 1) * P)
                 a = psum.tile([P, N], F32, name="a%d%d" % (h, t), tag="bank%d" % (PACK * h + t))
@@ -190,119 +196,155 @@ def tile_attend_gsq_nag_kernel(tc, xT, wT, y, wt, xm, mT, offs, out_0, out_1):
                         op0=MULT, op1=SUB,
                     )
 
-        def weave_xm(b):
-            for h in range(HALVES):
-                raw = (xm_first[h][:], xm_mid[h][:, :, :P], xm_mid[h][:, :, P:], xm_last[h][:])[b]
-                op, first = xm_place[b]
+        def weave_xm(b, halves=range(HALVES)):
+            op, first = xm_place[b]
+            for h in halves:
+                raw = (xm_first[h][:], xm_mid[h][:], xm_last[h][:, :, :P], xm_last[h][:, :, P:])[b]
                 lo = PACK * (first + h * P)
-                dst, src = plain_views(xm_ops[op][0][:, lo : lo + K], raw)
+                dst, src = weave_views(op[0][:, lo : lo + K], raw)
                 nc.scalar.copy(out=dst, in_=src)
 
-        weigh_y(0)
+        weigh_y(0, PACK)
         residual(0)
-        weigh_y(1)
-        weave(*plain_views(g_op[0][0][:], y_sb[0][:]), on_scalar=G_ON_SCALAR[0])
+        weigh_y(1, Y1_ON_SCALAR)
+        dst, src = weave_views(g_op[0][0][:], y_sb[0][:])
+        nc.scalar.copy(out=dst, in_=src)
         weave_xm(0)
         residual(1)
         for part in slot_halves:
-            weave(*plain_views(g_op[1][0][:, PACK * part.start : PACK * part.stop], y_sb[1][:, :, part]), on_scalar=0)
-        quantise(g_op[0], E5M2)
-        quantise(xm_ops[0], E4M3, slice(0, P))
-        quantise(g_op[1], E5M2)
-        quantise(xm_ops[0], E4M3, slice(P, 2 * P))
+            dst, src = weave_views(g_op[1][0][:, PACK * part.start : PACK * part.stop], y_sb[1][:, :, part])
+            nc.vector.tensor_copy(out=dst, in_=src)
+        for h in range(HALVES):
+            quantise(g_op[h], E5M2, slice(0, N))
+            quantise(xm_op0, E4M3, slice(h * P, (h + 1) * P))
 
-        dw = [psum.tile([P, N], F32, name="dw%d" % b, tag="bank%d" % b) for b in range(BLOCKS)]
+        dw = [psum.tile([P, N], F32, name="dw0", tag="bank0")]
 
         def gradient(b):
+            op, first = xm_place[b]
+            codes, scales = op[1:]
             for h in range(HALVES):
-                op, first = xm_place[b]
                 cols = slice(first + h * P, first + (h + 1) * P)
                 nc.tensor.matmul_mx(
-                    out=dw[b][:], lhsT=xm_ops[op][1][:, cols].bitcast(E4M3), lhsT_scale=xm_ops[op][2][:, cols],
+                    out=dw[b][:], lhsT=codes[:, cols].bitcast(E4M3), lhsT_scale=scales[:, cols],
                     rhs=g_op[h][1][:].bitcast(E5M2), rhs_scale=g_op[h][2][:],
                     start=(h == 0), stop=(h == HALVES - 1),
                 )
 
         m_cols = keep.tile([P, BLOCKS, N], F32, name="m_cols")
-        new_m = [keep.tile([P, N], F32, name="new_m%d" % b, align_bytes=64) for b in range(BLOCKS)]
-        m_term = [keep.tile([P, N], F32, name="m_term%d" % b, tag=tag, align_bytes=64)
-                  for b, tag in enumerate(("m_term0", "mid0", "m_term2", "m_term3"))]
+        new_m = [None] + [keep.tile([P, N], F32, name="new_m%d" % b, align_bytes=64) for b in range(1, BLOCKS)]
+        m_term = [keep.tile([P, N], F32, name="m_term0")]
         dw_sb = keep.tile([P, BLOCKS, N], F32, name="dw_sb", tag="y0")
         dw_term = keep.tile([P, BLOCKS, N], F32, name="dw_term", tag="y1")
         m_dst = [keep.tile([P, T], F32, name="m_dst%d" % b, tag=tag, align_bytes=64)
-                 for b, tag in enumerate(("table0", "mid1", "shared0", "shared1"))]
-        def load_tail(dst, table, b):
-            nc.sync.dma_start(out=dst[b][:, COPIED:], in_=block(table, b)[:, COPIED:])
+                 for b, tag in enumerate(("table0", "shared0", "rest0", "shared1"))]
 
-        nc.sync.dma_start(out=m_src[1][:], in_=block(mT, 1))
-        load_tail(m_dst, mT, 0)
-        for h in range(HALVES):
-            nc.sync.dma_start(out=xm_mid[h][:], in_=rows(xm[0, h * K : (h + 1) * K, P : 3 * P]))
-        nc.sync.dma_start(out=m_src[2][:], in_=block(mT, 2))
-        load_tail(w_dst, wT, 0)
-        for h in range(HALVES):
-            nc.sync.dma_start(out=xm_last[h][:], in_=rows(xm[0, h * K : (h + 1) * K, 3 * P :]))
-        nc.sync.dma_start(out=m_src[3][:], in_=block(mT, 3))
-        for b in range(2, BLOCKS):
-            w_dst.append(keep.tile([P, T], F32, name="w_dst%d" % b, tag="rest%d" % (b - 2)))
+        def load_tail(dst, table, b=0):
+            nc.sync.dma_start(out=dst[:, COPIED:], in_=block(table, b)[:, COPIED:])
 
-        def store(dst, out, b):
-            if out is out_0 and b == BLOCKS - 1:
-                nc.sync.dma_start(out=block(out, b)[:, : T // 2], in_=dst[:, : T // 2])
-                nc.scalar.dma_start(out=block(out, b)[:, T // 2 :], in_=dst[:, T // 2 :])
-            else:
-                nc.sync.dma_start(out=block(out, b), in_=dst[:])
+        load_m(1)
+        load_tail(m_dst[0], mT)
+        load_xm(xm_mid, 1, 2)
+        load_m(2)
+        load_tail(w_dst[0], wT)
+        nc.sync.dma_start(out=m_dst[1][:], in_=block(mT, 1))
+        load_xm(xm_last, 2, 4)
+        load_m(3)
+        load_tail(w_dst[1], wT, 1)
+        w_dst.append(keep.tile([P, T], F32, name="w_dst2", tag="rest1", align_bytes=64))
 
-        def update_w(b, new_w):
-            terms = [(dw_term[:, b, :], dw[b][:], -LR * (1.0 + BETA)), (m_term[b][:], m_cols[:, b, :], -LR * BETA)]
-            for (term, src, scale), total in zip(terms if b > 0 else terms[::-1], (w_cols[:, b, :], new_w)):
-                nc.scalar.activation(term, src, COPY, scale=scale)
-                nc.gpsimd.tensor_tensor(total, w_cols[:, b, :], term, ADD)
+        def gather_m(b):
+            nc.vector.tensor_scalar(m_cols[:, b, :], m_src[b][:].indirect(offsets[:]), BETA, 0.0, MULT, ADD)
 
         def update_m(b):
             nc.scalar.copy(dw_sb[:, b, :], dw[b][:])
             nc.gpsimd.tensor_tensor(new_m[b][:], m_cols[:, b, :], dw_sb[:, b, :], ADD)
 
-        def gather_m(b):
-            nc.vector.tensor_scalar(m_cols[:, b, :], m_src[b][:].indirect(offsets[:]), BETA, 0.0, MULT, ADD)
+        def add_dw_term(b, total):
+            nc.scalar.activation(dw_term[:, b, :], dw[b][:], COPY, scale=-LR * (1.0 + BETA))
+            nc.gpsimd.tensor_tensor(total, w_cols[:, b, :], dw_term[:, b, :], ADD)
 
-        def scatter(dst, src, out, b):
-            nc.vector.tensor_copy(dst[b][:].indirect(offsets[:]), src)
-            store(dst[b], out, b)
+        def add_m_term(b, total):
+            nc.scalar.activation(m_term[b][:], m_cols[:, b, :], COPY, scale=-LR * BETA)
+            nc.gpsimd.tensor_tensor(total, w_cols[:, b, :], m_term[b][:], ADD)
+
+        def scatter(dst, values):
+            nc.vector.tensor_copy(dst[:].indirect(offsets[:]), values)
+
+        def finish_m(b):
+            scatter(m_dst[b], new_m[b][:])
+            nc.sync.dma_start(out=block(out_1, b), in_=m_dst[b][:])
+
+        def finish_w(b, values):
+            scatter(w_dst[b], values)
+            nc.sync.dma_start(out=block(out_0, b), in_=w_dst[b][:])
+
+        sums = [psum.tile([P, P], F32, name="sum%d" % c, tag="bank%d" % (BLOCKS + c)) for c in range(CHUNKS)]
+
+        def add_turned(values, start, stop):
+            for c in range(CHUNKS):
+                nc.tensor.matmul(
+                    out=sums[c][:], lhsT=values[:, c * P : (c + 1) * P], rhs=ident[:], start=start, stop=stop, is_transpose=True)
 
         gradient(0)
         gather_m(0)
-        nc.vector.tensor_tensor(new_m[0][:], dw[0][:], m_cols[:, 0, :], ADD)
-        fill(m_dst[0], m_src[0], (slice(0, T // 2), slice(T // 2, COPIED)))
+        fill(m_dst[0], m_src[0], last=COPIED)
+        nc.scalar.copy(dw_sb[:, 0, :], dw[0][:])
         gather_m(1)
-        scatter(m_dst, new_m[0][:], out_1, 0)
-        update_w(0, w_cols[:, 0, :])
-        for b in (1, 2):
-            weave_xm(b)
-        for part in slot_halves:
-            quantise(xm_ops[1], E4M3, part)
-        for b in (1, 2):
-            gradient(b)
+        nc.vector.tensor_tensor(m_dst[0][:].indirect(offsets[:]), m_cols[:, 0, :], dw_sb[:, 0, :], ADD)
+        nc.sync.dma_start(out=block(out_1, 0), in_=m_dst[0][:])
+        nc.scalar.activation(m_term[0][:], m_cols[:, 0, :], COPY, scale=BETA / (1.0 + BETA))
+        add_turned(w0_scaled[:], True, False)
+        add_turned(dw_sb[:, 0, :], False, False)
+        add_turned(m_term[0][:], False, True)
+        weave_xm(1, (0,))
+        w0_turned = keep.tile([P, CHUNKS, P], F32, name="w0_turned", tag="mid0", align_bytes=64)
+        for c in range(CHUNKS):
+            nc.scalar.copy(w0_turned[:, c, :], sums[c][:])
+        weave_xm(1, (1,))
+        quantise(xm_op1, E4M3, slice(0, xm_width))
+        w0_back = psum.tile([P, CHUNKS, P], F32, name="w0_back", tag="bank1")
+        for c in range(CHUNKS):
+            nc.tensor.transpose(w0_back[:, c, :], w0_turned[:, c, :], ident[:])
+        new_w0 = keep.tile([P, N], F32, name="new_w0")
+        nc.scalar.activation(new_w0[:], w0_back[:].rearrange("p c s -> p (c s)"), COPY, scale=DW_FACTOR)
+        for b, bank in ((1, 7), (2, 2), (3, 3)):
+            dw.append(psum.tile([P, N], F32, name="dw%d" % b, tag="bank%d" % bank))
+        gradient(1)
         gather_m(2)
-        scatter(w_dst, w_cols[:, 0, :], out_0, 0)
+        finish_w(0, new_w0[:])
+
+        for b, tag in ((1, "mid0"), (2, "m_term2"), (3, "m_term3")):
+            m_term.append(keep.tile([P, N], F32, name="m_term%d" % b, tag=tag, align_bytes=64))
+        update_m(1)
+        finish_m(1)
+        add_dw_term(1, w_cols[:, 1, :])
+        add_m_term(1, w_cols[:, 1, :])
+        xm_op23 = operand("xm23", 2 * xm_width)
+        xm_place.extend([(xm_op23, 0), (xm_op23, xm_width)])
+        for b in (2, 3):
+            weave_xm(b)
+        for b in (2, 3):
+            quantise(xm_op23, E4M3, slice(xm_place[b][1], xm_place[b][1] + xm_width))
+            gradient(b)
+        w_dst.append(keep.tile([P, T], F32, name="w_dst3", tag="xm23_grouped", align_bytes=64))
         gather_m(3)
-        for b in range(1, BLOCKS):
-            if b == 2:
-                fill(m_dst[b], m_src[b], (slice(0, FIRST_PART[b]),))
-                update_m(b)
-                xm_ops[2] = operand("xm3", HALVES * P, codes_tag="new_m1")
-                weave_xm(3)
-                quantise(xm_ops[2], E4M3)
-                gradient(3)
-            else:
-                update_m(b)
-                fill(m_dst[b], m_src[b], (slice(0, FIRST_PART[b]),))
-            fill(m_dst[b], m_src[b], (slice(FIRST_PART[b], T),))
-            scatter(m_dst, new_m[b][:], out_1, b)
-            new_w = w_cols[:, b, :]
-            if b == 2:
-                new_w = keep.tile([P, N], F32, name="new_w2", tag="xm3_grouped", align_bytes=64)[:]
-            update_w(b, new_w)
-            if b >= 2:
-                fill(w_dst[b], w_src[b])
-            scatter(w_dst, new_w, out_0, b)
+        finish_w(1, w_cols[:, 1, :])
+
+        update_m(2)
+        fill(m_dst[2], m_src[2])
+        finish_m(2)
+        add_dw_term(2, w_cols[:, 2, :])
+        add_m_term(2, w_cols[:, 2, :])
+        fill(w_dst[2], w_src[2])
+        finish_w(2, w_cols[:, 2, :])
+
+        update_m(3)
+        fill(m_dst[3], m_src[3])
+        finish_m(3)
+        add_dw_term(3, w_cols[:, 3, :])
+        add_m_term(3, w_cols[:, 3, :])
+        fill(w_dst[3], w_src[3])
+        scatter(w_dst[3], w_cols[:, 3, :])
+        nc.sync.dma_start(out=block(out_0, 3)[:, : T // 2], in_=w_dst[3][:, : T // 2])
+        nc.scalar.dma_start(out=block(out_0, 3)[:, T // 2 :], in_=w_dst[3][:, T // 2 :])

@@ -75,8 +75,9 @@ def tile_attend_gsq_nag_kernel(tc, xT, wT, y, wt, xm, mT, offs, out_0, out_1):
         xm_last = [keep.tile([P, PACK, 2 * P], F32, name="xm_last%d" % h, tag="rest%d" % h, align_bytes=64) for h in range(HALVES)]
         w_src = [keep.tile([P, T], F32, name="w_src%d" % b, tag="table%d" % b, align_bytes=64) for b in range(BLOCKS)]
         m_src = [keep.tile([P, T], F32, name="m_src%d" % b) for b in range(BLOCKS)]
-        wt_all = keep.tile([P, HALVES, 2 * PACK], F32, name="wt_sb", tag="wt1", align_bytes=64)
-        wt_sb = [wt_all[:, h, :PACK] for h in range(HALVES)]
+        wt_rows = keep.tile([P, K], F32, name="wt_rows")
+        wt_all = keep.tile([P, HALVES, PACK], F32, name="wt_sb", tag="wt1", align_bytes=64)
+        wt_sb = [wt_all[:, h, :] for h in range(HALVES)]
         ident = keep.tile([P, P], F32, name="ident")
         make_identity(nc, ident[:])
 
@@ -87,9 +88,10 @@ def tile_attend_gsq_nag_kernel(tc, xT, wT, y, wt, xm, mT, offs, out_0, out_1):
         def load_m(b):
             nc.sync.dma_start(out=m_src[b][:], in_=block(mT, b))
 
-        nc.scalar.dma_start(out=wt_all[:, :, :PACK], in_=wt[0].rearrange("(h p t) o -> p h (t o)", h=HALVES, t=PACK))
+        nc.vector.memset(wt_rows[:], 0.0)
         nc.sync.dma_start(out=w_src[0][:], in_=block(wT, 0))
         nc.sync.dma_start(offsets[:], offs)
+        nc.sync.dma_start(out=wt_rows[:: P // HALVES, :], in_=wt[0].rearrange("(h k) o -> h (k o)", h=HALVES))
         for b in range(1, BLOCKS):
             nc.sync.dma_start(out=w_src[b][:], in_=block(wT, b))
         for h in range(HALVES):
@@ -157,6 +159,10 @@ def tile_attend_gsq_nag_kernel(tc, xT, wT, y, wt, xm, mT, offs, out_0, out_1):
         turn(0, every_chunk)
         fill(w_dst[1], w_src[1], last=COPIED)
         turn(1, every_chunk)
+        wt_turned = psum.tile([P, PACK, P], F32, name="wt_turned", tag="bank7")
+        for t in range(PACK):
+            nc.tensor.transpose(wt_turned[:, t, :], wt_rows[:, t::PACK], ident[:])
+        nc.scalar.copy(out=wt_all[:], in_=wt_turned[:, :, :: P // HALVES].rearrange("p t h -> p h t"))
         w0_scaled = keep.tile([P, N], F32, name="w0_scaled")
         nc.scalar.activation(w0_scaled[:], w_cols[:, 0, :], COPY, scale=1.0 / DW_FACTOR)
         turn(2, every_chunk)
@@ -243,7 +249,6 @@ def tile_attend_gsq_nag_kernel(tc, xT, wT, y, wt, xm, mT, offs, out_0, out_1):
             nc.sync.dma_start(out=dst[:, COPIED:], in_=block(table, b)[:, COPIED:])
 
         load_m(1)
-        load_tail(m_dst[0], mT)
         load_xm(xm_mid, 1, 2)
         load_m(2)
         load_tail(w_dst[0], wT)
@@ -288,7 +293,7 @@ def tile_attend_gsq_nag_kernel(tc, xT, wT, y, wt, xm, mT, offs, out_0, out_1):
 
         gradient(0)
         gather_m(0)
-        fill(m_dst[0], m_src[0], last=COPIED)
+        fill(m_dst[0], m_src[0])
         nc.scalar.copy(dw_sb[:, 0, :], dw[0][:])
         gather_m(1)
         nc.vector.tensor_tensor(m_dst[0][:].indirect(offsets[:]), m_cols[:, 0, :], dw_sb[:, 0, :], ADD)

@@ -32,6 +32,7 @@ BAND = 16
 X_ON_SCALAR = (32, 64)
 Y1_ON_SCALAR = 2
 COPIED = 1792
+M0_COPIED = 1536
 M1_FIRST = 1536
 
 
@@ -70,8 +71,7 @@ def tile_attend_gsq_nag_kernel(tc, xT, wT, y, wt, xm, mT, offs, out_0, out_1):
         offsets = lists.tile([P, N // BAND], U16, name="offsets")
         x_raw = [keep.tile([P, PACK, K], F32, name="x_raw%d" % h, tag="shared%d" % h, align_bytes=64) for h in range(HALVES)]
         y_sb = [keep.tile([P, PACK, N], F32, name="y_sb%d" % h, tag="y%d" % h) for h in range(HALVES)]
-        xm_first = [keep.tile([P, PACK, P], F32, name="xm_first%d" % h) for h in range(HALVES)]
-        xm_mid = [keep.tile([P, PACK, P], F32, name="xm_mid%d" % h, tag="mid%d" % h, align_bytes=64) for h in range(HALVES)]
+        xm_first = [keep.tile([P, PACK, 2 * P], F32, name="xm_first%d" % h) for h in range(HALVES)]
         xm_last = [keep.tile([P, PACK, 2 * P], F32, name="xm_last%d" % h, tag="rest%d" % h, align_bytes=64) for h in range(HALVES)]
         w_src = [keep.tile([P, T], F32, name="w_src%d" % b, tag="table%d" % b, align_bytes=64) for b in range(BLOCKS)]
         m_src = [keep.tile([P, T], F32, name="m_src%d" % b) for b in range(BLOCKS)]
@@ -99,7 +99,7 @@ def tile_attend_gsq_nag_kernel(tc, xT, wT, y, wt, xm, mT, offs, out_0, out_1):
         for h in range(HALVES):
             for pair in (slice(0, PACK // 2), slice(PACK // 2, PACK)):
                 nc.sync.dma_start(out=y_sb[h][:, pair, :], in_=rows(y[0, h * K : (h + 1) * K, :])[:, pair, :])
-        load_xm(xm_first, 0, 1)
+        load_xm(xm_first, 0, 2)
         load_m(0)
 
         w_cols = keep.tile([P, BLOCKS, N], F32, name="w_cols")
@@ -117,9 +117,7 @@ def tile_attend_gsq_nag_kernel(tc, xT, wT, y, wt, xm, mT, offs, out_0, out_1):
         w_scales = keep.tile([P, N], U8, name="w_scales", align_bytes=64)
         g_op = [operand("g0", scales_tag="wt1"), operand("g1")]
         xm_width = HALVES * P
-        xm_op0 = operand("xm0", xm_width)
-        xm_op1 = operand("xm1", xm_width)
-        xm_place = [(xm_op0, 0), (xm_op1, 0)]
+        xm_ops = [operand("xm01", HALVES * xm_width)]
 
         def turn(b, chunks):
             slots = slice(chunks[0] * P, (chunks[-1] + 1) * P)
@@ -202,12 +200,10 @@ def tile_attend_gsq_nag_kernel(tc, xT, wT, y, wt, xm, mT, offs, out_0, out_1):
                         op0=MULT, op1=SUB,
                     )
 
-        def weave_xm(b, halves=range(HALVES)):
-            op, first = xm_place[b]
-            for h in halves:
-                raw = (xm_first[h][:], xm_mid[h][:], xm_last[h][:, :, :P], xm_last[h][:, :, P:])[b]
-                lo = PACK * (first + h * P)
-                dst, src = weave_views(op[0][:, lo : lo + K], raw)
+        def weave_xm(pair):
+            for h in range(HALVES):
+                lo = PACK * h * xm_width
+                dst, src = weave_views(xm_ops[pair][0][:, lo : lo + PACK * xm_width], (xm_first, xm_last)[pair][h][:])
                 nc.scalar.copy(out=dst, in_=src)
 
         weigh_y(0, PACK)
@@ -222,15 +218,15 @@ def tile_attend_gsq_nag_kernel(tc, xT, wT, y, wt, xm, mT, offs, out_0, out_1):
             nc.vector.tensor_copy(out=dst, in_=src)
         for h in range(HALVES):
             quantise(g_op[h], E5M2, slice(0, N))
-            quantise(xm_op0, E4M3, slice(h * P, (h + 1) * P))
+            quantise(xm_ops[0], E4M3, slice(h * xm_width, (h + 1) * xm_width))
 
-        dw = [psum.tile([P, N], F32, name="dw0", tag="bank0")]
+        dw = [psum.tile([P, N], F32, name="dw%d" % b, tag="bank%d" % b) for b in range(BLOCKS - 1)]
 
         def gradient(b):
-            op, first = xm_place[b]
-            codes, scales = op[1:]
+            codes, scales = xm_ops[b // 2][1:]
             for h in range(HALVES):
-                cols = slice(first + h * P, first + (h + 1) * P)
+                first = h * xm_width + b % 2 * P
+                cols = slice(first, first + P)
                 nc.tensor.matmul_mx(
                     out=dw[b][:], lhsT=codes[:, cols].bitcast(E4M3), lhsT_scale=scales[:, cols],
                     rhs=g_op[h][1][:].bitcast(E5M2), rhs_scale=g_op[h][2][:],
@@ -243,20 +239,19 @@ def tile_attend_gsq_nag_kernel(tc, xT, wT, y, wt, xm, mT, offs, out_0, out_1):
         dw_sb = keep.tile([P, BLOCKS, N], F32, name="dw_sb", tag="y0")
         dw_term = keep.tile([P, BLOCKS, N], F32, name="dw_term", tag="y1")
         m_dst = [keep.tile([P, T], F32, name="m_dst%d" % b, tag=tag, align_bytes=64)
-                 for b, tag in enumerate(("table0", "shared0", "rest0", "shared1"))]
+                 for b, tag in enumerate(("table0", "shared0", "rest1", "shared1"))]
 
         def load_tail(dst, table, b=0):
             nc.sync.dma_start(out=dst[:, COPIED:], in_=block(table, b)[:, COPIED:])
 
         load_m(1)
-        load_xm(xm_mid, 1, 2)
+        nc.sync.dma_start(out=m_dst[0][:, M0_COPIED:], in_=block(mT, 0)[:, M0_COPIED:])
         load_m(2)
         load_tail(w_dst[0], wT)
-        nc.sync.dma_start(out=m_dst[1][:], in_=block(mT, 1))
         load_xm(xm_last, 2, 4)
-        load_m(3)
+        nc.sync.dma_start(out=m_dst[1][:], in_=block(mT, 1))
         load_tail(w_dst[1], wT, 1)
-        w_dst.append(keep.tile([P, T], F32, name="w_dst2", tag="rest1", align_bytes=64))
+        load_m(3)
 
         def gather_m(b):
             nc.vector.tensor_scalar(m_cols[:, b, :], m_src[b][:].indirect(offsets[:]), BETA, 0.0, MULT, ADD)
@@ -292,8 +287,9 @@ def tile_attend_gsq_nag_kernel(tc, xT, wT, y, wt, xm, mT, offs, out_0, out_1):
                     out=sums[c][:], lhsT=values[:, c * P : (c + 1) * P], rhs=ident[:], start=start, stop=stop, is_transpose=True)
 
         gradient(0)
+        gradient(1)
         gather_m(0)
-        fill(m_dst[0], m_src[0])
+        nc.scalar.activation(m_dst[0][:, :M0_COPIED], m_src[0][:, :M0_COPIED], COPY)
         nc.scalar.copy(dw_sb[:, 0, :], dw[0][:])
         gather_m(1)
         nc.vector.tensor_tensor(m_dst[0][:].indirect(offsets[:]), m_cols[:, 0, :], dw_sb[:, 0, :], ADD)
@@ -302,39 +298,35 @@ def tile_attend_gsq_nag_kernel(tc, xT, wT, y, wt, xm, mT, offs, out_0, out_1):
         add_turned(w0_scaled[:], True, False)
         add_turned(dw_sb[:, 0, :], False, False)
         add_turned(m_term[0][:], False, True)
-        weave_xm(1, (0,))
         w0_turned = keep.tile([P, CHUNKS, P], F32, name="w0_turned", tag="mid0", align_bytes=64)
         for c in range(CHUNKS):
             nc.scalar.copy(w0_turned[:, c, :], sums[c][:])
-        weave_xm(1, (1,))
-        quantise(xm_op1, E4M3, slice(0, xm_width))
-        w0_back = psum.tile([P, CHUNKS, P], F32, name="w0_back", tag="bank1")
+        w0_back = psum.tile([P, CHUNKS, P], F32, name="w0_back", tag="bank3")
         for c in range(CHUNKS):
             nc.tensor.transpose(w0_back[:, c, :], w0_turned[:, c, :], ident[:])
         new_w0 = keep.tile([P, N], F32, name="new_w0")
         nc.scalar.activation(new_w0[:], w0_back[:].rearrange("p c s -> p (c s)"), COPY, scale=DW_FACTOR)
-        for b, bank in ((1, 7), (2, 2), (3, 3)):
-            dw.append(psum.tile([P, N], F32, name="dw%d" % b, tag="bank%d" % bank))
-        gradient(1)
+        dw.append(psum.tile([P, N], F32, name="dw3", tag="bank3"))
         gather_m(2)
         finish_w(0, new_w0[:])
 
-        for b, tag in ((1, "mid0"), (2, "m_term2"), (3, "m_term3")):
+        for b, tag in ((1, "mid0"), (2, "rest0"), (3, "m_term3")):
             m_term.append(keep.tile([P, N], F32, name="m_term%d" % b, tag=tag, align_bytes=64))
         update_m(1)
-        finish_m(1)
         add_dw_term(1, w_cols[:, 1, :])
-        add_m_term(1, w_cols[:, 1, :])
-        xm_op23 = operand("xm23", 2 * xm_width)
-        xm_place.extend([(xm_op23, 0), (xm_op23, xm_width)])
+        xm_ops.append(operand("xm23", HALVES * xm_width))
+        weave_xm(1)
+        for h in range(HALVES):
+            quantise(xm_ops[1], E4M3, slice(h * xm_width, (h + 1) * xm_width))
         for b in (2, 3):
-            weave_xm(b)
-        for b in (2, 3):
-            quantise(xm_op23, E4M3, slice(xm_place[b][1], xm_place[b][1] + xm_width))
             gradient(b)
-        w_dst.append(keep.tile([P, T], F32, name="w_dst3", tag="xm23_grouped", align_bytes=64))
+        finish_m(1)
+        new_w1 = keep.tile([P, N], F32, name="new_w1", tag="xm23_grouped", align_bytes=64)
+        add_m_term(1, new_w1[:])
         gather_m(3)
-        finish_w(1, w_cols[:, 1, :])
+        finish_w(1, new_w1[:])
+        w_dst.append(keep.tile([P, T], F32, name="w_dst2", tag="mid0", align_bytes=64))
+        w_dst.append(keep.tile([P, T], F32, name="w_dst3", tag="xm23_grouped", align_bytes=64))
 
         update_m(2)
         fill(m_dst[2], m_src[2])

@@ -173,8 +173,12 @@ def tile_attend_gsq_nag_kernel(tc, xT, wT, y, wt, xm, mT, offs, out_0, out_1):
         copy_back(nc.vector.tensor_copy, 1, backs[1])
         for half, part in enumerate(slot_halves):
             nc.vector.quantize_mx(out=w_codes[:, part].bitcast(E4M3), scales=w_scales[:, part], in_=w_grouped[half])
-        weave_x(1)
-        quantise(x_op[1], E4M3, slice(0, K))
+        dst = x_op[1][0][:].rearrange("p (t m j) -> p m j t", t=PACK, j=PACK)
+        src = x_raw[1][:].rearrange("p j (m t) -> p m j t", t=PACK)
+        nc.scalar.copy(out=dst[:, :, :, :2], in_=src[:, :, :, :2])
+        nc.vector.tensor_copy(out=dst[:, :, :, 2:], in_=src[:, :, :, 2:])
+        for part in slot_halves[::1]:
+            quantise(x_op[1], E4M3, part)
 
         def weigh_y(h, on_scalar):
             for t in range(PACK):
@@ -193,7 +197,7 @@ def tile_attend_gsq_nag_kernel(tc, xT, wT, y, wt, xm, mT, offs, out_0, out_1):
                     out=a[:], lhsT=codes[:, cols].bitcast(E4M3), lhsT_scale=scales[:, cols],
                     rhs=w_codes[:].bitcast(E4M3), rhs_scale=w_scales[:], start=True, stop=True,
                 )
-                last = h == HALVES - 1 and t == PACK - 1
+                last = t == PACK - 1
                 for part in (slot_halves if last else (slice(0, N),)):
                     nc.vector.scalar_tensor_tensor(
                         out=y_sb[h][:, t, part], in0=a[:, part], scalar=wt_sb[h][:, t : t + 1], in1=y_sb[h][:, t, part],
@@ -209,8 +213,9 @@ def tile_attend_gsq_nag_kernel(tc, xT, wT, y, wt, xm, mT, offs, out_0, out_1):
         weigh_y(0, PACK)
         residual(0)
         weigh_y(1, Y1_ON_SCALAR)
-        dst, src = weave_views(g_op[0][0][:], y_sb[0][:])
-        nc.scalar.copy(out=dst, in_=src)
+        for part in slot_halves:
+            dst, src = weave_views(g_op[0][0][:, PACK * part.start : PACK * part.stop], y_sb[0][:, :, part])
+            nc.scalar.copy(out=dst, in_=src)
         weave_xm(0)
         residual(1)
         for part in slot_halves:

@@ -6,6 +6,7 @@ from concourse.masks import make_identity
 D, T, N, R = 512, 2048, 512, 1024
 LR, BETA = 0.1, 0.9
 DW_FACTOR = -LR * (1.0 + BETA)
+M_FACTOR = -LR * BETA
 FLOPS = 2 * 2 * D * N * R
 
 F32 = mybir.dt.float32
@@ -27,13 +28,13 @@ HALVES = R // K
 BLOCKS = D // P
 CHUNKS = N // P
 SPAN = P // PACK
+XM_COLS = 2 * P
 BAND = 16
 
-X_ON_SCALAR = (32, 64)
+X0_ON_SCALAR = 32
 Y1_ON_SCALAR = 2
-COPIED = 1792
+W_COPIED = 1792
 M0_COPIED = 1536
-M1_FIRST = 1536
 
 
 def tile_attend_gsq_nag_kernel(tc, xT, wT, y, wt, xm, mT, offs, out_0, out_1):
@@ -44,6 +45,8 @@ def tile_attend_gsq_nag_kernel(tc, xT, wT, y, wt, xm, mT, offs, out_0, out_1):
         psum = ctx.enter_context(tc.psum_pool(name="psum", bufs=1))
 
         slot_halves = (slice(0, N // 2), slice(N // 2, N))
+        column_halves = (slice(0, K // 2), slice(K // 2, K))
+        row_pairs = (slice(0, PACK // 2), slice(PACK // 2, PACK))
 
         def block(table, b):
             return table[b * P : (b + 1) * P, :]
@@ -51,10 +54,10 @@ def tile_attend_gsq_nag_kernel(tc, xT, wT, y, wt, xm, mT, offs, out_0, out_1):
         def rows(src):
             return src.rearrange("(p j) c -> p j c", j=PACK)
 
-        def operand(name, width=K, codes_tag=None, scales_tag=None):
-            grouped = keep.tile([P, width * PACK], BF16, name=name + "_grouped", align_bytes=64)
-            codes = keep.tile([P, width], U32, name=name + "_codes", tag=codes_tag or name + "_codes", align_bytes=64)
-            scales = keep.tile([P, width], U8, name=name + "_scales", tag=scales_tag or name + "_scales", align_bytes=64)
+        def operand(name, scales_tag=None):
+            grouped = keep.tile([P, K * PACK], BF16, name=name + "_grouped", align_bytes=64)
+            codes = keep.tile([P, K], U32, name=name + "_codes", align_bytes=64)
+            scales = keep.tile([P, K], U8, name=name + "_scales", tag=scales_tag or name + "_scales", align_bytes=64)
             return grouped, codes, scales
 
         def quantise(op, fmt, cols):
@@ -71,8 +74,8 @@ def tile_attend_gsq_nag_kernel(tc, xT, wT, y, wt, xm, mT, offs, out_0, out_1):
         offsets = lists.tile([P, N // BAND], U16, name="offsets")
         x_raw = [keep.tile([P, PACK, K], F32, name="x_raw%d" % h, tag="shared%d" % h, align_bytes=64) for h in range(HALVES)]
         y_sb = [keep.tile([P, PACK, N], F32, name="y_sb%d" % h, tag="y%d" % h) for h in range(HALVES)]
-        xm_first = [keep.tile([P, PACK, 2 * P], F32, name="xm_first%d" % h) for h in range(HALVES)]
-        xm_last = [keep.tile([P, PACK, 2 * P], F32, name="xm_last%d" % h, tag="rest%d" % h, align_bytes=64) for h in range(HALVES)]
+        xm_first = [keep.tile([P, PACK, XM_COLS], F32, name="xm_first%d" % h) for h in range(HALVES)]
+        xm_last = [keep.tile([P, PACK, XM_COLS], F32, name="xm_last%d" % h, tag="rest%d" % h, align_bytes=64) for h in range(HALVES)]
         w_src = [keep.tile([P, T], F32, name="w_src%d" % b, tag="table%d" % b, align_bytes=64) for b in range(BLOCKS)]
         m_src = [keep.tile([P, T], F32, name="m_src%d" % b) for b in range(BLOCKS)]
         wt_rows = keep.tile([P, K], F32, name="wt_rows")
@@ -81,9 +84,9 @@ def tile_attend_gsq_nag_kernel(tc, xT, wT, y, wt, xm, mT, offs, out_0, out_1):
         ident = keep.tile([P, P], F32, name="ident")
         make_identity(nc, ident[:])
 
-        def load_xm(tiles, first, last):
+        def load_xm(tiles, first):
             for h in range(HALVES):
-                nc.sync.dma_start(out=tiles[h][:], in_=rows(xm[0, h * K : (h + 1) * K, first * P : last * P]))
+                nc.sync.dma_start(out=tiles[h][:], in_=rows(xm[0, h * K : (h + 1) * K, first : first + XM_COLS]))
 
         def load_m(b):
             nc.sync.dma_start(out=m_src[b][:], in_=block(mT, b))
@@ -97,17 +100,17 @@ def tile_attend_gsq_nag_kernel(tc, xT, wT, y, wt, xm, mT, offs, out_0, out_1):
         for h in range(HALVES):
             nc.sync.dma_start(out=x_raw[h][:], in_=rows(xT[0, :, h * K : (h + 1) * K]))
         for h in range(HALVES):
-            for pair in (slice(0, PACK // 2), slice(PACK // 2, PACK)):
-                nc.sync.dma_start(out=y_sb[h][:, pair, :], in_=rows(y[0, h * K : (h + 1) * K, :])[:, pair, :])
-        load_xm(xm_first, 0, 2)
+            for two_rows in row_pairs:
+                nc.sync.dma_start(out=y_sb[h][:, two_rows, :], in_=rows(y[0, h * K : (h + 1) * K, :])[:, two_rows, :])
+        load_xm(xm_first, 0)
         load_m(0)
 
         w_cols = keep.tile([P, BLOCKS, N], F32, name="w_cols")
         w_dst = [keep.tile([P, T], F32, name="w_dst%d" % b) for b in range(2)]
         w_turned = [keep.tile([P, 2, 2, P, 2], BF16, name="w_turned%d" % i, align_bytes=64) for i in range(CHUNKS // 2)]
 
-        def fill(dst, src, first=0, cut=T // 2, last=T):
-            for part in (slice(first, cut), slice(cut, last)):
+        def fill(dst, src, last=T):
+            for part in (slice(0, T // 2), slice(T // 2, last)):
                 nc.scalar.activation(dst[:, part], src[:, part], COPY)
 
         x_op = [operand("x%d" % h) for h in range(HALVES)]
@@ -116,8 +119,7 @@ def tile_attend_gsq_nag_kernel(tc, xT, wT, y, wt, xm, mT, offs, out_0, out_1):
         w_codes = keep.tile([P, N], U32, name="w_codes", align_bytes=64)
         w_scales = keep.tile([P, N], U8, name="w_scales", align_bytes=64)
         g_op = [operand("g0", scales_tag="wt1"), operand("g1")]
-        xm_width = HALVES * P
-        xm_ops = [operand("xm01", HALVES * xm_width)]
+        xm_ops = [operand("xm01")]
 
         def turn(b, chunks):
             slots = slice(chunks[0] * P, (chunks[-1] + 1) * P)
@@ -145,17 +147,15 @@ def tile_attend_gsq_nag_kernel(tc, xT, wT, y, wt, xm, mT, offs, out_0, out_1):
             dst = w_grouped[half].bitcast(F32).rearrange("p (c s u) -> p c s u", c=2, u=2)
             copy(out=dst, in_=back[:].rearrange("p c u s -> p c s u"))
 
-        def weave_x(h):
+        def x_views(h):
             dst = x_op[h][0][:].rearrange("p (t m j) -> p m j t", t=PACK, j=PACK)
             src = x_raw[h][:].rearrange("p j (m t) -> p m j t", t=PACK)
-            cut = X_ON_SCALAR[h]
-            nc.scalar.copy(out=dst[:, :cut], in_=src[:, :cut])
-            nc.vector.tensor_copy(out=dst[:, cut:], in_=src[:, cut:])
+            return dst, src
 
         every_chunk = tuple(range(CHUNKS))
-        fill(w_dst[0], w_src[0], last=COPIED)
+        fill(w_dst[0], w_src[0], last=W_COPIED)
         turn(0, every_chunk)
-        fill(w_dst[1], w_src[1], last=COPIED)
+        fill(w_dst[1], w_src[1], last=W_COPIED)
         turn(1, every_chunk)
         wt_turned = psum.tile([P, PACK, P], F32, name="wt_turned", tag="bank7")
         for t in range(PACK):
@@ -167,18 +167,19 @@ def tile_attend_gsq_nag_kernel(tc, xT, wT, y, wt, xm, mT, offs, out_0, out_1):
         turn(3, every_chunk[: CHUNKS // 2])
         turn(3, every_chunk[CHUNKS // 2 :])
         backs = [turn_back(half) for half in range(2)]
-        weave_x(0)
+        dst, src = x_views(0)
+        nc.scalar.copy(out=dst[:, :X0_ON_SCALAR], in_=src[:, :X0_ON_SCALAR])
+        nc.vector.tensor_copy(out=dst[:, X0_ON_SCALAR:], in_=src[:, X0_ON_SCALAR:])
         quantise(x_op[0], E4M3, slice(0, K))
         copy_back(nc.scalar.copy, 0, backs[0])
         copy_back(nc.vector.tensor_copy, 1, backs[1])
         for half, part in enumerate(slot_halves):
             nc.vector.quantize_mx(out=w_codes[:, part].bitcast(E4M3), scales=w_scales[:, part], in_=w_grouped[half])
-        dst = x_op[1][0][:].rearrange("p (t m j) -> p m j t", t=PACK, j=PACK)
-        src = x_raw[1][:].rearrange("p j (m t) -> p m j t", t=PACK)
-        nc.scalar.copy(out=dst[:, :, :, :2], in_=src[:, :, :, :2])
-        nc.vector.tensor_copy(out=dst[:, :, :, 2:], in_=src[:, :, :, 2:])
-        for part in slot_halves[::1]:
-            quantise(x_op[1], E4M3, part)
+        dst, src = x_views(1)
+        nc.scalar.copy(out=dst[:, :, :, row_pairs[0]], in_=src[:, :, :, row_pairs[0]])
+        nc.vector.tensor_copy(out=dst[:, :, :, row_pairs[1]], in_=src[:, :, :, row_pairs[1]])
+        for cols in column_halves:
+            quantise(x_op[1], E4M3, cols)
 
         def weigh_y(h, on_scalar):
             for t in range(PACK):
@@ -197,40 +198,39 @@ def tile_attend_gsq_nag_kernel(tc, xT, wT, y, wt, xm, mT, offs, out_0, out_1):
                     out=a[:], lhsT=codes[:, cols].bitcast(E4M3), lhsT_scale=scales[:, cols],
                     rhs=w_codes[:].bitcast(E4M3), rhs_scale=w_scales[:], start=True, stop=True,
                 )
-                last = t == PACK - 1
-                for part in (slot_halves if last else (slice(0, N),)):
+                for part in (slot_halves if t == PACK - 1 else (slice(0, N),)):
                     nc.vector.scalar_tensor_tensor(
                         out=y_sb[h][:, t, part], in0=a[:, part], scalar=wt_sb[h][:, t : t + 1], in1=y_sb[h][:, t, part],
                         op0=MULT, op1=SUB,
                     )
 
-        def weave_xm(pair):
-            for h in range(HALVES):
-                lo = PACK * h * xm_width
-                dst, src = weave_views(xm_ops[pair][0][:, lo : lo + PACK * xm_width], (xm_first, xm_last)[pair][h][:])
+        def weave_g(copy, h):
+            for part in slot_halves:
+                dst, src = weave_views(g_op[h][0][:, PACK * part.start : PACK * part.stop], y_sb[h][:, :, part])
+                copy(out=dst, in_=src)
+
+        def weave_xm(op, tiles):
+            for h, cols in enumerate(column_halves):
+                dst, src = weave_views(op[0][:, PACK * cols.start : PACK * cols.stop], tiles[h][:])
                 nc.scalar.copy(out=dst, in_=src)
 
         weigh_y(0, PACK)
         residual(0)
         weigh_y(1, Y1_ON_SCALAR)
-        for part in slot_halves:
-            dst, src = weave_views(g_op[0][0][:, PACK * part.start : PACK * part.stop], y_sb[0][:, :, part])
-            nc.scalar.copy(out=dst, in_=src)
-        weave_xm(0)
+        weave_g(nc.scalar.copy, 0)
+        weave_xm(xm_ops[0], xm_first)
         residual(1)
-        for part in slot_halves:
-            dst, src = weave_views(g_op[1][0][:, PACK * part.start : PACK * part.stop], y_sb[1][:, :, part])
-            nc.vector.tensor_copy(out=dst, in_=src)
+        weave_g(nc.vector.tensor_copy, 1)
         for h in range(HALVES):
             quantise(g_op[h], E5M2, slice(0, N))
-            quantise(xm_ops[0], E4M3, slice(h * xm_width, (h + 1) * xm_width))
+            quantise(xm_ops[0], E4M3, column_halves[h])
 
         dw = [psum.tile([P, N], F32, name="dw%d" % b, tag="bank%d" % b) for b in range(BLOCKS - 1)]
 
         def gradient(b):
             codes, scales = xm_ops[b // 2][1:]
             for h in range(HALVES):
-                first = h * xm_width + b % 2 * P
+                first = h * XM_COLS + b % 2 * P
                 cols = slice(first, first + P)
                 nc.tensor.matmul_mx(
                     out=dw[b][:], lhsT=codes[:, cols].bitcast(E4M3), lhsT_scale=scales[:, cols],
@@ -239,23 +239,23 @@ def tile_attend_gsq_nag_kernel(tc, xT, wT, y, wt, xm, mT, offs, out_0, out_1):
                 )
 
         m_cols = keep.tile([P, BLOCKS, N], F32, name="m_cols")
-        new_m = [None] + [keep.tile([P, N], F32, name="new_m%d" % b, align_bytes=64) for b in range(1, BLOCKS)]
+        new_m = {b: keep.tile([P, N], F32, name="new_m%d" % b, align_bytes=64) for b in range(1, BLOCKS)}
         m_term = [keep.tile([P, N], F32, name="m_term0")]
         dw_sb = keep.tile([P, BLOCKS, N], F32, name="dw_sb", tag="y0")
         dw_term = keep.tile([P, BLOCKS, N], F32, name="dw_term", tag="y1")
         m_dst = [keep.tile([P, T], F32, name="m_dst%d" % b, tag=tag, align_bytes=64)
                  for b, tag in enumerate(("table0", "shared0", "rest1", "shared1"))]
 
-        def load_tail(dst, table, b=0):
-            nc.sync.dma_start(out=dst[:, COPIED:], in_=block(table, b)[:, COPIED:])
+        def load_columns(dst, table, b, first):
+            nc.sync.dma_start(out=dst[b][:, first:], in_=block(table, b)[:, first:])
 
         load_m(1)
-        nc.sync.dma_start(out=m_dst[0][:, M0_COPIED:], in_=block(mT, 0)[:, M0_COPIED:])
+        load_columns(m_dst, mT, 0, M0_COPIED)
         load_m(2)
-        load_tail(w_dst[0], wT)
-        load_xm(xm_last, 2, 4)
-        nc.sync.dma_start(out=m_dst[1][:], in_=block(mT, 1))
-        load_tail(w_dst[1], wT, 1)
+        load_columns(w_dst, wT, 0, W_COPIED)
+        load_xm(xm_last, XM_COLS)
+        load_columns(m_dst, mT, 1, 0)
+        load_columns(w_dst, wT, 1, W_COPIED)
         load_m(3)
 
         def gather_m(b):
@@ -266,11 +266,11 @@ def tile_attend_gsq_nag_kernel(tc, xT, wT, y, wt, xm, mT, offs, out_0, out_1):
             nc.gpsimd.tensor_tensor(new_m[b][:], m_cols[:, b, :], dw_sb[:, b, :], ADD)
 
         def add_dw_term(b, total):
-            nc.scalar.activation(dw_term[:, b, :], dw[b][:], COPY, scale=-LR * (1.0 + BETA))
+            nc.scalar.activation(dw_term[:, b, :], dw[b][:], COPY, scale=DW_FACTOR)
             nc.gpsimd.tensor_tensor(total, w_cols[:, b, :], dw_term[:, b, :], ADD)
 
         def add_m_term(b, total):
-            nc.scalar.activation(m_term[b][:], m_cols[:, b, :], COPY, scale=-LR * BETA)
+            nc.scalar.activation(m_term[b][:], m_cols[:, b, :], COPY, scale=M_FACTOR)
             nc.gpsimd.tensor_tensor(total, w_cols[:, b, :], m_term[b][:], ADD)
 
         def scatter(dst, values):
@@ -319,10 +319,10 @@ def tile_attend_gsq_nag_kernel(tc, xT, wT, y, wt, xm, mT, offs, out_0, out_1):
             m_term.append(keep.tile([P, N], F32, name="m_term%d" % b, tag=tag, align_bytes=64))
         update_m(1)
         add_dw_term(1, w_cols[:, 1, :])
-        xm_ops.append(operand("xm23", HALVES * xm_width))
-        weave_xm(1)
-        for h in range(HALVES):
-            quantise(xm_ops[1], E4M3, slice(h * xm_width, (h + 1) * xm_width))
+        xm_ops.append(operand("xm23"))
+        weave_xm(xm_ops[1], xm_last)
+        for cols in column_halves:
+            quantise(xm_ops[1], E4M3, cols)
         for b in (2, 3):
             gradient(b)
         finish_m(1)
@@ -347,6 +347,4 @@ def tile_attend_gsq_nag_kernel(tc, xT, wT, y, wt, xm, mT, offs, out_0, out_1):
         add_dw_term(3, w_cols[:, 3, :])
         add_m_term(3, w_cols[:, 3, :])
         fill(w_dst[3], w_src[3])
-        scatter(w_dst[3], w_cols[:, 3, :])
-        nc.sync.dma_start(out=block(out_0, 3)[:, : T // 2], in_=w_dst[3][:, : T // 2])
-        nc.scalar.dma_start(out=block(out_0, 3)[:, T // 2 :], in_=w_dst[3][:, T // 2 :])
+        finish_w(3, w_cols[:, 3, :])

@@ -32,7 +32,7 @@ XM_COLS = 2 * P
 BAND = 16
 
 X0_ON_SCALAR = 32
-Y1_ON_SCALAR = 2
+X1_ON_SCALAR = 80
 W_COPIED = 1792
 M0_COPIED = 1536
 
@@ -172,18 +172,19 @@ def tile_attend_gsq_nag_kernel(tc, xT, wT, y, wt, xm, mT, offs, out_0, out_1):
         nc.vector.tensor_copy(out=dst[:, X0_ON_SCALAR:], in_=src[:, X0_ON_SCALAR:])
         quantise(x_op[0], E4M3, slice(0, K))
         copy_back(nc.scalar.copy, 0, backs[0])
-        copy_back(nc.vector.tensor_copy, 1, backs[1])
+        copy_back(nc.scalar.copy, 1, backs[1])
         for half, part in enumerate(slot_halves):
             nc.vector.quantize_mx(out=w_codes[:, part].bitcast(E4M3), scales=w_scales[:, part], in_=w_grouped[half])
         dst, src = x_views(1)
-        nc.scalar.copy(out=dst[:, :, :, row_pairs[0]], in_=src[:, :, :, row_pairs[0]])
+        nc.scalar.copy(out=dst[:, :X1_ON_SCALAR, :, row_pairs[0]], in_=src[:, :X1_ON_SCALAR, :, row_pairs[0]])
+        nc.vector.tensor_copy(out=dst[:, X1_ON_SCALAR:, :, row_pairs[0]], in_=src[:, X1_ON_SCALAR:, :, row_pairs[0]])
         nc.vector.tensor_copy(out=dst[:, :, :, row_pairs[1]], in_=src[:, :, :, row_pairs[1]])
         for cols in column_halves:
             quantise(x_op[1], E4M3, cols)
 
         def weigh_y(h, on_scalar):
             for t in range(PACK):
-                if t < on_scalar:
+                if t in on_scalar:
                     nc.scalar.activation(y_sb[h][:, t, :], y_sb[h][:, t, :], COPY, scale=wt_sb[h][:, t : t + 1])
                 else:
                     nc.gpsimd.tensor_scalar(
@@ -214,9 +215,9 @@ def tile_attend_gsq_nag_kernel(tc, xT, wT, y, wt, xm, mT, offs, out_0, out_1):
                 dst, src = weave_views(op[0][:, PACK * cols.start : PACK * cols.stop], tiles[h][:])
                 nc.scalar.copy(out=dst, in_=src)
 
-        weigh_y(0, PACK)
+        weigh_y(0, (0, 1, 3))
         residual(0)
-        weigh_y(1, Y1_ON_SCALAR)
+        weigh_y(1, (0, 1))
         weave_g(nc.scalar.copy, 0)
         weave_xm(xm_ops[0], xm_first)
         residual(1)

@@ -35,6 +35,7 @@ X0_ON_SCALAR = 32
 X1_ON_SCALAR = 80
 W_COPIED = 1792
 M0_COPIED = 1536
+G1_ON_VECTOR = 384
 
 
 def tile_attend_gsq_nag_kernel(tc, xT, wT, y, wt, xm, mT, offs, out_0, out_1):
@@ -190,8 +191,9 @@ def tile_attend_gsq_nag_kernel(tc, xT, wT, y, wt, xm, mT, offs, out_0, out_1):
                     nc.gpsimd.tensor_scalar(
                         y_sb[h][:, t, :], y_sb[h][:, t, :], wt_sb[h][:, t : t + 1], 0.0, MULT, ADD)
 
-        def residual(h):
+        def residual(h, whole):
             codes, scales = x_op[h][1:]
+            banks = []
             for t in range(PACK):
                 cols = slice(t * P, (t + 1) * P)
                 a = psum.tile([P, N], F32, name="a%d%d" % (h, t), tag="bank%d" % (PACK * h + t))
@@ -199,14 +201,17 @@ def tile_attend_gsq_nag_kernel(tc, xT, wT, y, wt, xm, mT, offs, out_0, out_1):
                     out=a[:], lhsT=codes[:, cols].bitcast(E4M3), lhsT_scale=scales[:, cols],
                     rhs=w_codes[:].bitcast(E4M3), rhs_scale=w_scales[:], start=True, stop=True,
                 )
-                for part in (slot_halves if t == PACK - 1 else (slice(0, N),)):
-                    nc.vector.scalar_tensor_tensor(
-                        out=y_sb[h][:, t, part], in0=a[:, part], scalar=wt_sb[h][:, t : t + 1], in1=y_sb[h][:, t, part],
-                        op0=MULT, op1=SUB,
-                    )
+                banks.append(a)
+            steps = [(t, slice(0, N)) for t in range(whole)]
+            steps.extend((t, part) for part in slot_halves for t in range(whole, PACK))
+            for t, part in steps:
+                nc.vector.scalar_tensor_tensor(
+                    out=y_sb[h][:, t, part], in0=banks[t][:, part], scalar=wt_sb[h][:, t : t + 1],
+                    in1=y_sb[h][:, t, part], op0=MULT, op1=SUB,
+                )
 
-        def weave_g(copy, h):
-            for part in slot_halves:
+        def weave_g(copy, h, parts):
+            for part in parts:
                 dst, src = weave_views(g_op[h][0][:, PACK * part.start : PACK * part.stop], y_sb[h][:, :, part])
                 copy(out=dst, in_=src)
 
@@ -216,12 +221,13 @@ def tile_attend_gsq_nag_kernel(tc, xT, wT, y, wt, xm, mT, offs, out_0, out_1):
                 nc.scalar.copy(out=dst, in_=src)
 
         weigh_y(0, (0, 1, 3))
-        residual(0)
-        weigh_y(1, (0, 1))
-        weave_g(nc.scalar.copy, 0)
+        residual(0, whole=2)
+        weigh_y(1, (1,))
+        weave_g(nc.scalar.copy, 0, slot_halves)
+        residual(1, whole=3)
+        weave_g(nc.vector.tensor_copy, 1, (slot_halves[0], slice(N // 2, G1_ON_VECTOR)))
+        weave_g(nc.scalar.copy, 1, (slice(G1_ON_VECTOR, N),))
         weave_xm(xm_ops[0], xm_first)
-        residual(1)
-        weave_g(nc.vector.tensor_copy, 1)
         for h in range(HALVES):
             quantise(g_op[h], E5M2, slice(0, N))
             quantise(xm_ops[0], E4M3, column_halves[h])

@@ -75,7 +75,8 @@ def tile_attend_gsq_nag_kernel(tc, xT, wT, y, wt, xm, mT, offs, out_0, out_1):
         offsets = lists.tile([P, N // BAND], U16, name="offsets")
         x_raw = [keep.tile([P, PACK, K], F32, name="x_raw%d" % h, tag="shared%d" % h, align_bytes=64) for h in range(HALVES)]
         y_sb = [keep.tile([P, PACK, N], F32, name="y_sb%d" % h, tag="y%d" % h) for h in range(HALVES)]
-        xm_first = [keep.tile([P, PACK, XM_COLS], F32, name="xm_first%d" % h) for h in range(HALVES)]
+        xm_first = keep.tile([P, PACK, XM_COLS], F32, name="xm_first")
+        xm_second = [keep.tile([P, PACK, P], F32, name="xm_second%d" % b) for b in range(2)]
         xm_last = [keep.tile([P, PACK, XM_COLS], F32, name="xm_last%d" % h, tag="rest%d" % h, align_bytes=64) for h in range(HALVES)]
         w_src = [keep.tile([P, T], F32, name="w_src%d" % b, tag="table%d" % b, align_bytes=64) for b in range(BLOCKS)]
         m_src = [keep.tile([P, T], F32, name="m_src%d" % b) for b in range(BLOCKS)]
@@ -103,7 +104,8 @@ def tile_attend_gsq_nag_kernel(tc, xT, wT, y, wt, xm, mT, offs, out_0, out_1):
         for h in range(HALVES):
             for two_rows in row_pairs:
                 nc.sync.dma_start(out=y_sb[h][:, two_rows, :], in_=rows(y[0, h * K : (h + 1) * K, :])[:, two_rows, :])
-        load_xm(xm_first, 0)
+        nc.sync.dma_start(out=xm_first[:], in_=rows(xm[0, :K, :XM_COLS]))
+        nc.sync.dma_start(out=xm_second[0][:], in_=rows(xm[0, K:, :P]))
         load_m(0)
 
         w_cols = keep.tile([P, BLOCKS, N], F32, name="w_cols")
@@ -154,7 +156,7 @@ def tile_attend_gsq_nag_kernel(tc, xT, wT, y, wt, xm, mT, offs, out_0, out_1):
             return dst, src
 
         every_chunk = tuple(range(CHUNKS))
-        fill(w_dst[0], w_src[0], last=W_COPIED)
+        fill(w_dst[0], w_src[0])
         turn(0, every_chunk)
         fill(w_dst[1], w_src[1], last=W_COPIED)
         turn(1, every_chunk)
@@ -215,10 +217,11 @@ def tile_attend_gsq_nag_kernel(tc, xT, wT, y, wt, xm, mT, offs, out_0, out_1):
                 dst, src = weave_views(g_op[h][0][:, PACK * part.start : PACK * part.stop], y_sb[h][:, :, part])
                 copy(out=dst, in_=src)
 
-        def weave_xm(op, tiles):
-            for h, cols in enumerate(column_halves):
-                dst, src = weave_views(op[0][:, PACK * cols.start : PACK * cols.stop], tiles[h][:])
-                nc.scalar.copy(out=dst, in_=src)
+        def weave_xm(op, cols, tile):
+            dst, src = weave_views(op[0][:, PACK * cols.start : PACK * cols.stop], tile[:])
+            nc.scalar.copy(out=dst, in_=src)
+
+        second = [slice(XM_COLS + b * P, XM_COLS + (b + 1) * P) for b in range(2)]
 
         weigh_y(0, (0, 1, 3))
         residual(0, whole=2)
@@ -227,10 +230,11 @@ def tile_attend_gsq_nag_kernel(tc, xT, wT, y, wt, xm, mT, offs, out_0, out_1):
         residual(1, whole=3)
         weave_g(nc.vector.tensor_copy, 1, (slot_halves[0], slice(N // 2, G1_ON_VECTOR)))
         weave_g(nc.scalar.copy, 1, (slice(G1_ON_VECTOR, N),))
-        weave_xm(xm_ops[0], xm_first)
+        weave_xm(xm_ops[0], column_halves[0], xm_first)
+        weave_xm(xm_ops[0], second[0], xm_second[0])
         for h in range(HALVES):
             quantise(g_op[h], E5M2, slice(0, N))
-            quantise(xm_ops[0], E4M3, column_halves[h])
+            quantise(xm_ops[0], E4M3, (column_halves[0], second[0])[h])
 
         dw = [psum.tile([P, N], F32, name="dw%d" % b, tag="bank%d" % b) for b in range(BLOCKS - 1)]
 
@@ -258,8 +262,8 @@ def tile_attend_gsq_nag_kernel(tc, xT, wT, y, wt, xm, mT, offs, out_0, out_1):
 
         load_m(1)
         load_columns(m_dst, mT, 0, M0_COPIED)
+        nc.sync.dma_start(out=xm_second[1][:], in_=rows(xm[0, K:, P:XM_COLS]))
         load_m(2)
-        load_columns(w_dst, wT, 0, W_COPIED)
         load_xm(xm_last, XM_COLS)
         load_columns(m_dst, mT, 1, 0)
         load_columns(w_dst, wT, 1, W_COPIED)
@@ -299,7 +303,6 @@ def tile_attend_gsq_nag_kernel(tc, xT, wT, y, wt, xm, mT, offs, out_0, out_1):
                     out=sums[c][:], lhsT=values[:, c * P : (c + 1) * P], rhs=ident[:], start=start, stop=stop, is_transpose=True)
 
         gradient(0)
-        gradient(1)
         gather_m(0)
         nc.scalar.activation(m_dst[0][:, :M0_COPIED], m_src[0][:, :M0_COPIED], COPY)
         nc.scalar.copy(dw_sb[:, 0, :], dw[0][:])
@@ -313,12 +316,15 @@ def tile_attend_gsq_nag_kernel(tc, xT, wT, y, wt, xm, mT, offs, out_0, out_1):
         w0_turned = keep.tile([P, CHUNKS, P], F32, name="w0_turned", tag="mid0", align_bytes=64)
         for c in range(CHUNKS):
             nc.scalar.copy(w0_turned[:, c, :], sums[c][:])
+        weave_xm(xm_ops[0], second[1], xm_second[1])
+        quantise(xm_ops[0], E4M3, second[1])
         w0_back = psum.tile([P, CHUNKS, P], F32, name="w0_back", tag="bank3")
         for c in range(CHUNKS):
             nc.tensor.transpose(w0_back[:, c, :], w0_turned[:, c, :], ident[:])
         new_w0 = keep.tile([P, N], F32, name="new_w0")
         nc.scalar.activation(new_w0[:], w0_back[:].rearrange("p c s -> p (c s)"), COPY, scale=DW_FACTOR)
         dw.append(psum.tile([P, N], F32, name="dw3", tag="bank3"))
+        gradient(1)
         gather_m(2)
         finish_w(0, new_w0[:])
 
@@ -327,7 +333,8 @@ def tile_attend_gsq_nag_kernel(tc, xT, wT, y, wt, xm, mT, offs, out_0, out_1):
         update_m(1)
         add_dw_term(1, w_cols[:, 1, :])
         xm_ops.append(operand("xm23"))
-        weave_xm(xm_ops[1], xm_last)
+        for h, cols in enumerate(column_halves):
+            weave_xm(xm_ops[1], cols, xm_last[h])
         for cols in column_halves:
             quantise(xm_ops[1], E4M3, cols)
         for b in (2, 3):

@@ -35,7 +35,7 @@ X0_ON_SCALAR = 32
 X1_ON_SCALAR = 80
 W_COPIED = 1792
 M0_COPIED = 1536
-G1_ON_VECTOR = 384
+G1_ON_VECTOR = 256
 
 
 def tile_attend_gsq_nag_kernel(tc, xT, wT, y, wt, xm, mT, offs, out_0, out_1):
@@ -55,10 +55,10 @@ def tile_attend_gsq_nag_kernel(tc, xT, wT, y, wt, xm, mT, offs, out_0, out_1):
         def rows(src):
             return src.rearrange("(p j) c -> p j c", j=PACK)
 
-        def operand(name, scales_tag=None):
-            grouped = keep.tile([P, K * PACK], BF16, name=name + "_grouped", align_bytes=64)
-            codes = keep.tile([P, K], U32, name=name + "_codes", align_bytes=64)
-            scales = keep.tile([P, K], U8, name=name + "_scales", tag=scales_tag or name + "_scales", align_bytes=64)
+        def operand(name, scales_tag=None, grouped_tag=None, columns=K):
+            grouped = keep.tile([P, columns * PACK], BF16, name=name + "_grouped", tag=grouped_tag or name + "_grouped", align_bytes=64)
+            codes = keep.tile([P, columns], U32, name=name + "_codes", align_bytes=64)
+            scales = keep.tile([P, columns], U8, name=name + "_scales", tag=scales_tag or name + "_scales", align_bytes=64)
             return grouped, codes, scales
 
         def quantise(op, fmt, cols):
@@ -117,12 +117,12 @@ def tile_attend_gsq_nag_kernel(tc, xT, wT, y, wt, xm, mT, offs, out_0, out_1):
                 nc.scalar.activation(dst[:, part], src[:, part], COPY)
 
         x_op = [operand("x%d" % h) for h in range(HALVES)]
-        w_whole = keep.tile([P, K * PACK], BF16, name="w_grouped", tag="shared0", align_bytes=64)
+        w_whole = keep.tile([P, K * PACK], BF16, name="w_grouped", align_bytes=64)
         w_grouped = [w_whole[:, PACK * part.start : PACK * part.stop] for part in slot_halves]
         w_codes = keep.tile([P, N], U32, name="w_codes", align_bytes=64)
         w_scales = keep.tile([P, N], U8, name="w_scales", align_bytes=64)
         g_op = [operand("g0", scales_tag="wt1"), operand("g1")]
-        xm_ops = [operand("xm01")]
+        xm_ops = [operand("xm0", columns=HALVES * P)]
 
         def turn(b, chunks):
             slots = slice(chunks[0] * P, (chunks[-1] + 1) * P)
@@ -217,31 +217,36 @@ def tile_attend_gsq_nag_kernel(tc, xT, wT, y, wt, xm, mT, offs, out_0, out_1):
                 dst, src = weave_views(g_op[h][0][:, PACK * part.start : PACK * part.stop], y_sb[h][:, :, part])
                 copy(out=dst, in_=src)
 
-        def weave_xm(op, cols, tile):
-            dst, src = weave_views(op[0][:, PACK * cols.start : PACK * cols.stop], tile[:])
-            nc.scalar.copy(out=dst, in_=src)
+        def gpsimd_round(out, in_):
+            nc.gpsimd.tensor_scalar(out, in_, 1.0, 0.0, MULT, ADD)
 
-        second = [slice(XM_COLS + b * P, XM_COLS + (b + 1) * P) for b in range(2)]
+        def weave_xm(op, cols, four_rows, copy=nc.scalar.copy):
+            dst, src = weave_views(op[0][:, PACK * cols.start : PACK * cols.stop], four_rows)
+            copy(out=dst, in_=src)
+
+        block_halves = (slice(0, P), slice(P, 2 * P))
 
         weigh_y(0, (0, 1, 3))
         residual(0, whole=2)
         weigh_y(1, (1,))
         weave_g(nc.scalar.copy, 0, slot_halves)
         residual(1, whole=3)
-        weave_g(nc.vector.tensor_copy, 1, (slot_halves[0], slice(N // 2, G1_ON_VECTOR)))
+        weave_g(nc.vector.tensor_copy, 1, (slice(0, G1_ON_VECTOR),))
+        weave_xm(xm_ops[0], block_halves[0], xm_first[:, :, :P], gpsimd_round)
+        weave_xm(xm_ops[0], block_halves[1], xm_second[0][:])
         weave_g(nc.scalar.copy, 1, (slice(G1_ON_VECTOR, N),))
-        weave_xm(xm_ops[0], column_halves[0], xm_first)
-        weave_xm(xm_ops[0], second[0], xm_second[0])
-        for h in range(HALVES):
-            quantise(g_op[h], E5M2, slice(0, N))
-            quantise(xm_ops[0], E4M3, (column_halves[0], second[0])[h])
+        quantise(g_op[0], E5M2, slice(0, N))
+        quantise(xm_ops[0], E4M3, slice(0, HALVES * P))
+        quantise(g_op[1], E5M2, slice(0, N))
+        xm_ops.append(operand("xm1", grouped_tag="g1_grouped", columns=HALVES * P))
+        weave_xm(xm_ops[1], block_halves[0], xm_first[:, :, P:], gpsimd_round)
 
         dw = [psum.tile([P, N], F32, name="dw%d" % b, tag="bank%d" % b) for b in range(BLOCKS - 1)]
 
         def gradient(b):
-            codes, scales = xm_ops[b // 2][1:]
+            codes, scales = xm_ops[min(b, 2)][1:]
             for h in range(HALVES):
-                first = h * XM_COLS + b % 2 * P
+                first = h * P if b < 2 else h * XM_COLS + b % 2 * P
                 cols = slice(first, first + P)
                 nc.tensor.matmul_mx(
                     out=dw[b][:], lhsT=codes[:, cols].bitcast(E4M3), lhsT_scale=scales[:, cols],
@@ -253,7 +258,8 @@ def tile_attend_gsq_nag_kernel(tc, xT, wT, y, wt, xm, mT, offs, out_0, out_1):
         new_m = {b: keep.tile([P, N], F32, name="new_m%d" % b, align_bytes=64) for b in range(1, BLOCKS)}
         m_term = [keep.tile([P, N], F32, name="m_term0")]
         dw_sb = keep.tile([P, BLOCKS, N], F32, name="dw_sb", tag="y0")
-        dw_term = keep.tile([P, BLOCKS, N], F32, name="dw_term", tag="y1")
+        dw_terms = keep.tile([P, 2, N], F32, name="dw_terms", tag="y1")
+        dw_term = {b: dw_terms[:, b - 2, :] for b in (2, 3)}
         m_dst = [keep.tile([P, T], F32, name="m_dst%d" % b, tag=tag, align_bytes=64)
                  for b, tag in enumerate(("table0", "shared0", "rest1", "shared1"))]
 
@@ -277,8 +283,8 @@ def tile_attend_gsq_nag_kernel(tc, xT, wT, y, wt, xm, mT, offs, out_0, out_1):
             nc.gpsimd.tensor_tensor(new_m[b][:], m_cols[:, b, :], dw_sb[:, b, :], ADD)
 
         def add_dw_term(b, total):
-            nc.scalar.activation(dw_term[:, b, :], dw[b][:], COPY, scale=DW_FACTOR)
-            nc.gpsimd.tensor_tensor(total, w_cols[:, b, :], dw_term[:, b, :], ADD)
+            nc.scalar.activation(dw_term[b], dw[b][:], COPY, scale=DW_FACTOR)
+            nc.gpsimd.tensor_tensor(total, w_cols[:, b, :], dw_term[b], ADD)
 
         def add_m_term(b, total):
             nc.scalar.activation(m_term[b][:], m_cols[:, b, :], COPY, scale=M_FACTOR)
@@ -316,8 +322,8 @@ def tile_attend_gsq_nag_kernel(tc, xT, wT, y, wt, xm, mT, offs, out_0, out_1):
         w0_turned = keep.tile([P, CHUNKS, P], F32, name="w0_turned", tag="mid0", align_bytes=64)
         for c in range(CHUNKS):
             nc.scalar.copy(w0_turned[:, c, :], sums[c][:])
-        weave_xm(xm_ops[0], second[1], xm_second[1])
-        quantise(xm_ops[0], E4M3, second[1])
+        weave_xm(xm_ops[1], block_halves[1], xm_second[1][:])
+        quantise(xm_ops[1], E4M3, slice(0, HALVES * P))
         w0_back = psum.tile([P, CHUNKS, P], F32, name="w0_back", tag="bank3")
         for c in range(CHUNKS):
             nc.tensor.transpose(w0_back[:, c, :], w0_turned[:, c, :], ident[:])
@@ -328,15 +334,16 @@ def tile_attend_gsq_nag_kernel(tc, xT, wT, y, wt, xm, mT, offs, out_0, out_1):
         gather_m(2)
         finish_w(0, new_w0[:])
 
+        dw_term[1] = keep.tile([P, N], F32, name="dw_term1", tag="rest0", align_bytes=64)[:]
         for b, tag in ((1, "mid0"), (2, "rest0"), (3, "m_term3")):
             m_term.append(keep.tile([P, N], F32, name="m_term%d" % b, tag=tag, align_bytes=64))
         update_m(1)
-        add_dw_term(1, w_cols[:, 1, :])
         xm_ops.append(operand("xm23"))
         for h, cols in enumerate(column_halves):
-            weave_xm(xm_ops[1], cols, xm_last[h])
+            weave_xm(xm_ops[2], cols, xm_last[h][:])
         for cols in column_halves:
-            quantise(xm_ops[1], E4M3, cols)
+            quantise(xm_ops[2], E4M3, cols)
+        add_dw_term(1, w_cols[:, 1, :])
         for b in (2, 3):
             gradient(b)
         finish_m(1)

@@ -33,8 +33,6 @@ BAND = 16
 
 X0_ON_SCALAR = 32
 X1_ON_SCALAR = 80
-W_COPIED = 1792
-M0_COPIED = 1536
 G1_ON_VECTOR = 256
 
 
@@ -75,8 +73,7 @@ def tile_attend_gsq_nag_kernel(tc, xT, wT, y, wt, xm, mT, offs, out_0, out_1):
         offsets = lists.tile([P, N // BAND], U16, name="offsets")
         x_raw = [keep.tile([P, PACK, K], F32, name="x_raw%d" % h, tag="shared%d" % h, align_bytes=64) for h in range(HALVES)]
         y_sb = [keep.tile([P, PACK, N], F32, name="y_sb%d" % h, tag="y%d" % h) for h in range(HALVES)]
-        xm_first = keep.tile([P, PACK, XM_COLS], F32, name="xm_first")
-        xm_second = [keep.tile([P, PACK, P], F32, name="xm_second%d" % b) for b in range(2)]
+        xm_raw = [[keep.tile([P, PACK, P], F32, name="xm_raw%d%d" % (b, h)) for h in range(HALVES)] for b in range(2)]
         xm_last = [keep.tile([P, PACK, XM_COLS], F32, name="xm_last%d" % h, tag="rest%d" % h, align_bytes=64) for h in range(HALVES)]
         w_src = [keep.tile([P, T], F32, name="w_src%d" % b, tag="table%d" % b, align_bytes=64) for b in range(BLOCKS)]
         m_src = [keep.tile([P, T], F32, name="m_src%d" % b) for b in range(BLOCKS)]
@@ -89,6 +86,10 @@ def tile_attend_gsq_nag_kernel(tc, xT, wT, y, wt, xm, mT, offs, out_0, out_1):
         def load_xm(tiles, first):
             for h in range(HALVES):
                 nc.sync.dma_start(out=tiles[h][:], in_=rows(xm[0, h * K : (h + 1) * K, first : first + XM_COLS]))
+
+        def load_xm_block(b):
+            for h in range(HALVES):
+                nc.sync.dma_start(out=xm_raw[b][h][:], in_=rows(xm[0, h * K : (h + 1) * K, b * P : (b + 1) * P]))
 
         def load_m(b):
             nc.sync.dma_start(out=m_src[b][:], in_=block(mT, b))
@@ -104,8 +105,7 @@ def tile_attend_gsq_nag_kernel(tc, xT, wT, y, wt, xm, mT, offs, out_0, out_1):
         for h in range(HALVES):
             for two_rows in row_pairs:
                 nc.sync.dma_start(out=y_sb[h][:, two_rows, :], in_=rows(y[0, h * K : (h + 1) * K, :])[:, two_rows, :])
-        nc.sync.dma_start(out=xm_first[:], in_=rows(xm[0, :K, :XM_COLS]))
-        nc.sync.dma_start(out=xm_second[0][:], in_=rows(xm[0, K:, :P]))
+        load_xm_block(0)
         load_m(0)
 
         w_cols = keep.tile([P, BLOCKS, N], F32, name="w_cols")
@@ -158,7 +158,7 @@ def tile_attend_gsq_nag_kernel(tc, xT, wT, y, wt, xm, mT, offs, out_0, out_1):
         every_chunk = tuple(range(CHUNKS))
         fill(w_dst[0], w_src[0])
         turn(0, every_chunk)
-        fill(w_dst[1], w_src[1], last=W_COPIED)
+        fill(w_dst[1], w_src[1])
         turn(1, every_chunk)
         wt_turned = psum.tile([P, PACK, P], F32, name="wt_turned", tag="bank7")
         for t in range(PACK):
@@ -232,16 +232,14 @@ def tile_attend_gsq_nag_kernel(tc, xT, wT, y, wt, xm, mT, offs, out_0, out_1):
         weave_g(nc.scalar.copy, 0, slot_halves)
         residual(1, whole=3)
         weave_g(nc.vector.tensor_copy, 1, (slice(0, G1_ON_VECTOR),))
-        weave_xm(xm_ops[0], block_halves[0], xm_first[:, :, :P], gpsimd_round)
-        weave_xm(xm_ops[0], block_halves[1], xm_second[0][:])
+        weave_xm(xm_ops[0], block_halves[0], xm_raw[0][0][:], gpsimd_round)
+        weave_xm(xm_ops[0], block_halves[1], xm_raw[0][1][:])
         weave_g(nc.scalar.copy, 1, (slice(G1_ON_VECTOR, N),))
         quantise(g_op[0], E5M2, slice(0, N))
         quantise(xm_ops[0], E4M3, slice(0, HALVES * P))
         quantise(g_op[1], E5M2, slice(0, N))
-        xm_ops.append(operand("xm1", grouped_tag="g1_grouped", columns=HALVES * P))
-        weave_xm(xm_ops[1], block_halves[0], xm_first[:, :, P:], gpsimd_round)
 
-        dw = [psum.tile([P, N], F32, name="dw%d" % b, tag="bank%d" % b) for b in range(BLOCKS - 1)]
+        dw = {b: psum.tile([P, N], F32, name="dw%d" % b, tag="bank%d" % b) for b in (0, 2)}
 
         def gradient(b):
             codes, scales = xm_ops[min(b, 2)][1:]
@@ -255,51 +253,41 @@ def tile_attend_gsq_nag_kernel(tc, xT, wT, y, wt, xm, mT, offs, out_0, out_1):
                 )
 
         m_cols = keep.tile([P, BLOCKS, N], F32, name="m_cols")
-        new_m = {b: keep.tile([P, N], F32, name="new_m%d" % b, align_bytes=64) for b in range(1, BLOCKS)}
-        m_term = [keep.tile([P, N], F32, name="m_term0")]
         dw_sb = keep.tile([P, BLOCKS, N], F32, name="dw_sb", tag="y0")
-        dw_terms = keep.tile([P, 2, N], F32, name="dw_terms", tag="y1")
-        dw_term = {b: dw_terms[:, b - 2, :] for b in (2, 3)}
-        m_dst = [keep.tile([P, T], F32, name="m_dst%d" % b, tag=tag, align_bytes=64)
-                 for b, tag in enumerate(("table0", "shared0", "rest1", "shared1"))]
-
-        def load_columns(dst, table, b, first):
-            nc.sync.dma_start(out=dst[b][:, first:], in_=block(table, b)[:, first:])
+        dw_term = keep.tile([P, BLOCKS, N], F32, name="dw_term", tag="y1")
+        m_dst = {b: keep.tile([P, T], F32, name="m_dst%d" % b, tag=tag, align_bytes=64)
+                 for b, tag in ((0, "table0"), (3, "shared1"))}
 
         load_m(1)
-        load_columns(m_dst, mT, 0, M0_COPIED)
-        nc.sync.dma_start(out=xm_second[1][:], in_=rows(xm[0, K:, P:XM_COLS]))
+        load_xm_block(1)
         load_m(2)
         load_xm(xm_last, XM_COLS)
-        load_columns(m_dst, mT, 1, 0)
-        load_columns(w_dst, wT, 1, W_COPIED)
         load_m(3)
 
         def gather_m(b):
             nc.vector.tensor_scalar(m_cols[:, b, :], m_src[b][:].indirect(offsets[:]), BETA, 0.0, MULT, ADD)
 
-        def update_m(b):
+        def copy_dw(b):
             nc.scalar.copy(dw_sb[:, b, :], dw[b][:])
-            nc.gpsimd.tensor_tensor(new_m[b][:], m_cols[:, b, :], dw_sb[:, b, :], ADD)
 
-        def add_dw_term(b, total):
-            nc.scalar.activation(dw_term[b], dw[b][:], COPY, scale=DW_FACTOR)
-            nc.gpsimd.tensor_tensor(total, w_cols[:, b, :], dw_term[b], ADD)
+        def scale_dw(b):
+            nc.scalar.activation(dw_term[:, b, :], dw[b][:], COPY, scale=DW_FACTOR)
 
-        def add_m_term(b, total):
-            nc.scalar.activation(m_term[b][:], m_cols[:, b, :], COPY, scale=M_FACTOR)
-            nc.gpsimd.tensor_tensor(total, w_cols[:, b, :], m_term[b][:], ADD)
+        def scale_m(b, tag):
+            term = keep.tile([P, N], F32, name="m_term%d" % b, tag=tag, align_bytes=64)
+            nc.scalar.activation(term[:], m_cols[:, b, :], COPY, scale=M_FACTOR)
+            return term[:]
 
-        def scatter(dst, values):
+        def add(total, first, second):
+            nc.gpsimd.tensor_tensor(total, first, second, ADD)
+
+        def finish(table, dst, b, values):
             nc.vector.tensor_copy(dst[:].indirect(offsets[:]), values)
+            nc.sync.dma_start(out=block(table, b), in_=dst[:])
 
-        def finish_m(b):
-            scatter(m_dst[b], new_m[b][:])
+        def finish_m_adding(b):
+            nc.vector.tensor_tensor(m_dst[b][:].indirect(offsets[:]), m_cols[:, b, :], dw_sb[:, b, :], ADD)
             nc.sync.dma_start(out=block(out_1, b), in_=m_dst[b][:])
-
-        def finish_w(b, values):
-            scatter(w_dst[b], values)
-            nc.sync.dma_start(out=block(out_0, b), in_=w_dst[b][:])
 
         sums = [psum.tile([P, P], F32, name="sum%d" % c, tag="bank%d" % (BLOCKS + c)) for c in range(CHUNKS)]
 
@@ -310,62 +298,69 @@ def tile_attend_gsq_nag_kernel(tc, xT, wT, y, wt, xm, mT, offs, out_0, out_1):
 
         gradient(0)
         gather_m(0)
-        nc.scalar.activation(m_dst[0][:, :M0_COPIED], m_src[0][:, :M0_COPIED], COPY)
-        nc.scalar.copy(dw_sb[:, 0, :], dw[0][:])
+        fill(m_dst[0], m_src[0])
+        copy_dw(0)
         gather_m(1)
-        nc.vector.tensor_tensor(m_dst[0][:].indirect(offsets[:]), m_cols[:, 0, :], dw_sb[:, 0, :], ADD)
-        nc.sync.dma_start(out=block(out_1, 0), in_=m_dst[0][:])
-        nc.scalar.activation(m_term[0][:], m_cols[:, 0, :], COPY, scale=BETA / (1.0 + BETA))
+        finish_m_adding(0)
+        m_term0 = keep.tile([P, N], F32, name="m_term0")
+        nc.scalar.activation(m_term0[:], m_cols[:, 0, :], COPY, scale=BETA / (1.0 + BETA))
         add_turned(w0_scaled[:], True, False)
         add_turned(dw_sb[:, 0, :], False, False)
-        add_turned(m_term[0][:], False, True)
+        add_turned(m_term0[:], False, True)
         w0_turned = keep.tile([P, CHUNKS, P], F32, name="w0_turned", tag="mid0", align_bytes=64)
         for c in range(CHUNKS):
             nc.scalar.copy(w0_turned[:, c, :], sums[c][:])
-        weave_xm(xm_ops[1], block_halves[1], xm_second[1][:])
+        xm_ops.append(operand("xm1", columns=HALVES * P))
+        for h in range(HALVES):
+            weave_xm(xm_ops[1], block_halves[h], xm_raw[1][h][:])
         quantise(xm_ops[1], E4M3, slice(0, HALVES * P))
         w0_back = psum.tile([P, CHUNKS, P], F32, name="w0_back", tag="bank3")
         for c in range(CHUNKS):
             nc.tensor.transpose(w0_back[:, c, :], w0_turned[:, c, :], ident[:])
-        new_w0 = keep.tile([P, N], F32, name="new_w0")
+        new_w0 = keep.tile([P, N], F32, name="new_w0", tag="xm_raw11")
         nc.scalar.activation(new_w0[:], w0_back[:].rearrange("p c s -> p (c s)"), COPY, scale=DW_FACTOR)
-        dw.append(psum.tile([P, N], F32, name="dw3", tag="bank3"))
+        dw[3] = psum.tile([P, N], F32, name="dw3", tag="bank3")
+        dw[1] = psum.tile([P, N], F32, name="dw1", tag="bank7")
         gradient(1)
         gather_m(2)
-        finish_w(0, new_w0[:])
+        finish(out_0, w_dst[0], 0, new_w0[:])
 
-        dw_term[1] = keep.tile([P, N], F32, name="dw_term1", tag="rest0", align_bytes=64)[:]
-        for b, tag in ((1, "mid0"), (2, "rest0"), (3, "m_term3")):
-            m_term.append(keep.tile([P, N], F32, name="m_term%d" % b, tag=tag, align_bytes=64))
-        update_m(1)
-        xm_ops.append(operand("xm23"))
+        new_w1 = keep.tile([P, N], F32, name="new_w1", tag="xm1_grouped", align_bytes=64)
+        add(new_w1[:], w_cols[:, 1, :], scale_m(1, "m_term1"))
+        scale_dw(1)
+        add(new_w1[:], new_w1[:], dw_term[:, 1, :])
+        copy_dw(1)
+        new_m1 = keep.tile([P, N], F32, name="new_m1")
+        add(new_m1[:], m_cols[:, 1, :], dw_sb[:, 1, :])
+        gather_m(3)
+        finish(out_0, w_dst[1], 1, new_w1[:])
+
+        xm_ops.append(operand("xm23", grouped_tag="mid0"))
         for h, cols in enumerate(column_halves):
             weave_xm(xm_ops[2], cols, xm_last[h][:])
         for cols in column_halves:
             quantise(xm_ops[2], E4M3, cols)
-        add_dw_term(1, w_cols[:, 1, :])
         for b in (2, 3):
             gradient(b)
-        finish_m(1)
-        new_w1 = keep.tile([P, N], F32, name="new_w1", tag="xm23_grouped", align_bytes=64)
-        add_m_term(1, new_w1[:])
-        gather_m(3)
-        finish_w(1, new_w1[:])
-        w_dst.append(keep.tile([P, T], F32, name="w_dst2", tag="mid0", align_bytes=64))
-        w_dst.append(keep.tile([P, T], F32, name="w_dst3", tag="xm23_grouped", align_bytes=64))
-
-        update_m(2)
-        fill(m_dst[2], m_src[2])
-        finish_m(2)
-        add_dw_term(2, w_cols[:, 2, :])
-        add_m_term(2, w_cols[:, 2, :])
+        add(w_cols[:, 2, :], w_cols[:, 2, :], scale_m(2, "rest0"))
+        m_dst[1] = keep.tile([P, T], F32, name="m_dst1", tag="rest1", align_bytes=64)
+        fill(m_dst[1], m_src[1])
+        finish(out_1, m_dst[1], 1, new_m1[:])
+        w_dst.append(keep.tile([P, T], F32, name="w_dst2", tag="xm_raw11"))
+        w_dst.append(keep.tile([P, T], F32, name="w_dst3", tag="mid0", align_bytes=64))
+        m_dst[2] = keep.tile([P, T], F32, name="m_dst2", tag="xm23_codes", align_bytes=64)
         fill(w_dst[2], w_src[2])
-        finish_w(2, w_cols[:, 2, :])
-
-        update_m(3)
-        fill(m_dst[3], m_src[3])
-        finish_m(3)
-        add_dw_term(3, w_cols[:, 3, :])
-        add_m_term(3, w_cols[:, 3, :])
+        scale_dw(2)
+        add(w_cols[:, 2, :], w_cols[:, 2, :], dw_term[:, 2, :])
+        add(w_cols[:, 3, :], w_cols[:, 3, :], scale_m(3, "xm23_scales"))
+        scale_dw(3)
+        add(w_cols[:, 3, :], w_cols[:, 3, :], dw_term[:, 3, :])
+        finish(out_0, w_dst[2], 2, w_cols[:, 2, :])
+        copy_dw(2)
+        fill(m_dst[2], m_src[2])
+        finish_m_adding(2)
         fill(w_dst[3], w_src[3])
-        finish_w(3, w_cols[:, 3, :])
+        finish(out_0, w_dst[3], 3, w_cols[:, 3, :])
+        copy_dw(3)
+        fill(m_dst[3], m_src[3])
+        finish_m_adding(3)

@@ -31,7 +31,6 @@ SPAN = P // PACK
 XM_COLS = 2 * P
 BAND = 16
 
-X0_ON_SCALAR = 32
 X1_ON_SCALAR = 80
 G1_ON_VECTOR = 256
 
@@ -171,8 +170,7 @@ def tile_attend_gsq_nag_kernel(tc, xT, wT, y, wt, xm, mT, offs, out_0, out_1):
         turn(3, every_chunk[CHUNKS // 2 :])
         backs = [turn_back(half) for half in range(2)]
         dst, src = x_views(0)
-        nc.scalar.copy(out=dst[:, :X0_ON_SCALAR], in_=src[:, :X0_ON_SCALAR])
-        nc.vector.tensor_copy(out=dst[:, X0_ON_SCALAR:], in_=src[:, X0_ON_SCALAR:])
+        nc.vector.tensor_copy(out=dst, in_=src)
         quantise(x_op[0], E4M3, slice(0, K))
         copy_back(nc.scalar.copy, 0, backs[0])
         copy_back(nc.scalar.copy, 1, backs[1])
@@ -352,15 +350,17 @@ def tile_attend_gsq_nag_kernel(tc, xT, wT, y, wt, xm, mT, offs, out_0, out_1):
         fill(w_dst[2], w_src[2])
         scale_dw(2)
         add(w_cols[:, 2, :], w_cols[:, 2, :], dw_term[:, 2, :])
+        copy_dw(2)
+        add(m_cols[:, 2, :], m_cols[:, 2, :], dw_sb[:, 2, :])
         add(w_cols[:, 3, :], w_cols[:, 3, :], scale_m(3, "xm23_scales"))
         scale_dw(3)
         add(w_cols[:, 3, :], w_cols[:, 3, :], dw_term[:, 3, :])
         finish(out_0, w_dst[2], 2, w_cols[:, 2, :])
-        copy_dw(2)
         fill(m_dst[2], m_src[2])
-        finish_m_adding(2)
+        finish(out_1, m_dst[2], 2, m_cols[:, 2, :])
         fill(w_dst[3], w_src[3])
         finish(out_0, w_dst[3], 3, w_cols[:, 3, :])
         copy_dw(3)
+        add(m_cols[:, 3, :], m_cols[:, 3, :], dw_sb[:, 3, :])
         fill(m_dst[3], m_src[3])
-        finish_m_adding(3)
+        finish(out_1, m_dst[3], 3, m_cols[:, 3, :])

@@ -101,9 +101,9 @@ def tile_attend_gsq_nag_kernel(tc, xT, wT, y, wt, xm, mT, offs, out_0, out_1):
             nc.sync.dma_start(out=w_src[b][:], in_=block(wT, b))
         for h in range(HALVES):
             nc.sync.dma_start(out=x_raw[h][:], in_=rows(xT[0, :, h * K : (h + 1) * K]))
-        for h in range(HALVES):
-            for two_rows in row_pairs:
-                nc.sync.dma_start(out=y_sb[h][:, two_rows, :], in_=rows(y[0, h * K : (h + 1) * K, :])[:, two_rows, :])
+        for h, some_rows in ((0, row_pairs), (1, (row_pairs[0], slice(2, 3), slice(3, 4)))):
+            for part in some_rows:
+                nc.sync.dma_start(out=y_sb[h][:, part, :], in_=rows(y[0, h * K : (h + 1) * K, :])[:, part, :])
         load_xm_block(0)
         load_m(0)
 
@@ -170,8 +170,10 @@ def tile_attend_gsq_nag_kernel(tc, xT, wT, y, wt, xm, mT, offs, out_0, out_1):
         turn(3, every_chunk[CHUNKS // 2 :])
         backs = [turn_back(half) for half in range(2)]
         dst, src = x_views(0)
-        nc.vector.tensor_copy(out=dst, in_=src)
-        quantise(x_op[0], E4M3, slice(0, K))
+        for pair in row_pairs:
+            nc.vector.tensor_copy(out=dst[:, :, :, pair], in_=src[:, :, :, pair])
+        for cols in column_halves:
+            quantise(x_op[0], E4M3, cols)
         copy_back(nc.scalar.copy, 0, backs[0])
         copy_back(nc.scalar.copy, 1, backs[1])
         for half, part in enumerate(slot_halves):

@@ -136,18 +136,16 @@ def tile_attend_gsq_nag_kernel(tc, xT, wT, y, wt, xm, mT, offs, out_0, out_1):
                     out=w_turned[chunks[i] // 2][:, :, :, SPAN * b : SPAN * (b + 1), :].rearrange("s c u q e -> s c q u e"),
                     in_=turned[:, i : i + 2, :].rearrange("s c (q u e) -> s c q u e", u=2, e=2))
 
-        def turn_back(half):
-            back = psum.tile([P, 2, 2, P], F32, name="back%d" % half, tag="bank%d" % (BLOCKS + 1 + half))
+        def turn_back(chunks, bank):
+            half, first = divmod(chunks[0], 2)
+            back = psum.tile([P, len(chunks), 2, P], F32, name="back%d" % chunks[0], tag="bank%d" % bank)
             pairs = w_turned[half][:].rearrange("s c u q e -> s (c u q e)").bitcast(F32)
-            for c in range(2):
+            for i in range(len(chunks)):
                 for u in range(2):
-                    run = 2 * c + u
-                    nc.tensor.transpose(back[:, c, u, :], pairs[:, run * P : (run + 1) * P], ident[:])
-            return back
-
-        def copy_back(copy, half, back):
+                    run = 2 * (first + i) + u
+                    nc.tensor.transpose(back[:, i, u, :], pairs[:, run * P : (run + 1) * P], ident[:])
             dst = w_grouped[half].bitcast(F32).rearrange("p (c s u) -> p c s u", c=2, u=2)
-            copy(out=dst, in_=back[:].rearrange("p c u s -> p c s u"))
+            nc.scalar.copy(out=dst[:, first : first + len(chunks)], in_=back[:].rearrange("p c u s -> p c s u"))
 
         def x_views(h):
             dst = x_op[h][0][:].rearrange("p (t m j) -> p m j t", t=PACK, j=PACK)
@@ -168,14 +166,13 @@ def tile_attend_gsq_nag_kernel(tc, xT, wT, y, wt, xm, mT, offs, out_0, out_1):
         turn(2, every_chunk)
         turn(3, every_chunk[: CHUNKS // 2])
         turn(3, every_chunk[CHUNKS // 2 :])
-        backs = [turn_back(half) for half in range(2)]
+        for chunks, bank in (((0, 1), 5), ((2,), 6), ((3,), 7)):
+            turn_back(chunks, bank)
         dst, src = x_views(0)
         for pair in row_pairs:
             nc.vector.tensor_copy(out=dst[:, :, :, pair], in_=src[:, :, :, pair])
         for cols in column_halves:
             quantise(x_op[0], E4M3, cols)
-        copy_back(nc.scalar.copy, 0, backs[0])
-        copy_back(nc.scalar.copy, 1, backs[1])
         for half, part in enumerate(slot_halves):
             nc.vector.quantize_mx(out=w_codes[:, part].bitcast(E4M3), scales=w_scales[:, part], in_=w_grouped[half])
         dst, src = x_views(1)
@@ -227,7 +224,7 @@ def tile_attend_gsq_nag_kernel(tc, xT, wT, y, wt, xm, mT, offs, out_0, out_1):
         block_halves = (slice(0, P), slice(P, 2 * P))
 
         weigh_y(0, (0, 1, 3))
-        residual(0, whole=2)
+        residual(0, whole=1)
         weigh_y(1, (1,))
         weave_g(nc.scalar.copy, 0, slot_halves)
         residual(1, whole=3)

@@ -6,7 +6,7 @@ from concourse.masks import make_identity
 D, T, N, R = 512, 2048, 512, 1024
 LR, BETA = 0.1, 0.9
 DW_FACTOR = -LR * (1.0 + BETA)
-M_FACTOR = -LR * BETA
+M_FACTOR = -LR * BETA * BETA
 FLOPS = 2 * 2 * D * N * R
 
 F32 = mybir.dt.float32
@@ -25,14 +25,10 @@ P = 128
 PACK = 4
 K = P * PACK
 HALVES = R // K
-BLOCKS = D // P
-CHUNKS = N // P
-SPAN = P // PACK
-XM_COLS = 2 * P
 BAND = 16
 
-X1_ON_SCALAR = 80
-G1_ON_VECTOR = 256
+X_ON_SCALAR = (40, 40)
+G1_ON_SCALAR = 160
 
 
 def tile_attend_gsq_nag_kernel(tc, xT, wT, y, wt, xm, mT, offs, out_0, out_1):
@@ -46,141 +42,100 @@ def tile_attend_gsq_nag_kernel(tc, xT, wT, y, wt, xm, mT, offs, out_0, out_1):
         column_halves = (slice(0, K // 2), slice(K // 2, K))
         row_pairs = (slice(0, PACK // 2), slice(PACK // 2, PACK))
 
-        def block(table, b):
-            return table[b * P : (b + 1) * P, :]
-
         def rows(src):
             return src.rearrange("(p j) c -> p j c", j=PACK)
 
-        def operand(name, scales_tag=None, grouped_tag=None, columns=K):
-            grouped = keep.tile([P, columns * PACK], BF16, name=name + "_grouped", tag=grouped_tag or name + "_grouped", align_bytes=64)
-            codes = keep.tile([P, columns], U32, name=name + "_codes", align_bytes=64)
-            scales = keep.tile([P, columns], U8, name=name + "_scales", tag=scales_tag or name + "_scales", align_bytes=64)
+        def plane(table, t):
+            return rows(table)[:, t, :]
+
+        def operand(name):
+            grouped = keep.tile([P, K * PACK], BF16, name=name + "_grouped", align_bytes=64)
+            codes = keep.tile([P, K], U32, name=name + "_codes", align_bytes=64)
+            scales = keep.tile([P, K], U8, name=name + "_scales", align_bytes=64)
             return grouped, codes, scales
 
-        def quantise(op, fmt, cols):
+        def quantise(op, fmt, cols=slice(0, K)):
             grouped, codes, scales = op
             nc.vector.quantize_mx(
                 out=codes[:, cols].bitcast(fmt), scales=scales[:, cols],
                 in_=grouped[:, PACK * cols.start : PACK * cols.stop])
 
-        def weave_views(grouped, four_rows):
-            dst = grouped.rearrange("p (c i t) -> p c t i", i=PACK, t=PACK)
-            src = four_rows.rearrange("p t (c i) -> p c t i", i=PACK)
+        def weave(copy, op, four_rows, cols):
+            dst = op[0][:, PACK * cols.start : PACK * cols.stop].rearrange("p (c i t) -> p c t i", i=PACK, t=PACK)
+            src = four_rows[:, :, cols].rearrange("p t (c i) -> p c t i", i=PACK)
+            copy(out=dst, in_=src)
+
+        def dealt_views(op, raw):
+            dst = op[0][:].rearrange("p (t m j) -> p m j t", t=PACK, j=PACK)
+            src = raw[:].rearrange("p j (m t) -> p m j t", t=PACK)
             return dst, src
 
         offsets = lists.tile([P, N // BAND], U16, name="offsets")
-        x_raw = [keep.tile([P, PACK, K], F32, name="x_raw%d" % h, tag="shared%d" % h, align_bytes=64) for h in range(HALVES)]
-        y_sb = [keep.tile([P, PACK, N], F32, name="y_sb%d" % h, tag="y%d" % h) for h in range(HALVES)]
-        xm_raw = [[keep.tile([P, PACK, P], F32, name="xm_raw%d%d" % (b, h)) for h in range(HALVES)] for b in range(2)]
-        xm_last = [keep.tile([P, PACK, XM_COLS], F32, name="xm_last%d" % h, tag="rest%d" % h, align_bytes=64) for h in range(HALVES)]
-        w_src = [keep.tile([P, T], F32, name="w_src%d" % b, tag="table%d" % b, align_bytes=64) for b in range(BLOCKS)]
-        m_src = [keep.tile([P, T], F32, name="m_src%d" % b) for b in range(BLOCKS)]
+        x_raw = [keep.tile([P, PACK, K], F32, name="x_raw%d" % h, align_bytes=256) for h in range(HALVES)]
+        y_sb = [keep.tile([P, PACK, N], F32, name="y_sb%d" % h, align_bytes=256) for h in range(HALVES)]
+        xm_raw = [keep.tile([P, PACK, D], F32, name="xm_raw%d" % h, align_bytes=256) for h in range(HALVES)]
+        w_src = [keep.tile([P, T], F32, name="w_src%d" % t, tag="window%d" % t, align_bytes=256) for t in range(PACK)]
+        w_dst = [keep.tile([P, T], F32, name="w_dst%d" % t, align_bytes=256) for t in range(PACK)]
+        m_dst = [keep.tile([P, T], F32, name="m_dst%d" % t, align_bytes=256) for t in range(PACK)]
         wt_rows = keep.tile([P, K], F32, name="wt_rows")
-        wt_all = keep.tile([P, HALVES, PACK], F32, name="wt_sb", tag="wt1", align_bytes=64)
+        wt_all = keep.tile([P, HALVES, PACK], F32, name="wt_sb")
         wt_sb = [wt_all[:, h, :] for h in range(HALVES)]
         ident = keep.tile([P, P], F32, name="ident")
         make_identity(nc, ident[:])
-
-        def load_xm(tiles, first):
-            for h in range(HALVES):
-                nc.sync.dma_start(out=tiles[h][:], in_=rows(xm[0, h * K : (h + 1) * K, first : first + XM_COLS]))
-
-        def load_xm_block(b):
-            for h in range(HALVES):
-                nc.sync.dma_start(out=xm_raw[b][h][:], in_=rows(xm[0, h * K : (h + 1) * K, b * P : (b + 1) * P]))
-
-        def load_m(b):
-            nc.sync.dma_start(out=m_src[b][:], in_=block(mT, b))
+        ones = keep.tile([P, 1], F32, name="ones")
+        m_scale = keep.tile([P, 1], F32, name="m_scale")
+        new_m_scale = keep.tile([P, 1], F32, name="new_m_scale")
+        nc.vector.memset(ones[:], 1.0)
+        nc.vector.tensor_scalar(m_scale[:], ones[:], M_FACTOR, 0.0, MULT, ADD)
+        nc.vector.tensor_scalar(new_m_scale[:], ones[:], BETA / M_FACTOR, 0.0, MULT, ADD)
 
         nc.vector.memset(wt_rows[:], 0.0)
-        nc.sync.dma_start(out=w_src[0][:], in_=block(wT, 0))
+        nc.sync.dma_start(out=w_src[0][:], in_=plane(wT, 0))
         nc.sync.dma_start(offsets[:], offs)
         nc.sync.dma_start(out=wt_rows[:: P // HALVES, :], in_=wt[0].rearrange("(h k) o -> h (k o)", h=HALVES))
-        for b in range(1, BLOCKS):
-            nc.sync.dma_start(out=w_src[b][:], in_=block(wT, b))
+        for t in range(1, PACK):
+            nc.sync.dma_start(out=w_src[t][:], in_=plane(wT, t))
         for h in range(HALVES):
             nc.sync.dma_start(out=x_raw[h][:], in_=rows(xT[0, :, h * K : (h + 1) * K]))
-        for h, some_rows in ((0, row_pairs), (1, (row_pairs[0], slice(2, 3), slice(3, 4)))):
-            for part in some_rows:
+        for h in range(HALVES):
+            for part in row_pairs:
                 nc.sync.dma_start(out=y_sb[h][:, part, :], in_=rows(y[0, h * K : (h + 1) * K, :])[:, part, :])
-        load_xm_block(0)
-        load_m(0)
+        for h in range(HALVES):
+            nc.sync.dma_start(out=xm_raw[h][:], in_=rows(xm[0, h * K : (h + 1) * K, :]))
 
-        w_cols = keep.tile([P, BLOCKS, N], F32, name="w_cols")
-        w_dst = [keep.tile([P, T], F32, name="w_dst%d" % b) for b in range(2)]
-        w_turned = [keep.tile([P, 2, 2, P, 2], BF16, name="w_turned%d" % i, align_bytes=64) for i in range(CHUNKS // 2)]
+        w_cols = keep.tile([P, PACK, N], F32, name="w_cols")
+        w_op = operand("w")
+        x_op = [operand("x%d" % h) for h in range(HALVES)]
+        g_op = [operand("g%d" % h) for h in range(HALVES)]
+        xm_op = [operand("xm%d" % h) for h in range(HALVES)]
 
-        def fill(dst, src, last=T):
-            for part in (slice(0, T // 2), slice(T // 2, last)):
+        def fill_on_scalar(dst, src):
+            for part in (slice(0, T // 2), slice(T // 2, T)):
                 nc.scalar.activation(dst[:, part], src[:, part], COPY)
 
-        x_op = [operand("x%d" % h) for h in range(HALVES)]
-        w_whole = keep.tile([P, K * PACK], BF16, name="w_grouped", align_bytes=64)
-        w_grouped = [w_whole[:, PACK * part.start : PACK * part.stop] for part in slot_halves]
-        w_codes = keep.tile([P, N], U32, name="w_codes", align_bytes=64)
-        w_scales = keep.tile([P, N], U8, name="w_scales", align_bytes=64)
-        g_op = [operand("g0", scales_tag="wt1"), operand("g1")]
-        xm_ops = [operand("xm0", columns=HALVES * P)]
-
-        def turn(b, chunks):
-            slots = slice(chunks[0] * P, (chunks[-1] + 1) * P)
-            nc.vector.tensor_copy(
-                w_cols[:, b, slots], w_src[b][:].indirect(offsets[:, slots.start // BAND : slots.stop // BAND]))
-            turned = psum.tile(
-                [P, len(chunks), P], F32, name="turned%d%d" % (b, chunks[0]), tag="bank%d" % (b + chunks[0] // 2))
-            for i, c in enumerate(chunks):
-                nc.tensor.transpose(turned[:, i, :], w_cols[:, b, c * P : (c + 1) * P], ident[:])
-            for i in range(0, len(chunks), 2):
-                nc.scalar.copy(
-                    out=w_turned[chunks[i] // 2][:, :, :, SPAN * b : SPAN * (b + 1), :].rearrange("s c u q e -> s c q u e"),
-                    in_=turned[:, i : i + 2, :].rearrange("s c (q u e) -> s c q u e", u=2, e=2))
-
-        def turn_back(chunks, bank):
-            half, first = divmod(chunks[0], 2)
-            back = psum.tile([P, len(chunks), 2, P], F32, name="back%d" % chunks[0], tag="bank%d" % bank)
-            pairs = w_turned[half][:].rearrange("s c u q e -> s (c u q e)").bitcast(F32)
-            for i in range(len(chunks)):
-                for u in range(2):
-                    run = 2 * (first + i) + u
-                    nc.tensor.transpose(back[:, i, u, :], pairs[:, run * P : (run + 1) * P], ident[:])
-            dst = w_grouped[half].bitcast(F32).rearrange("p (c s u) -> p c s u", c=2, u=2)
-            nc.scalar.copy(out=dst[:, first : first + len(chunks)], in_=back[:].rearrange("p c u s -> p c s u"))
-
-        def x_views(h):
-            dst = x_op[h][0][:].rearrange("p (t m j) -> p m j t", t=PACK, j=PACK)
-            src = x_raw[h][:].rearrange("p j (m t) -> p m j t", t=PACK)
-            return dst, src
-
-        every_chunk = tuple(range(CHUNKS))
-        fill(w_dst[0], w_src[0])
-        turn(0, every_chunk)
-        fill(w_dst[1], w_src[1])
-        turn(1, every_chunk)
         wt_turned = psum.tile([P, PACK, P], F32, name="wt_turned", tag="bank7")
         for t in range(PACK):
             nc.tensor.transpose(wt_turned[:, t, :], wt_rows[:, t::PACK], ident[:])
         nc.scalar.copy(out=wt_all[:], in_=wt_turned[:, :, :: P // HALVES].rearrange("p t h -> p h t"))
-        w0_scaled = keep.tile([P, N], F32, name="w0_scaled")
-        nc.scalar.activation(w0_scaled[:], w_cols[:, 0, :], COPY, scale=1.0 / DW_FACTOR)
-        turn(2, every_chunk)
-        turn(3, every_chunk[: CHUNKS // 2])
-        turn(3, every_chunk[CHUNKS // 2 :])
-        for chunks, bank in (((0, 1), 5), ((2,), 6), ((3,), 7)):
-            turn_back(chunks, bank)
-        dst, src = x_views(0)
-        for pair in row_pairs:
-            nc.vector.tensor_copy(out=dst[:, :, :, pair], in_=src[:, :, :, pair])
-        for cols in column_halves:
-            quantise(x_op[0], E4M3, cols)
-        for half, part in enumerate(slot_halves):
-            nc.vector.quantize_mx(out=w_codes[:, part].bitcast(E4M3), scales=w_scales[:, part], in_=w_grouped[half])
-        dst, src = x_views(1)
-        nc.scalar.copy(out=dst[:, :X1_ON_SCALAR, :, row_pairs[0]], in_=src[:, :X1_ON_SCALAR, :, row_pairs[0]])
-        nc.vector.tensor_copy(out=dst[:, X1_ON_SCALAR:, :, row_pairs[0]], in_=src[:, X1_ON_SCALAR:, :, row_pairs[0]])
-        nc.vector.tensor_copy(out=dst[:, :, :, row_pairs[1]], in_=src[:, :, :, row_pairs[1]])
-        for cols in column_halves:
-            quantise(x_op[1], E4M3, cols)
+        for t in range(PACK):
+            nc.vector.tensor_copy(w_cols[:, t, :], w_src[t][:].indirect(offsets[:]))
+            fill_on_scalar(w_dst[t], w_src[t])
+        for part in slot_halves:
+            weave(nc.vector.tensor_copy, w_op, w_cols, part)
+        for part in slot_halves:
+            quantise(w_op, E4M3, part)
+        for h in range(HALVES):
+            dst, src = dealt_views(x_op[h], x_raw[h])
+            cut = X_ON_SCALAR[h]
+            nc.scalar.copy(out=dst[:, : 2 * cut, :, row_pairs[1]], in_=src[:, : 2 * cut, :, row_pairs[1]])
+            nc.vector.tensor_copy(out=dst[:, :, :, row_pairs[0]], in_=src[:, :, :, row_pairs[0]])
+            nc.vector.tensor_copy(out=dst[:, 2 * cut :, :, row_pairs[1]], in_=src[:, 2 * cut :, :, row_pairs[1]])
+            for cols in column_halves:
+                quantise(x_op[h], E4M3, cols)
+
+        m_src = [keep.tile([P, T], F32, name="m_src%d" % t, tag="window%d" % t, align_bytes=256) for t in range(PACK)]
+        for t in range(PACK):
+            nc.sync.dma_start(out=m_src[t][:], in_=plane(mT, t))
 
         def weigh_y(h, on_scalar):
             for t in range(PACK):
@@ -198,7 +153,7 @@ def tile_attend_gsq_nag_kernel(tc, xT, wT, y, wt, xm, mT, offs, out_0, out_1):
                 a = psum.tile([P, N], F32, name="a%d%d" % (h, t), tag="bank%d" % (PACK * h + t))
                 nc.tensor.matmul_mx(
                     out=a[:], lhsT=codes[:, cols].bitcast(E4M3), lhsT_scale=scales[:, cols],
-                    rhs=w_codes[:].bitcast(E4M3), rhs_scale=w_scales[:], start=True, stop=True,
+                    rhs=w_op[1][:].bitcast(E4M3), rhs_scale=w_op[2][:], start=True, stop=True,
                 )
                 banks.append(a)
             steps = [(t, slice(0, N)) for t in range(whole)]
@@ -209,157 +164,54 @@ def tile_attend_gsq_nag_kernel(tc, xT, wT, y, wt, xm, mT, offs, out_0, out_1):
                     in1=y_sb[h][:, t, part], op0=MULT, op1=SUB,
                 )
 
-        def weave_g(copy, h, parts):
-            for part in parts:
-                dst, src = weave_views(g_op[h][0][:, PACK * part.start : PACK * part.stop], y_sb[h][:, :, part])
-                copy(out=dst, in_=src)
-
-        def gpsimd_round(out, in_):
-            nc.gpsimd.tensor_scalar(out, in_, 1.0, 0.0, MULT, ADD)
-
-        def weave_xm(op, cols, four_rows, copy=nc.scalar.copy):
-            dst, src = weave_views(op[0][:, PACK * cols.start : PACK * cols.stop], four_rows)
-            copy(out=dst, in_=src)
-
-        block_halves = (slice(0, P), slice(P, 2 * P))
-
-        weigh_y(0, (0, 1, 3))
-        residual(0, whole=1)
+        weigh_y(0, (0, 1, 2, 3))
+        residual(0, whole=2)
         weigh_y(1, (1,))
-        weave_g(nc.scalar.copy, 0, slot_halves)
+        for part in slot_halves:
+            weave(nc.scalar.copy, g_op[0], y_sb[0], part)
         residual(1, whole=3)
-        weave_g(nc.vector.tensor_copy, 1, (slice(0, G1_ON_VECTOR),))
-        weave_xm(xm_ops[0], block_halves[0], xm_raw[0][0][:], gpsimd_round)
-        weave_xm(xm_ops[0], block_halves[1], xm_raw[0][1][:])
-        weave_g(nc.scalar.copy, 1, (slice(G1_ON_VECTOR, N),))
-        quantise(g_op[0], E5M2, slice(0, N))
-        quantise(xm_ops[0], E4M3, slice(0, HALVES * P))
-        quantise(g_op[1], E5M2, slice(0, N))
-
-        dw = {b: psum.tile([P, N], F32, name="dw%d" % b, tag="bank%d" % b) for b in (0, 2)}
-
-        def gradient(b):
-            codes, scales = xm_ops[min(b, 2)][1:]
-            for h in range(HALVES):
-                first = h * P if b < 2 else h * XM_COLS + b % 2 * P
-                cols = slice(first, first + P)
-                nc.tensor.matmul_mx(
-                    out=dw[b][:], lhsT=codes[:, cols].bitcast(E4M3), lhsT_scale=scales[:, cols],
-                    rhs=g_op[h][1][:].bitcast(E5M2), rhs_scale=g_op[h][2][:],
-                    start=(h == 0), stop=(h == HALVES - 1),
-                )
-
-        m_cols = keep.tile([P, BLOCKS, N], F32, name="m_cols")
-        dw_sb = keep.tile([P, BLOCKS, N], F32, name="dw_sb", tag="y0")
-        dw_term = keep.tile([P, BLOCKS, N], F32, name="dw_term", tag="y1")
-        m_dst = {b: keep.tile([P, T], F32, name="m_dst%d" % b, tag=tag, align_bytes=64)
-                 for b, tag in ((0, "table0"), (3, "shared1"))}
-
-        load_m(1)
-        load_xm_block(1)
-        load_m(2)
-        load_xm(xm_last, XM_COLS)
-        load_m(3)
-
-        def gather_m(b):
-            nc.vector.tensor_scalar(m_cols[:, b, :], m_src[b][:].indirect(offsets[:]), BETA, 0.0, MULT, ADD)
-
-        def copy_dw(b):
-            nc.scalar.copy(dw_sb[:, b, :], dw[b][:])
-
-        def scale_dw(b):
-            nc.scalar.activation(dw_term[:, b, :], dw[b][:], COPY, scale=DW_FACTOR)
-
-        def scale_m(b, tag):
-            term = keep.tile([P, N], F32, name="m_term%d" % b, tag=tag, align_bytes=64)
-            nc.scalar.activation(term[:], m_cols[:, b, :], COPY, scale=M_FACTOR)
-            return term[:]
-
-        def add(total, first, second):
-            nc.gpsimd.tensor_tensor(total, first, second, ADD)
-
-        def finish(table, dst, b, values):
-            nc.vector.tensor_copy(dst[:].indirect(offsets[:]), values)
-            nc.sync.dma_start(out=block(table, b), in_=dst[:])
-
-        def finish_m_adding(b):
-            nc.vector.tensor_tensor(m_dst[b][:].indirect(offsets[:]), m_cols[:, b, :], dw_sb[:, b, :], ADD)
-            nc.sync.dma_start(out=block(out_1, b), in_=m_dst[b][:])
-
-        sums = [psum.tile([P, P], F32, name="sum%d" % c, tag="bank%d" % (BLOCKS + c)) for c in range(CHUNKS)]
-
-        def add_turned(values, start, stop):
-            for c in range(CHUNKS):
-                nc.tensor.matmul(
-                    out=sums[c][:], lhsT=values[:, c * P : (c + 1) * P], rhs=ident[:], start=start, stop=stop, is_transpose=True)
-
-        gradient(0)
-        gather_m(0)
-        fill(m_dst[0], m_src[0])
-        copy_dw(0)
-        gather_m(1)
-        finish_m_adding(0)
-        m_term0 = keep.tile([P, N], F32, name="m_term0")
-        nc.scalar.activation(m_term0[:], m_cols[:, 0, :], COPY, scale=BETA / (1.0 + BETA))
-        add_turned(w0_scaled[:], True, False)
-        add_turned(dw_sb[:, 0, :], False, False)
-        add_turned(m_term0[:], False, True)
-        w0_turned = keep.tile([P, CHUNKS, P], F32, name="w0_turned", tag="mid0", align_bytes=64)
-        for c in range(CHUNKS):
-            nc.scalar.copy(w0_turned[:, c, :], sums[c][:])
-        xm_ops.append(operand("xm1", columns=HALVES * P))
-        for h in range(HALVES):
-            weave_xm(xm_ops[1], block_halves[h], xm_raw[1][h][:])
-        quantise(xm_ops[1], E4M3, slice(0, HALVES * P))
-        w0_back = psum.tile([P, CHUNKS, P], F32, name="w0_back", tag="bank3")
-        for c in range(CHUNKS):
-            nc.tensor.transpose(w0_back[:, c, :], w0_turned[:, c, :], ident[:])
-        new_w0 = keep.tile([P, N], F32, name="new_w0", tag="xm_raw11")
-        nc.scalar.activation(new_w0[:], w0_back[:].rearrange("p c s -> p (c s)"), COPY, scale=DW_FACTOR)
-        dw[3] = psum.tile([P, N], F32, name="dw3", tag="bank3")
-        dw[1] = psum.tile([P, N], F32, name="dw1", tag="bank7")
-        gradient(1)
-        gather_m(2)
-        finish(out_0, w_dst[0], 0, new_w0[:])
-
-        new_w1 = keep.tile([P, N], F32, name="new_w1", tag="xm1_grouped", align_bytes=64)
-        add(new_w1[:], w_cols[:, 1, :], scale_m(1, "m_term1"))
-        scale_dw(1)
-        add(new_w1[:], new_w1[:], dw_term[:, 1, :])
-        copy_dw(1)
-        new_m1 = keep.tile([P, N], F32, name="new_m1")
-        add(new_m1[:], m_cols[:, 1, :], dw_sb[:, 1, :])
-        gather_m(3)
-        finish(out_0, w_dst[1], 1, new_w1[:])
-
-        xm_ops.append(operand("xm23", grouped_tag="mid0"))
-        for h, cols in enumerate(column_halves):
-            weave_xm(xm_ops[2], cols, xm_last[h][:])
+        weave(nc.scalar.copy, g_op[1], y_sb[1], slice(0, G1_ON_SCALAR))
+        weave(nc.vector.tensor_copy, g_op[1], y_sb[1], slice(G1_ON_SCALAR, N))
+        quantise(g_op[0], E5M2)
+        quantise(g_op[1], E5M2)
+        dst, src = dealt_views(xm_op[0], xm_raw[0])
+        for pair in row_pairs:
+            nc.scalar.copy(out=dst[:, :, :, pair], in_=src[:, :, :, pair])
+        dst, src = dealt_views(xm_op[1], xm_raw[1])
+        for pair in row_pairs:
+            nc.vector.tensor_copy(out=dst[:, :, :, pair], in_=src[:, :, :, pair])
         for cols in column_halves:
-            quantise(xm_ops[2], E4M3, cols)
-        for b in (2, 3):
-            gradient(b)
-        add(w_cols[:, 2, :], w_cols[:, 2, :], scale_m(2, "rest0"))
-        m_dst[1] = keep.tile([P, T], F32, name="m_dst1", tag="rest1", align_bytes=64)
-        fill(m_dst[1], m_src[1])
-        finish(out_1, m_dst[1], 1, new_m1[:])
-        w_dst.append(keep.tile([P, T], F32, name="w_dst2", tag="xm_raw11"))
-        w_dst.append(keep.tile([P, T], F32, name="w_dst3", tag="mid0", align_bytes=64))
-        m_dst[2] = keep.tile([P, T], F32, name="m_dst2", tag="xm23_codes", align_bytes=64)
-        fill(w_dst[2], w_src[2])
-        scale_dw(2)
-        add(w_cols[:, 2, :], w_cols[:, 2, :], dw_term[:, 2, :])
-        copy_dw(2)
-        add(m_cols[:, 2, :], m_cols[:, 2, :], dw_sb[:, 2, :])
-        add(w_cols[:, 3, :], w_cols[:, 3, :], scale_m(3, "xm23_scales"))
-        scale_dw(3)
-        add(w_cols[:, 3, :], w_cols[:, 3, :], dw_term[:, 3, :])
-        finish(out_0, w_dst[2], 2, w_cols[:, 2, :])
-        fill(m_dst[2], m_src[2])
-        finish(out_1, m_dst[2], 2, m_cols[:, 2, :])
-        fill(w_dst[3], w_src[3])
-        finish(out_0, w_dst[3], 3, w_cols[:, 3, :])
-        copy_dw(3)
-        add(m_cols[:, 3, :], m_cols[:, 3, :], dw_sb[:, 3, :])
-        fill(m_dst[3], m_src[3])
-        finish(out_1, m_dst[3], 3, m_cols[:, 3, :])
+            for h in (1, 0):
+                quantise(xm_op[h], E4M3, cols)
+
+        dw = []
+        for t in range(PACK):
+            cols = slice(t * P, (t + 1) * P)
+            bank = psum.tile([P, N], F32, name="dw%d" % t, tag="bank%d" % t)
+            for h in (1, 0):
+                codes, scales = xm_op[h][1:]
+                nc.tensor.matmul_mx(
+                    out=bank[:], lhsT=codes[:, cols].bitcast(E4M3), lhsT_scale=scales[:, cols],
+                    rhs=g_op[h][1][:].bitcast(E5M2), rhs_scale=g_op[h][2][:],
+                    start=(h == 1), stop=(h == 0),
+                )
+            dw.append(bank)
+
+        m_terms = keep.tile([P, PACK, N], F32, name="m_terms", tag="x_raw0", align_bytes=256)
+        new_m = keep.tile([P, PACK, N], F32, name="new_m", tag="x_raw1", align_bytes=256)
+
+        for t in range(PACK):
+            if t == 0:
+                nc.vector.tensor_scalar(m_terms[:, t, :], m_src[t][:].indirect(offsets[:]), M_FACTOR, 0.0, MULT, ADD)
+                fill_on_scalar(m_dst[t], m_src[t])
+            else:
+                nc.scalar.activation(m_terms[:, t, :], m_src[t][:].indirect(offsets[:]), COPY, scale=m_scale[:])
+                nc.vector.tensor_copy(m_dst[t][:], m_src[t][:])
+            nc.vector.scalar_tensor_tensor(
+                out=new_m[:, t, :], in0=dw[t][:], scalar=M_FACTOR / BETA, in1=m_terms[:, t, :], op0=MULT, op1=ADD)
+            nc.vector.scalar_tensor_tensor(
+                out=w_cols[:, t, :], in0=dw[t][:], scalar=DW_FACTOR, in1=w_cols[:, t, :], op0=MULT, op1=ADD)
+            nc.scalar.activation(m_dst[t][:].indirect(offsets[:]), new_m[:, t, :], COPY, scale=new_m_scale[:])
+            nc.sync.dma_start(out=plane(out_1, t), in_=m_dst[t][:])
+            nc.vector.tensor_tensor(w_dst[t][:].indirect(offsets[:]), w_cols[:, t, :], m_terms[:, t, :], ADD)
+            nc.sync.dma_start(out=plane(out_0, t), in_=w_dst[t][:])

@@ -27,8 +27,10 @@ K = P * PACK
 HALVES = R // K
 BAND = 16
 
-X_ON_SCALAR = (40, 40)
-G1_ON_SCALAR = 160
+X_ON_SCALAR = (64, 64)
+W3_ON_SCALAR = 1280
+M1_ON_SCALAR = 1536
+M3_ON_SCALAR = 1024
 
 
 def tile_attend_gsq_nag_kernel(tc, xT, wT, y, wt, xm, mT, offs, out_0, out_1):
@@ -48,10 +50,11 @@ def tile_attend_gsq_nag_kernel(tc, xT, wT, y, wt, xm, mT, offs, out_0, out_1):
         def plane(table, t):
             return rows(table)[:, t, :]
 
-        def operand(name):
-            grouped = keep.tile([P, K * PACK], BF16, name=name + "_grouped", align_bytes=64)
-            codes = keep.tile([P, K], U32, name=name + "_codes", align_bytes=64)
-            scales = keep.tile([P, K], U8, name=name + "_scales", align_bytes=64)
+        def operand(name, columns=K, codes_tag=None, grouped=None):
+            if grouped is None:
+                grouped = keep.tile([P, columns * PACK], BF16, name=name + "_grouped", align_bytes=256)
+            codes = keep.tile([P, columns], U32, name=name + "_codes", tag=codes_tag or name + "_codes", align_bytes=256)
+            scales = keep.tile([P, columns], U8, name=name + "_scales", align_bytes=64)
             return grouped, codes, scales
 
         def quantise(op, fmt, cols=slice(0, K)):
@@ -76,7 +79,6 @@ def tile_attend_gsq_nag_kernel(tc, xT, wT, y, wt, xm, mT, offs, out_0, out_1):
         xm_raw = [keep.tile([P, PACK, D], F32, name="xm_raw%d" % h, align_bytes=256) for h in range(HALVES)]
         w_src = [keep.tile([P, T], F32, name="w_src%d" % t, tag="window%d" % t, align_bytes=256) for t in range(PACK)]
         w_dst = [keep.tile([P, T], F32, name="w_dst%d" % t, align_bytes=256) for t in range(PACK)]
-        m_dst = [keep.tile([P, T], F32, name="m_dst%d" % t, align_bytes=256) for t in range(PACK)]
         wt_rows = keep.tile([P, K], F32, name="wt_rows")
         wt_all = keep.tile([P, HALVES, PACK], F32, name="wt_sb")
         wt_sb = [wt_all[:, h, :] for h in range(HALVES)]
@@ -86,8 +88,8 @@ def tile_attend_gsq_nag_kernel(tc, xT, wT, y, wt, xm, mT, offs, out_0, out_1):
         m_scale = keep.tile([P, 1], F32, name="m_scale")
         new_m_scale = keep.tile([P, 1], F32, name="new_m_scale")
         nc.vector.memset(ones[:], 1.0)
-        nc.vector.tensor_scalar(m_scale[:], ones[:], M_FACTOR, 0.0, MULT, ADD)
         nc.vector.tensor_scalar(new_m_scale[:], ones[:], BETA / M_FACTOR, 0.0, MULT, ADD)
+        nc.vector.tensor_scalar(m_scale[:], ones[:], M_FACTOR, 0.0, MULT, ADD)
 
         nc.vector.memset(wt_rows[:], 0.0)
         nc.sync.dma_start(out=w_src[0][:], in_=plane(wT, 0))
@@ -103,11 +105,11 @@ def tile_attend_gsq_nag_kernel(tc, xT, wT, y, wt, xm, mT, offs, out_0, out_1):
         for h in range(HALVES):
             nc.sync.dma_start(out=xm_raw[h][:], in_=rows(xm[0, h * K : (h + 1) * K, :]))
 
-        w_cols = keep.tile([P, PACK, N], F32, name="w_cols")
+        w_pairs = [keep.tile([P, 2, N], F32, name="w_pair%d" % i, align_bytes=256) for i in range(2)]
+        w_cols = [w_pairs[t // 2][:, t % 2, :] for t in range(PACK)]
         w_op = operand("w")
         x_op = [operand("x%d" % h) for h in range(HALVES)]
         g_op = [operand("g%d" % h) for h in range(HALVES)]
-        xm_op = [operand("xm%d" % h) for h in range(HALVES)]
 
         def fill_on_scalar(dst, src):
             for part in (slice(0, T // 2), slice(T // 2, T)):
@@ -117,11 +119,21 @@ def tile_attend_gsq_nag_kernel(tc, xT, wT, y, wt, xm, mT, offs, out_0, out_1):
         for t in range(PACK):
             nc.tensor.transpose(wt_turned[:, t, :], wt_rows[:, t::PACK], ident[:])
         nc.scalar.copy(out=wt_all[:], in_=wt_turned[:, :, :: P // HALVES].rearrange("p t h -> p h t"))
-        for t in range(PACK):
-            nc.vector.tensor_copy(w_cols[:, t, :], w_src[t][:].indirect(offsets[:]))
+        def weave_w(i, part):
+            dst = w_op[0][:, PACK * part.start : PACK * part.stop].rearrange("p (c i t) -> p c t i", i=PACK, t=PACK)
+            src = w_pairs[i][:, :, part].rearrange("p t (c i) -> p c t i", i=PACK)
+            nc.vector.tensor_copy(out=dst[:, :, row_pairs[i], :], in_=src)
+
+        for t in range(PACK - 1):
+            nc.vector.tensor_copy(w_cols[t], w_src[t][:].indirect(offsets[:]))
             fill_on_scalar(w_dst[t], w_src[t])
+            if t == 1:
+                weave_w(0, slice(0, N))
+        first, second = (offsets[:, part.start // BAND : part.stop // BAND] for part in slot_halves)
+        nc.vector.tensor_copy(w_cols[3][:, slot_halves[0]], w_src[3][:].indirect(first))
+        nc.scalar.activation(w_cols[3][:, slot_halves[1]], w_src[3][:].indirect(second), COPY)
         for part in slot_halves:
-            weave(nc.vector.tensor_copy, w_op, w_cols, part)
+            weave_w(1, part)
         for part in slot_halves:
             quantise(w_op, E4M3, part)
         for h in range(HALVES):
@@ -129,9 +141,10 @@ def tile_attend_gsq_nag_kernel(tc, xT, wT, y, wt, xm, mT, offs, out_0, out_1):
             cut = X_ON_SCALAR[h]
             nc.scalar.copy(out=dst[:, : 2 * cut, :, row_pairs[1]], in_=src[:, : 2 * cut, :, row_pairs[1]])
             nc.vector.tensor_copy(out=dst[:, :, :, row_pairs[0]], in_=src[:, :, :, row_pairs[0]])
-            nc.vector.tensor_copy(out=dst[:, 2 * cut :, :, row_pairs[1]], in_=src[:, 2 * cut :, :, row_pairs[1]])
             for cols in column_halves:
                 quantise(x_op[h], E4M3, cols)
+        nc.scalar.activation(w_dst[3][:, :W3_ON_SCALAR], w_src[3][:, :W3_ON_SCALAR], COPY)
+        nc.vector.tensor_copy(w_dst[3][:, W3_ON_SCALAR:], w_src[3][:, W3_ON_SCALAR:])
 
         m_src = [keep.tile([P, T], F32, name="m_src%d" % t, tag="window%d" % t, align_bytes=256) for t in range(PACK)]
         for t in range(PACK):
@@ -164,54 +177,93 @@ def tile_attend_gsq_nag_kernel(tc, xT, wT, y, wt, xm, mT, offs, out_0, out_1):
                     in1=y_sb[h][:, t, part], op0=MULT, op1=SUB,
                 )
 
-        weigh_y(0, (0, 1, 2, 3))
+        weigh_y(0, (1, 3))
         residual(0, whole=2)
-        weigh_y(1, (1,))
+        weigh_y(1, (1, 3))
         for part in slot_halves:
             weave(nc.scalar.copy, g_op[0], y_sb[0], part)
         residual(1, whole=3)
-        weave(nc.scalar.copy, g_op[1], y_sb[1], slice(0, G1_ON_SCALAR))
-        weave(nc.vector.tensor_copy, g_op[1], y_sb[1], slice(G1_ON_SCALAR, N))
+        for part in slot_halves:
+            weave(nc.vector.tensor_copy, g_op[1], y_sb[1], part)
         quantise(g_op[0], E5M2)
         quantise(g_op[1], E5M2)
-        dst, src = dealt_views(xm_op[0], xm_raw[0])
-        for pair in row_pairs:
-            nc.scalar.copy(out=dst[:, :, :, pair], in_=src[:, :, :, pair])
-        dst, src = dealt_views(xm_op[1], xm_raw[1])
-        for pair in row_pairs:
-            nc.vector.tensor_copy(out=dst[:, :, :, pair], in_=src[:, :, :, pair])
-        for cols in column_halves:
-            for h in (1, 0):
-                quantise(xm_op[h], E4M3, cols)
+        xm_op = {}
 
-        dw = []
-        for t in range(PACK):
-            cols = slice(t * P, (t + 1) * P)
-            bank = psum.tile([P, N], F32, name="dw%d" % t, tag="bank%d" % t)
-            for h in (1, 0):
-                codes, scales = xm_op[h][1:]
+        def prepare_xm(copy, h, i, codes_tag=None, grouped=None):
+            op = operand("xm%d%d" % (h, i), K // 2, codes_tag, grouped)
+            dst = op[0][:].rearrange("p (t m j) -> p m j t", t=2, j=PACK)
+            src = xm_raw[h][:].rearrange("p j (m t) -> p m j t", t=PACK)
+            copy(out=dst, in_=src[:, :, :, row_pairs[i]])
+            quantise(op, E4M3, slice(0, K // 2))
+            xm_op[h, i] = op
+
+        prepare_xm(nc.scalar.copy, 0, 0)
+        prepare_xm(nc.vector.tensor_copy, 1, 0)
+        prepare_xm(nc.scalar.copy, 0, 1, "xm10_grouped")
+
+        dw = {}
+
+        def gradient(t, order):
+            cols = slice(t % 2 * P, (t % 2 + 1) * P)
+            dw[t] = psum.tile([P, N], F32, name="dw%d" % t, tag="bank%d" % t)
+            for h in order:
+                codes, scales = xm_op[h, t // 2][1:]
                 nc.tensor.matmul_mx(
-                    out=bank[:], lhsT=codes[:, cols].bitcast(E4M3), lhsT_scale=scales[:, cols],
+                    out=dw[t][:], lhsT=codes[:, cols].bitcast(E4M3), lhsT_scale=scales[:, cols],
                     rhs=g_op[h][1][:].bitcast(E5M2), rhs_scale=g_op[h][2][:],
-                    start=(h == 1), stop=(h == 0),
+                    start=(h == order[0]), stop=(h == order[1]),
                 )
-            dw.append(bank)
 
-        m_terms = keep.tile([P, PACK, N], F32, name="m_terms", tag="x_raw0", align_bytes=256)
-        new_m = keep.tile([P, PACK, N], F32, name="new_m", tag="x_raw1", align_bytes=256)
+        gradient(0, (0, 1))
+        gradient(1, (1, 0))
 
-        for t in range(PACK):
-            if t == 0:
-                nc.vector.tensor_scalar(m_terms[:, t, :], m_src[t][:].indirect(offsets[:]), M_FACTOR, 0.0, MULT, ADD)
-                fill_on_scalar(m_dst[t], m_src[t])
-            else:
-                nc.scalar.activation(m_terms[:, t, :], m_src[t][:].indirect(offsets[:]), COPY, scale=m_scale[:])
-                nc.vector.tensor_copy(m_dst[t][:], m_src[t][:])
+        def values(name, tag=None):
+            return keep.tile([P, N], F32, name=name, tag=tag or name, align_bytes=256)[:]
+
+        def table_tile(name, tag):
+            return keep.tile([P, T], F32, name=name, tag=tag, align_bytes=256)
+
+        def gather_m(m_term, t):
+            nc.scalar.activation(m_term, m_src[t][:].indirect(offsets[:]), COPY, scale=m_scale[:])
+
+        def update_w(t, step, m_term):
+            nc.vector.scalar_tensor_tensor(out=step, in0=dw[t][:], scalar=DW_FACTOR, in1=m_term, op0=MULT, op1=ADD)
             nc.vector.scalar_tensor_tensor(
-                out=new_m[:, t, :], in0=dw[t][:], scalar=M_FACTOR / BETA, in1=m_terms[:, t, :], op0=MULT, op1=ADD)
-            nc.vector.scalar_tensor_tensor(
-                out=w_cols[:, t, :], in0=dw[t][:], scalar=DW_FACTOR, in1=w_cols[:, t, :], op0=MULT, op1=ADD)
-            nc.scalar.activation(m_dst[t][:].indirect(offsets[:]), new_m[:, t, :], COPY, scale=new_m_scale[:])
-            nc.sync.dma_start(out=plane(out_1, t), in_=m_dst[t][:])
-            nc.vector.tensor_tensor(w_dst[t][:].indirect(offsets[:]), w_cols[:, t, :], m_terms[:, t, :], ADD)
+                out=m_term, in0=dw[t][:], scalar=M_FACTOR / BETA, in1=m_term, op0=MULT, op1=ADD)
+            nc.vector.tensor_tensor(w_dst[t][:].indirect(offsets[:]), w_cols[t], step, ADD)
             nc.sync.dma_start(out=plane(out_0, t), in_=w_dst[t][:])
+
+        def update_m(t, dst, new):
+            nc.scalar.activation(dst[:].indirect(offsets[:]), new, COPY, scale=new_m_scale[:])
+            nc.sync.dma_start(out=plane(out_1, t), in_=dst[:])
+
+        m_dst2 = table_tile("m_dst2", "m_dst2")
+        nc.sync.dma_start(out=m_dst2[:], in_=plane(mT, 2))
+        m_dst3 = table_tile("m_dst3", "m_dst3")
+        nc.sync.dma_start(out=m_dst3[:, M3_ON_SCALAR:], in_=plane(mT, 3)[:, M3_ON_SCALAR:])
+        m_term0 = values("m_term0", "xm_raw0")
+        gather_m(m_term0, 0)
+        m_dst0 = table_tile("m_dst0", "xm01_grouped")
+        nc.vector.tensor_copy(m_dst0[:], m_src[0][:])
+        update_w(0, values("step0"), m_term0)
+        shared = keep.tile([P, 2, N], F32, name="shared", tag="window0", align_bytes=256)
+        prepare_xm(nc.scalar.copy, 1, 1, grouped=shared[:, 0, :].bitcast(BF16))
+        for t in (2, 3):
+            gradient(t, (1, 0))
+        m_term1 = shared[:, 1, :]
+        gather_m(m_term1, 1)
+        update_m(0, m_dst0, m_term0)
+        m_dst1 = table_tile("m_dst1", "step0")
+        nc.scalar.activation(m_dst1[:, :M1_ON_SCALAR], m_src[1][:, :M1_ON_SCALAR], COPY)
+        nc.vector.tensor_copy(m_dst1[:, M1_ON_SCALAR:], m_src[1][:, M1_ON_SCALAR:])
+        update_w(1, w_cols[0], m_term1)
+        m_term2 = values("m_term2", "window1")
+        gather_m(m_term2, 2)
+        update_m(1, m_dst1, m_term1)
+        update_w(2, w_cols[1], m_term2)
+        m_term3 = w_cols[0]
+        gather_m(m_term3, 3)
+        update_m(2, m_dst2, m_term2)
+        update_w(3, w_cols[2], m_term3)
+        nc.scalar.activation(m_dst3[:, :M3_ON_SCALAR], m_src[3][:, :M3_ON_SCALAR], COPY)
+        update_m(3, m_dst3, m_term3)

@@ -29,8 +29,6 @@ BAND = 16
 
 X_ON_SCALAR = (64, 64)
 W3_ON_SCALAR = 1280
-M1_ON_SCALAR = 1536
-M3_ON_SCALAR = 1024
 
 
 def tile_attend_gsq_nag_kernel(tc, xT, wT, y, wt, xm, mT, offs, out_0, out_1):
@@ -226,10 +224,10 @@ def tile_attend_gsq_nag_kernel(tc, xT, wT, y, wt, xm, mT, offs, out_0, out_1):
         def gather_m(m_term, t):
             nc.scalar.activation(m_term, m_src[t][:].indirect(offsets[:]), COPY, scale=m_scale[:])
 
-        def update_w(t, step, m_term):
+        def update_w(t, step, new_m, m_term):
             nc.vector.scalar_tensor_tensor(out=step, in0=dw[t][:], scalar=DW_FACTOR, in1=m_term, op0=MULT, op1=ADD)
             nc.vector.scalar_tensor_tensor(
-                out=m_term, in0=dw[t][:], scalar=M_FACTOR / BETA, in1=m_term, op0=MULT, op1=ADD)
+                out=new_m, in0=dw[t][:], scalar=M_FACTOR / BETA, in1=m_term, op0=MULT, op1=ADD)
             nc.vector.tensor_tensor(w_dst[t][:].indirect(offsets[:]), w_cols[t], step, ADD)
             nc.sync.dma_start(out=plane(out_0, t), in_=w_dst[t][:])
 
@@ -239,31 +237,28 @@ def tile_attend_gsq_nag_kernel(tc, xT, wT, y, wt, xm, mT, offs, out_0, out_1):
 
         m_dst2 = table_tile("m_dst2", "m_dst2")
         nc.sync.dma_start(out=m_dst2[:], in_=plane(mT, 2))
-        m_dst3 = table_tile("m_dst3", "m_dst3")
-        nc.sync.dma_start(out=m_dst3[:, M3_ON_SCALAR:], in_=plane(mT, 3)[:, M3_ON_SCALAR:])
         m_term0 = values("m_term0", "xm_raw0")
+        new_m = [values("new_m%d" % t) for t in range(PACK)]
         gather_m(m_term0, 0)
         m_dst0 = table_tile("m_dst0", "xm01_grouped")
         nc.vector.tensor_copy(m_dst0[:], m_src[0][:])
-        update_w(0, values("step0"), m_term0)
+        update_w(0, values("step0"), new_m[0], m_term0)
         shared = keep.tile([P, 2, N], F32, name="shared", tag="window0", align_bytes=256)
         prepare_xm(nc.scalar.copy, 1, 1, grouped=shared[:, 0, :].bitcast(BF16))
+        m_term1 = shared[:, 1, :]
         for t in (2, 3):
             gradient(t, (1, 0))
-        m_term1 = shared[:, 1, :]
         gather_m(m_term1, 1)
-        update_m(0, m_dst0, m_term0)
+        update_m(0, m_dst0, new_m[0])
         m_dst1 = table_tile("m_dst1", "step0")
-        nc.scalar.activation(m_dst1[:, :M1_ON_SCALAR], m_src[1][:, :M1_ON_SCALAR], COPY)
-        nc.vector.tensor_copy(m_dst1[:, M1_ON_SCALAR:], m_src[1][:, M1_ON_SCALAR:])
-        update_w(1, w_cols[0], m_term1)
-        m_term2 = values("m_term2", "window1")
-        gather_m(m_term2, 2)
-        update_m(1, m_dst1, m_term1)
-        update_w(2, w_cols[1], m_term2)
-        m_term3 = w_cols[0]
-        gather_m(m_term3, 3)
-        update_m(2, m_dst2, m_term2)
-        update_w(3, w_cols[2], m_term3)
-        nc.scalar.activation(m_dst3[:, :M3_ON_SCALAR], m_src[3][:, :M3_ON_SCALAR], COPY)
-        update_m(3, m_dst3, m_term3)
+        nc.vector.tensor_copy(m_dst1[:], m_src[1][:])
+        update_w(1, values("step1"), new_m[1], m_term1)
+        gather_m(m_term0, 2)
+        update_m(1, m_dst1, new_m[1])
+        update_w(2, values("step2"), new_m[2], m_term0)
+        gather_m(m_term1, 3)
+        update_m(2, m_dst2, new_m[2])
+        m_dst3 = table_tile("m_dst3", "new_m2")
+        nc.scalar.activation(m_dst3[:], m_src[3][:], COPY)
+        update_w(3, values("step3"), new_m[3], m_term1)
+        update_m(3, m_dst3, new_m[3])

@@ -28,7 +28,6 @@ HALVES = R // K
 BAND = 16
 
 X_ON_SCALAR = (64, 64)
-W3_ON_SCALAR = 1280
 
 
 def tile_attend_gsq_nag_kernel(tc, xT, wT, y, wt, xm, mT, offs, out_0, out_1):
@@ -141,8 +140,7 @@ def tile_attend_gsq_nag_kernel(tc, xT, wT, y, wt, xm, mT, offs, out_0, out_1):
             nc.vector.tensor_copy(out=dst[:, :, :, row_pairs[0]], in_=src[:, :, :, row_pairs[0]])
             for cols in column_halves:
                 quantise(x_op[h], E4M3, cols)
-        nc.scalar.activation(w_dst[3][:, :W3_ON_SCALAR], w_src[3][:, :W3_ON_SCALAR], COPY)
-        nc.vector.tensor_copy(w_dst[3][:, W3_ON_SCALAR:], w_src[3][:, W3_ON_SCALAR:])
+        fill_on_scalar(w_dst[3], w_src[3])
 
         m_src = [keep.tile([P, T], F32, name="m_src%d" % t, tag="window%d" % t, align_bytes=256) for t in range(PACK)]
         for t in range(PACK):
@@ -175,7 +173,7 @@ def tile_attend_gsq_nag_kernel(tc, xT, wT, y, wt, xm, mT, offs, out_0, out_1):
                     in1=y_sb[h][:, t, part], op0=MULT, op1=SUB,
                 )
 
-        weigh_y(0, (1, 3))
+        weigh_y(0, (0, 1, 2, 3))
         residual(0, whole=2)
         weigh_y(1, (1, 3))
         for part in slot_halves:

@@ -26,6 +26,7 @@ PACK = 4
 K = P * PACK
 HALVES = R // K
 BAND = 16
+M_COPIED = (1920, 1920, 0)
 
 X_ON_SCALAR = (64, 64)
 
@@ -143,8 +144,12 @@ def tile_attend_gsq_nag_kernel(tc, xT, wT, y, wt, xm, mT, offs, out_0, out_1):
         fill_on_scalar(w_dst[3], w_src[3])
 
         m_src = [keep.tile([P, T], F32, name="m_src%d" % t, tag="window%d" % t, align_bytes=256) for t in range(PACK)]
+        m_dst = [keep.tile([P, T], F32, name="m_dst%d" % t, align_bytes=256) for t in range(3)]
         for t in range(PACK):
             nc.sync.dma_start(out=m_src[t][:], in_=plane(mT, t))
+            if t > 0:
+                late = slice(M_COPIED[t - 1], T)
+                nc.sync.dma_start(out=m_dst[t - 1][:, late], in_=plane(mT, t - 1)[:, late])
 
         def weigh_y(h, on_scalar):
             for t in range(PACK):
@@ -233,13 +238,10 @@ def tile_attend_gsq_nag_kernel(tc, xT, wT, y, wt, xm, mT, offs, out_0, out_1):
             nc.scalar.activation(dst[:].indirect(offsets[:]), new, COPY, scale=new_m_scale[:])
             nc.sync.dma_start(out=plane(out_1, t), in_=dst[:])
 
-        m_dst2 = table_tile("m_dst2", "m_dst2")
-        nc.sync.dma_start(out=m_dst2[:], in_=plane(mT, 2))
         m_term0 = values("m_term0", "xm_raw0")
         new_m = [values("new_m%d" % t) for t in range(PACK)]
         gather_m(m_term0, 0)
-        m_dst0 = table_tile("m_dst0", "xm01_grouped")
-        nc.vector.tensor_copy(m_dst0[:], m_src[0][:])
+        nc.vector.tensor_copy(m_dst[0][:, : M_COPIED[0]], m_src[0][:, : M_COPIED[0]])
         update_w(0, values("step0"), new_m[0], m_term0)
         shared = keep.tile([P, 2, N], F32, name="shared", tag="window0", align_bytes=256)
         prepare_xm(nc.scalar.copy, 1, 1, grouped=shared[:, 0, :].bitcast(BF16))
@@ -247,15 +249,14 @@ def tile_attend_gsq_nag_kernel(tc, xT, wT, y, wt, xm, mT, offs, out_0, out_1):
         for t in (2, 3):
             gradient(t, (1, 0))
         gather_m(m_term1, 1)
-        update_m(0, m_dst0, new_m[0])
-        m_dst1 = table_tile("m_dst1", "step0")
-        nc.vector.tensor_copy(m_dst1[:], m_src[1][:])
+        update_m(0, m_dst[0], new_m[0])
+        nc.vector.tensor_copy(m_dst[1][:, : M_COPIED[1]], m_src[1][:, : M_COPIED[1]])
         update_w(1, values("step1"), new_m[1], m_term1)
         gather_m(m_term0, 2)
-        update_m(1, m_dst1, new_m[1])
+        update_m(1, m_dst[1], new_m[1])
         update_w(2, values("step2"), new_m[2], m_term0)
         gather_m(m_term1, 3)
-        update_m(2, m_dst2, new_m[2])
+        update_m(2, m_dst[2], new_m[2])
         m_dst3 = table_tile("m_dst3", "new_m2")
         nc.scalar.activation(m_dst3[:], m_src[3][:], COPY)
         update_w(3, values("step3"), new_m[3], m_term1)

@@ -27,6 +27,7 @@ K = P * PACK
 HALVES = R // K
 BAND = 16
 M_COPIED = (1920, 1920, 0)
+M0_ON_SCALAR = 640
 
 X_ON_SCALAR = (64, 64)
 
@@ -48,9 +49,8 @@ def tile_attend_gsq_nag_kernel(tc, xT, wT, y, wt, xm, mT, offs, out_0, out_1):
         def plane(table, t):
             return rows(table)[:, t, :]
 
-        def operand(name, columns=K, codes_tag=None, grouped=None):
-            if grouped is None:
-                grouped = keep.tile([P, columns * PACK], BF16, name=name + "_grouped", align_bytes=256)
+        def operand(name, columns=K, codes_tag=None):
+            grouped = keep.tile([P, columns * PACK], BF16, name=name + "_grouped", align_bytes=256)
             codes = keep.tile([P, columns], U32, name=name + "_codes", tag=codes_tag or name + "_codes", align_bytes=256)
             scales = keep.tile([P, columns], U8, name=name + "_scales", align_bytes=64)
             return grouped, codes, scales
@@ -190,8 +190,8 @@ def tile_attend_gsq_nag_kernel(tc, xT, wT, y, wt, xm, mT, offs, out_0, out_1):
         quantise(g_op[1], E5M2)
         xm_op = {}
 
-        def prepare_xm(copy, h, i, codes_tag=None, grouped=None):
-            op = operand("xm%d%d" % (h, i), K // 2, codes_tag, grouped)
+        def prepare_xm(copy, h, i, codes_tag=None):
+            op = operand("xm%d%d" % (h, i), K // 2, codes_tag)
             dst = op[0][:].rearrange("p (t m j) -> p m j t", t=2, j=PACK)
             src = xm_raw[h][:].rearrange("p j (m t) -> p m j t", t=PACK)
             copy(out=dst, in_=src[:, :, :, row_pairs[i]])
@@ -201,6 +201,7 @@ def tile_attend_gsq_nag_kernel(tc, xT, wT, y, wt, xm, mT, offs, out_0, out_1):
         prepare_xm(nc.scalar.copy, 0, 0)
         prepare_xm(nc.vector.tensor_copy, 1, 0)
         prepare_xm(nc.scalar.copy, 0, 1, "xm10_grouped")
+        prepare_xm(nc.scalar.copy, 1, 1)
 
         dw = {}
 
@@ -215,8 +216,8 @@ def tile_attend_gsq_nag_kernel(tc, xT, wT, y, wt, xm, mT, offs, out_0, out_1):
                     start=(h == order[0]), stop=(h == order[1]),
                 )
 
-        gradient(0, (0, 1))
-        gradient(1, (1, 0))
+        for t in range(PACK):
+            gradient(t, (1, 0) if t == 1 else (0, 1))
 
         def values(name, tag=None):
             return keep.tile([P, N], F32, name=name, tag=tag or name, align_bytes=256)[:]
@@ -238,16 +239,13 @@ def tile_attend_gsq_nag_kernel(tc, xT, wT, y, wt, xm, mT, offs, out_0, out_1):
             nc.scalar.activation(dst[:].indirect(offsets[:]), new, COPY, scale=new_m_scale[:])
             nc.sync.dma_start(out=plane(out_1, t), in_=dst[:])
 
-        m_term0 = values("m_term0", "xm_raw0")
+        m_term0 = values("m_term0", "xm_raw1")
         new_m = [values("new_m%d" % t) for t in range(PACK)]
         gather_m(m_term0, 0)
-        nc.vector.tensor_copy(m_dst[0][:, : M_COPIED[0]], m_src[0][:, : M_COPIED[0]])
+        nc.scalar.activation(m_dst[0][:, :M0_ON_SCALAR], m_src[0][:, :M0_ON_SCALAR], COPY)
+        nc.vector.tensor_copy(m_dst[0][:, M0_ON_SCALAR : M_COPIED[0]], m_src[0][:, M0_ON_SCALAR : M_COPIED[0]])
         update_w(0, values("step0"), new_m[0], m_term0)
-        shared = keep.tile([P, 2, N], F32, name="shared", tag="window0", align_bytes=256)
-        prepare_xm(nc.scalar.copy, 1, 1, grouped=shared[:, 0, :].bitcast(BF16))
-        m_term1 = shared[:, 1, :]
-        for t in (2, 3):
-            gradient(t, (1, 0))
+        m_term1 = values("m_term1", "window0")
         gather_m(m_term1, 1)
         update_m(0, m_dst[0], new_m[0])
         nc.vector.tensor_copy(m_dst[1][:, : M_COPIED[1]], m_src[1][:, : M_COPIED[1]])

@@ -26,7 +26,7 @@ PACK = 4
 K = P * PACK
 HALVES = R // K
 BAND = 16
-M_COPIED = (1920, 1920, 0)
+M_COPIED = (1984, 1088, 1024)
 M0_ON_SCALAR = 640
 
 X_ON_SCALAR = (64, 64)
@@ -252,6 +252,7 @@ def tile_attend_gsq_nag_kernel(tc, xT, wT, y, wt, xm, mT, offs, out_0, out_1):
         update_w(1, values("step1"), new_m[1], m_term1)
         gather_m(m_term0, 2)
         update_m(1, m_dst[1], new_m[1])
+        nc.vector.tensor_copy(m_dst[2][:, : M_COPIED[2]], m_src[2][:, : M_COPIED[2]])
         update_w(2, values("step2"), new_m[2], m_term0)
         gather_m(m_term1, 3)
         update_m(2, m_dst[2], new_m[2])

from contextlib import ExitStack

import concourse.mybir as mybir
from concourse.masks import make_identity

D, T, N, R = 512, 2048, 512, 1024
LR, BETA = 0.1, 0.9
DW_FACTOR = -LR * (1.0 + BETA)
M_FACTOR = -LR * BETA * BETA
FLOPS = 2 * 2 * D * N * R

F32 = mybir.dt.float32
BF16 = mybir.dt.bfloat16
U32 = mybir.dt.uint32
U16 = mybir.dt.uint16
U8 = mybir.dt.uint8
E4M3 = mybir.dt.float8_e4m3fn_x4
E5M2 = mybir.dt.float8_e5m2_x4
MULT = mybir.AluOpType.mult
ADD = mybir.AluOpType.add
SUB = mybir.AluOpType.subtract
COPY = mybir.ActivationFunctionType.Copy

P = 128
PACK = 4
K = P * PACK
HALVES = R // K
BAND = 16
M_COPIED = (1984, 1088, 1024)
M0_ON_SCALAR = 640

X_ON_SCALAR = (64, 64)


def tile_attend_gsq_nag_kernel(tc, xT, wT, y, wt, xm, mT, offs, out_0, out_1):
    nc = tc.nc
    with ExitStack() as ctx:
        lists = ctx.enter_context(tc.tile_pool(name="lists", bufs=1))
        keep = ctx.enter_context(tc.tile_pool(name="keep", bufs=1))
        psum = ctx.enter_context(tc.psum_pool(name="psum", bufs=1))

        slot_halves = (slice(0, N // 2), slice(N // 2, N))
        column_halves = (slice(0, K // 2), slice(K // 2, K))
        row_pairs = (slice(0, PACK // 2), slice(PACK // 2, PACK))

        def rows(src):
            return src.rearrange("(p j) c -> p j c", j=PACK)

        def plane(table, t):
            return rows(table)[:, t, :]

        def operand(name, columns=K, codes_tag=None):
            grouped = keep.tile([P, columns * PACK], BF16, name=name + "_grouped", align_bytes=256)
            codes = keep.tile([P, columns], U32, name=name + "_codes", tag=codes_tag or name + "_codes", align_bytes=256)
            scales = keep.tile([P, columns], U8, name=name + "_scales", align_bytes=64)
            return grouped, codes, scales

        def quantise(op, fmt, cols=slice(0, K)):
            grouped, codes, scales = op
            nc.vector.quantize_mx(
                out=codes[:, cols].bitcast(fmt), scales=scales[:, cols],
                in_=grouped[:, PACK * cols.start : PACK * cols.stop])

        def weave(copy, op, four_rows, cols):
            dst = op[0][:, PACK * cols.start : PACK * cols.stop].rearrange("p (c i t) -> p c t i", i=PACK, t=PACK)
            src = four_rows[:, :, cols].rearrange("p t (c i) -> p c t i", i=PACK)
            copy(out=dst, in_=src)

        def dealt_views(op, raw):
            dst = op[0][:].rearrange("p (t m j) -> p m j t", t=PACK, j=PACK)
            src = raw[:].rearrange("p j (m t) -> p m j t", t=PACK)
            return dst, src

        offsets = lists.tile([P, N // BAND], U16, name="offsets")
        x_raw = [keep.tile([P, PACK, K], F32, name="x_raw%d" % h, align_bytes=256) for h in range(HALVES)]
        y_sb = [keep.tile([P, PACK, N], F32, name="y_sb%d" % h, align_bytes=256) for h in range(HALVES)]
        xm_raw = [keep.tile([P, PACK, D], F32, name="xm_raw%d" % h, align_bytes=256) for h in range(HALVES)]
        w_src = [keep.tile([P, T], F32, name="w_src%d" % t, tag="window%d" % t, align_bytes=256) for t in range(PACK)]
        w_dst = [keep.tile([P, T], F32, name="w_dst%d" % t, align_bytes=256) for t in range(PACK)]
        wt_rows = keep.tile([P, K], F32, name="wt_rows")
        wt_all = keep.tile([P, HALVES, PACK], F32, name="wt_sb")
        wt_sb = [wt_all[:, h, :] for h in range(HALVES)]
        ident = keep.tile([P, P], F32, name="ident")
        make_identity(nc, ident[:])
        ones = keep.tile([P, 1], F32, name="ones")
        m_scale = keep.tile([P, 1], F32, name="m_scale")
        new_m_scale = keep.tile([P, 1], F32, name="new_m_scale")
        nc.vector.memset(ones[:], 1.0)
        nc.vector.tensor_scalar(new_m_scale[:], ones[:], BETA / M_FACTOR, 0.0, MULT, ADD)
        nc.vector.tensor_scalar(m_scale[:], ones[:], M_FACTOR, 0.0, MULT, ADD)

        nc.vector.memset(wt_rows[:], 0.0)
        nc.sync.dma_start(out=w_src[0][:], in_=plane(wT, 0))
        nc.sync.dma_start(offsets[:], offs)
        nc.sync.dma_start(out=wt_rows[:: P // HALVES, :], in_=wt[0].rearrange("(h k) o -> h (k o)", h=HALVES))
        for t in range(1, PACK):
            nc.sync.dma_start(out=w_src[t][:], in_=plane(wT, t))
        for h in range(HALVES):
            nc.sync.dma_start(out=x_raw[h][:], in_=rows(xT[0, :, h * K : (h + 1) * K]))
        for h in range(HALVES):
            for part in row_pairs:
                nc.sync.dma_start(out=y_sb[h][:, part, :], in_=rows(y[0, h * K : (h + 1) * K, :])[:, part, :])
        for h in range(HALVES):
            nc.sync.dma_start(out=xm_raw[h][:], in_=rows(xm[0, h * K : (h + 1) * K, :]))

        w_pairs = [keep.tile([P, 2, N], F32, name="w_pair%d" % i, align_bytes=256) for i in range(2)]
        w_cols = [w_pairs[t // 2][:, t % 2, :] for t in range(PACK)]
        w_op = operand("w")
        x_op = [operand("x%d" % h) for h in range(HALVES)]
        g_op = [operand("g%d" % h) for h in range(HALVES)]

        def fill_on_scalar(dst, src):
            for part in (slice(0, T // 2), slice(T // 2, T)):
                nc.scalar.activation(dst[:, part], src[:, part], COPY)

        wt_turned = psum.tile([P, PACK, P], F32, name="wt_turned", tag="bank7")
        for t in range(PACK):
            nc.tensor.transpose(wt_turned[:, t, :], wt_rows[:, t::PACK], ident[:])
        nc.scalar.copy(out=wt_all[:], in_=wt_turned[:, :, :: P // HALVES].rearrange("p t h -> p h t"))
        def weave_w(i, part):
            dst = w_op[0][:, PACK * part.start : PACK * part.stop].rearrange("p (c i t) -> p c t i", i=PACK, t=PACK)
            src = w_pairs[i][:, :, part].rearrange("p t (c i) -> p c t i", i=PACK)
            nc.vector.tensor_copy(out=dst[:, :, row_pairs[i], :], in_=src)

        for t in range(PACK - 1):
            nc.vector.tensor_copy(w_cols[t], w_src[t][:].indirect(offsets[:]))
            fill_on_scalar(w_dst[t], w_src[t])
            if t == 1:
                weave_w(0, slice(0, N))
        first, second = (offsets[:, part.start // BAND : part.stop // BAND] for part in slot_halves)
        nc.vector.tensor_copy(w_cols[3][:, slot_halves[0]], w_src[3][:].indirect(first))
        nc.scalar.activation(w_cols[3][:, slot_halves[1]], w_src[3][:].indirect(second), COPY)
        for part in slot_halves:
            weave_w(1, part)
        for part in slot_halves:
            quantise(w_op, E4M3, part)
        for h in range(HALVES):
            dst, src = dealt_views(x_op[h], x_raw[h])
            cut = X_ON_SCALAR[h]
            nc.scalar.copy(out=dst[:, : 2 * cut, :, row_pairs[1]], in_=src[:, : 2 * cut, :, row_pairs[1]])
            nc.vector.tensor_copy(out=dst[:, :, :, row_pairs[0]], in_=src[:, :, :, row_pairs[0]])
            for cols in column_halves:
                quantise(x_op[h], E4M3, cols)
        fill_on_scalar(w_dst[3], w_src[3])

        m_src = [keep.tile([P, T], F32, name="m_src%d" % t, tag="window%d" % t, align_bytes=256) for t in range(PACK)]
        m_dst = [keep.tile([P, T], F32, name="m_dst%d" % t, align_bytes=256) for t in range(3)]
        for t in range(PACK):
            nc.sync.dma_start(out=m_src[t][:], in_=plane(mT, t))
            if t > 0:
                late = slice(M_COPIED[t - 1], T)
                nc.sync.dma_start(out=m_dst[t - 1][:, late], in_=plane(mT, t - 1)[:, late])

        def weigh_y(h, on_scalar):
            for t in range(PACK):
                if t in on_scalar:
                    nc.scalar.activation(y_sb[h][:, t, :], y_sb[h][:, t, :], COPY, scale=wt_sb[h][:, t : t + 1])
                else:
                    nc.gpsimd.tensor_scalar(
                        y_sb[h][:, t, :], y_sb[h][:, t, :], wt_sb[h][:, t : t + 1], 0.0, MULT, ADD)

        def residual(h, whole):
            codes, scales = x_op[h][1:]
            banks = []
            for t in range(PACK):
                cols = slice(t * P, (t + 1) * P)
                a = psum.tile([P, N], F32, name="a%d%d" % (h, t), tag="bank%d" % (PACK * h + t))
                nc.tensor.matmul_mx(
                    out=a[:], lhsT=codes[:, cols].bitcast(E4M3), lhsT_scale=scales[:, cols],
                    rhs=w_op[1][:].bitcast(E4M3), rhs_scale=w_op[2][:], start=True, stop=True,
                )
                banks.append(a)
            steps = [(t, slice(0, N)) for t in range(whole)]
            steps.extend((t, part) for part in slot_halves for t in range(whole, PACK))
            for t, part in steps:
                nc.vector.scalar_tensor_tensor(
                    out=y_sb[h][:, t, part], in0=banks[t][:, part], scalar=wt_sb[h][:, t : t + 1],
                    in1=y_sb[h][:, t, part], op0=MULT, op1=SUB,
                )

        weigh_y(0, (0, 1, 2, 3))
        residual(0, whole=2)
        weigh_y(1, (1, 3))
        for part in slot_halves:
            weave(nc.scalar.copy, g_op[0], y_sb[0], part)
        residual(1, whole=3)
        for part in slot_halves:
            weave(nc.vector.tensor_copy, g_op[1], y_sb[1], part)
        quantise(g_op[0], E5M2)
        quantise(g_op[1], E5M2)
        xm_op = {}

        def prepare_xm(copy, h, i, codes_tag=None):
            op = operand("xm%d%d" % (h, i), K // 2, codes_tag)
            dst = op[0][:].rearrange("p (t m j) -> p m j t", t=2, j=PACK)
            src = xm_raw[h][:].rearrange("p j (m t) -> p m j t", t=PACK)
            copy(out=dst, in_=src[:, :, :, row_pairs[i]])
            quantise(op, E4M3, slice(0, K // 2))
            xm_op[h, i] = op

        prepare_xm(nc.scalar.copy, 0, 0)
        prepare_xm(nc.vector.tensor_copy, 1, 0)
        prepare_xm(nc.scalar.copy, 0, 1, "xm10_grouped")
        prepare_xm(nc.scalar.copy, 1, 1)

        dw = {}

        def gradient(t, order):
            cols = slice(t % 2 * P, (t % 2 + 1) * P)
            dw[t] = psum.tile([P, N], F32, name="dw%d" % t, tag="bank%d" % t)
            for h in order:
                codes, scales = xm_op[h, t // 2][1:]
                nc.tensor.matmul_mx(
                    out=dw[t][:], lhsT=codes[:, cols].bitcast(E4M3), lhsT_scale=scales[:, cols],
                    rhs=g_op[h][1][:].bitcast(E5M2), rhs_scale=g_op[h][2][:],
                    start=(h == order[0]), stop=(h == order[1]),
                )

        for t in range(PACK):
            gradient(t, (1, 0) if t == 1 else (0, 1))

        def values(name, tag=None):
            return keep.tile([P, N], F32, name=name, tag=tag or name, align_bytes=256)[:]

        def table_tile(name, tag):
            return keep.tile([P, T], F32, name=name, tag=tag, align_bytes=256)

        def gather_m(m_term, t):
            nc.scalar.activation(m_term, m_src[t][:].indirect(offsets[:]), COPY, scale=m_scale[:])

        def update_w(t, step, new_m, m_term):
            nc.vector.scalar_tensor_tensor(out=step, in0=dw[t][:], scalar=DW_FACTOR, in1=m_term, op0=MULT, op1=ADD)
            nc.vector.scalar_tensor_tensor(
                out=new_m, in0=dw[t][:], scalar=M_FACTOR / BETA, in1=m_term, op0=MULT, op1=ADD)
            nc.vector.tensor_tensor(w_dst[t][:].indirect(offsets[:]), w_cols[t], step, ADD)
            nc.sync.dma_start(out=plane(out_0, t), in_=w_dst[t][:])

        def update_m(t, dst, new):
            nc.scalar.activation(dst[:].indirect(offsets[:]), new, COPY, scale=new_m_scale[:])
            nc.sync.dma_start(out=plane(out_1, t), in_=dst[:])

        m_term0 = values("m_term0", "xm_raw1")
        new_m = [values("new_m%d" % t) for t in range(PACK)]
        gather_m(m_term0, 0)
        nc.scalar.activation(m_dst[0][:, :M0_ON_SCALAR], m_src[0][:, :M0_ON_SCALAR], COPY)
        nc.vector.tensor_copy(m_dst[0][:, M0_ON_SCALAR : M_COPIED[0]], m_src[0][:, M0_ON_SCALAR : M_COPIED[0]])
        update_w(0, values("step0"), new_m[0], m_term0)
        m_term1 = values("m_term1", "window0")
        gather_m(m_term1, 1)
        update_m(0, m_dst[0], new_m[0])
        nc.vector.tensor_copy(m_dst[1][:, : M_COPIED[1]], m_src[1][:, : M_COPIED[1]])
        update_w(1, values("step1"), new_m[1], m_term1)
        gather_m(m_term0, 2)
        update_m(1, m_dst[1], new_m[1])
        nc.vector.tensor_copy(m_dst[2][:, : M_COPIED[2]], m_src[2][:, : M_COPIED[2]])
        update_w(2, values("step2"), new_m[2], m_term0)
        gather_m(m_term1, 3)
        update_m(2, m_dst[2], new_m[2])
        m_dst3 = table_tile("m_dst3", "new_m2")
        nc.scalar.activation(m_dst3[:], m_src[3][:], COPY)
        update_w(3, values("step3"), new_m[3], m_term1)
        update_m(3, m_dst3, new_m[3])
